import numpy as np
import ml_dtypes


def mxq(x, axis, fmt="e4m3"):
    dtype, down = {"e4m3": (ml_dtypes.float8_e4m3fn, 7), "e5m2": (ml_dtypes.float8_e5m2, 14)}[fmt]
    v = np.moveaxis(np.asarray(x, np.float32).astype(ml_dtypes.bfloat16).astype(np.float64), axis, -1)
    blocks = v.reshape(v.shape[:-1] + (-1, 32))
    amax = np.abs(blocks).max(-1, keepdims=True)
    byte = np.maximum(np.where(amax > 0, np.frexp(amax)[1] - 1 + 127, 0) - down, 1)
    scale = np.exp2(byte - 127.0)
    codes = (blocks / scale).astype(np.float32).astype(dtype).astype(np.float64)
    return np.moveaxis((codes * scale).reshape(v.shape), -1, axis)


WIDE = False


def mx_kscale(k):
    if not WIDE:
        return np.ones(k)
    levels = np.array([10, -10, 5, -5, 0])
    if k % 512:
        return np.exp2(np.random.permutation(np.resize(levels, k // 32))).repeat(32)
    a = np.empty((k // 512, 16))
    for p in range(k // 512):
        a[p, :8] = np.random.permutation(np.resize(levels, 8))
        for g in range(8):
            far = levels[np.abs(levels - a[p, g]) >= 10]
            a[p, g + 8] = far[np.random.randint(len(far))]
    return np.exp2(a.ravel()).repeat(32)


BF16 = ml_dtypes.bfloat16


def bf(x):
    return np.asarray(x, np.float32).astype(BF16)


def f64(x):
    return np.asarray(x).astype(np.float64)


E2M1 = np.array([0.0, 0.5, 1.0, 1.5, 2.0, 3.0, 4.0, 6.0, -0.0, -0.5, -1.0, -1.5, -2.0, -3.0, -4.0, -6.0])


def pack_weight(w, fmt):
    k, n = w.shape
    w = f64(bf(w)).reshape(k // 32, 32, n)
    amax = np.abs(w).max(1)
    if fmt == "e4m3":
        byte = np.frexp(amax)[1] - 1 + 127 - 7
    else:
        mant, ex = np.frexp(amax / 6.0)
        byte = np.where(mant > 0.5, ex, ex - 1) + 127
    byte = np.clip(np.where(amax > 0, byte, 1), 1, 254)
    scaled = (w * np.exp2(127.0 - byte)[:, None, :]).reshape(k, n).astype(np.float32)
    by_word = np.ascontiguousarray(scaled.reshape(k // 512, 128, 4, n).transpose(0, 1, 3, 2))
    if fmt == "e4m3":
        words = by_word.astype(ml_dtypes.float8_e4m3fn).view(np.uint8)
    else:
        c = by_word.astype(ml_dtypes.float4_e2m1fn).view(np.uint8) & 0xF
        words = c[..., 0::2] | (c[..., 1::2] << 4)
    return np.ascontiguousarray(words), np.ascontiguousarray(byte.astype(np.uint8).reshape(k // 512, 16, n))


def unpack_weight(words, scales, fmt):
    g, p, n, _ = words.shape
    if fmt == "e4m3":
        vals = np.ascontiguousarray(words).view(ml_dtypes.float8_e4m3fn).astype(np.float64)
    else:
        nib = np.empty((g, p, n, 4), np.uint8)
        nib[..., 0::2] = words & 0xF
        nib[..., 1::2] = words >> 4
        vals = E2M1[nib]
    vals = vals * np.repeat(np.exp2(scales.astype(np.float64) - 127.0), 8, axis=1)[..., None]
    return vals.transpose(0, 1, 3, 2).reshape(g * 512, n)
def pack4(w):
    words, scales = pack_weight(w, "e2m1")
    return words.reshape(words.shape[0], 128, -1), scales


def unpack4(words, scales):
    return unpack_weight(words.reshape(words.shape[0], 128, -1, 2), scales, "e2m1")


E4M3FN = np.array([(-1.0 if i & 128 else 1.0) * ((1.0 + (i & 7) / 8.0) * 2.0 ** (((i >> 3) & 15) - 7) if i & 120 else (i & 7) * 2.0 ** -9) for i in range(256)])


def e4m3fn_bytes(y):
    return np.clip(np.asarray(y, np.float64), -448.0, 448.0).astype(np.float32).astype(ml_dtypes.float8_e4m3fn).view(np.uint8)


def e4m3fn_values(b):
    return E4M3FN[b]


M, K, J, N, B = 1024, 2048, 1024, 1536, 128


def setup_inputs():
    s, t = mx_kscale(K), mx_kscale(J)
    x = np.random.standard_normal((M, K)) * s
    scale = (np.abs(x).reshape(M, K // B, B).max(axis=2) / 448.0).astype(np.float32)
    tbank = np.random.standard_normal((K, N)) / np.sqrt(K) / s[:, None]
    words, scales = pack4(tbank)
    return {"teacher_bytes": e4m3fn_bytes(x / np.repeat(f64(scale), B, axis=1)),
            "teacher_scale": scale,
            "tbank_words": words,
            "tbank_scales": scales,
            "student": bf(np.random.standard_normal((M, J)) * t),
            "sbank": bf(np.random.standard_normal((N, J)) / np.sqrt(J) / t),
            "trust": bf(np.random.uniform(0.5, 1.5, N))}


def reference(teacher_bytes, teacher_scale, tbank_words, tbank_scales, student, sbank, trust):
    teacher = e4m3fn_values(teacher_bytes) * np.repeat(f64(teacher_scale), B, axis=1)
    rel_t = mxq(teacher, 1, "e4m3") @ unpack4(tbank_words, tbank_scales)
    rel_s = mxq(f64(student), 1, "e4m3") @ mxq(f64(sbank), 1, "e4m3").T
    gap = rel_t - rel_s
    pair_loss = np.square(gap) * f64(trust)
    sample_loss = pair_loss.mean(axis=1)
    return pair_loss, sample_loss

@@ -1,0 +1,476 @@
+from contextlib import ExitStack
+
+import concourse.mybir as mybir
+from concourse.masks import make_identity
+
+M, K, J, N = 1024, 2048, 1024, 1536
+FLOPS = 2 * M * N * (K + J)
+
+F32 = mybir.dt.float32
+BF16 = mybir.dt.bfloat16
+I32 = mybir.dt.int32
+U32 = mybir.dt.uint32
+U8 = mybir.dt.uint8
+FP8 = mybir.dt.float8_e4m3fn
+FP8X4 = mybir.dt.float8_e4m3fn_x4
+FP4X4 = mybir.dt.float4_e2m1fn_x4
+MULT = mybir.AluOpType.mult
+SQUARE = mybir.ActivationFunctionType.Square
+
+P = 128
+TILES = M // P
+CHUNK = 512
+CHUNKS = N // CHUNK
+GT = K // 512
+GS = J // 512
+
+
+def tile_bank_relation_distill_d6_kernel(
+    tc, teacher_bytes, teacher_scale, tbank_words, tbank_scales, student, sbank, trust, out_0, out_1
+):
+    nc = tc.nc
+    with ExitStack() as ctx:
+        const = ctx.enter_context(tc.tile_pool(name="const", bufs=1))
+        work = ctx.enter_context(tc.tile_pool(name="work", bufs=3))
+        keep = ctx.enter_context(tc.tile_pool(name="keep", bufs=6))
+        outs = ctx.enter_context(tc.tile_pool(name="outs", bufs=6))
+        wide = ctx.enter_context(tc.tile_pool(name="wide", bufs=4))
+        turned = ctx.enter_context(tc.psum_pool(name="turned", bufs=4))
+        sums_pool = ctx.enter_context(tc.psum_pool(name="acc", bufs=4))
+
+        warm = const.tile([P, CHUNK], BF16, name="warm")
+        nc.gpsimd.memset(warm[:].bitcast(I32), 0)
+        ident = const.tile([P, P], F32, name="ident")
+        make_identity(nc, ident[:])
+        ones = const.tile([P, P], BF16, name="ones")
+        trust_row = const.tile([P, N], BF16, name="trust_row")
+        nc.vector.memset(trust_row[:].bitcast(I32), 0)
+        nc.gpsimd.memset(ones[:], 1.0)
+        trust_all = const.tile([P, N], F32, name="trust_all")
+        tb_words = [const.tile([P, GT, 2 * CHUNK], U8, name="tb_words%d" % n, align_bytes=64) for n in range(CHUNKS)]
+        tb_scales = const.tile([P, GT, N], U8, name="tb_scales", align_bytes=64)
+        nc.vector.memset(tb_scales[:].rearrange("p g n -> p (g n)").bitcast(I32), 0)
+        scale = const.tile([P, TILES, K // P], F32, name="scale")
+        neg = const.tile([P, TILES, K // P], F32, name="neg")
+        parts = const.tile([P, TILES, CHUNKS], F32, name="parts")
+        means = const.tile([P, TILES], F32, name="means")
+
+        t_view = teacher_bytes.rearrange("(p m) k -> p m k", m=TILES)
+        s_view = student.rearrange("(p m) k -> p m k", m=TILES)
+        o_view = out_0.rearrange("(p m) n -> p m n", m=TILES)
+
+        t_raw = [const.tile([P, K], U8, name="t_raw%d" % m, align_bytes=64) for m in range(TILES)]
+        s_raw = [const.tile([P, J], BF16, name="s_raw%d" % m, align_bytes=64) for m in range(TILES)]
+        b_raw = [const.tile([P, J], BF16, name="b_raw%d" % i, align_bytes=64) for i in range(N // P)]
+        b_codes = const.tile([P, CHUNKS, GS, CHUNK], U32, name="b_codes", align_bytes=64)
+        b_scales = const.tile([P, CHUNKS, GS, CHUNK], U8, name="b_scales", align_bytes=64)
+
+        def load_s(m):
+            nc.sync.dma_start(out=s_raw[m][:], in_=s_view[:, m, :])
+
+        def load_t(m):
+            nc.sync.dma_start(out=t_raw[m][:], in_=t_view[:, m, :])
+
+        def load_b(c):
+            for i in range(4 * c, 4 * c + 4):
+                nc.sync.dma_start(out=b_raw[i][:], in_=sbank[P * i : P * (i + 1), :])
+
+        def load_words(c):
+            cols = slice(2 * CHUNK * c, 2 * CHUNK * (c + 1))
+            nc.sync.dma_start(
+                out=tb_words[c][:].bitcast(I32),
+                in_=tbank_words[:, :, cols].rearrange("g p w -> p g w").bitcast(I32),
+            )
+
+        live = {}
+
+        def perm_s(m):
+            xs = work.tile([P, GS, 2, P], F32, name="xs")
+            live["xs", m] = xs
+            nc.vector.tensor_copy(
+                out=xs[:], in_=s_raw[m][:].bitcast(F32).rearrange("p (g w u) -> p g u w", g=GS, u=2)
+            )
+
+        def turn_s(m):
+            bank = turned.tile([P, GS, 2, P], F32, name="bank")
+            live["bs", m] = bank
+            words = s_raw[m][:].bitcast(F32)
+            for g in range(GS):
+                for u in range(2):
+                    if ("xs", m) in live:
+                        rows = live["xs", m][:, g, u, :]
+                    else:
+                        rows = words[:, 256 * g + u : 256 * (g + 1) : 2]
+                    nc.tensor.transpose(bank[:, g, u, :], rows, ident[:])
+
+        def take_s(m):
+            grouped = work.tile([P, GS, P, 2], F32, name="s_grouped", align_bytes=64)
+            live["gs", m] = grouped
+            nc.scalar.copy(out=grouped[:], in_=live["bs", m][:].rearrange("p g u r -> p g r u"))
+
+        def quant_s(m):
+            codes = keep.tile([P, GS, P], U32, name="s_codes", align_bytes=64)
+            scales = keep.tile([P, GS, P], U8, name="s_scales", align_bytes=64)
+            live["cs", m] = (codes, scales)
+            nc.vector.quantize_mx(
+                out=codes[:].rearrange("p g r -> p (g r)").bitcast(FP8X4),
+                scales=scales[:].rearrange("p g r -> p (g r)"),
+                in_=live["gs", m][:].rearrange("p g r u -> p (g r u)").bitcast(BF16),
+            )
+
+        def widen(m, lo, hi):
+            if lo == 0:
+                live["xt", m] = work.tile([P, GT, 2, P, 2], BF16, name="xt", align_bytes=64)
+            xt = live["xt", m]
+            for c in range(lo, hi):
+                g, q = divmod(c, 4)
+                nc.vector.tensor_scalar(
+                    out=xt[:, g, :, 32 * q : 32 * (q + 1), :].rearrange("p u w e -> p w u e"),
+                    in0=t_raw[m][:, P * c : P * (c + 1)].bitcast(FP8).rearrange("p (w u e) -> p w u e", u=2, e=2),
+                    scalar1=neg[:, m, c : c + 1],
+                    scalar2=None,
+                    op0=MULT,
+                )
+
+        def turn_t(m):
+            words = live["xt", m][:].rearrange("p g u w e -> p (g u w e)").bitcast(F32)
+            for h in range(2):
+                bank = turned.tile([P, 2, 2, P], F32, name="bank")
+                live["bt", m, h] = bank
+                for g in range(2):
+                    for u in range(2):
+                        at = P * (2 * (2 * h + g) + u)
+                        nc.tensor.transpose(bank[:, g, u, :], words[:, at : at + P], ident[:])
+
+        def take_t(m, h, on_scalar=True):
+            if h == 0:
+                live["gt", m] = work.tile([P, GT, P, 2], F32, name="t_grouped", align_bytes=64)
+            dst = live["gt", m][:, 2 * h : 2 * h + 2]
+            src = live["bt", m, h][:].rearrange("p g u r -> p g r u")
+            if on_scalar:
+                nc.scalar.copy(out=dst, in_=src)
+            else:
+                nc.vector.tensor_copy(out=dst, in_=src)
+
+        def quant_t(m):
+            codes = keep.tile([P, GT, P], U32, name="t_codes", align_bytes=64)
+            scales = keep.tile([P, GT, P], U8, name="t_scales", align_bytes=64)
+            live["ct", m] = (codes, scales)
+            nc.vector.quantize_mx(
+                out=codes[:].rearrange("p g r -> p (g r)").bitcast(FP8X4),
+                scales=scales[:].rearrange("p g r -> p (g r)"),
+                in_=live["gt", m][:].rearrange("p g r u -> p (g r u)").bitcast(BF16),
+            )
+
+        def perm_b(i):
+            xb = wide.tile([P, GS, 2, P], F32, name="xb")
+            live["xb", i] = xb
+            nc.vector.tensor_copy(
+                out=xb[:], in_=b_raw[i][:].bitcast(F32).rearrange("p (g w u) -> p g u w", g=GS, u=2)
+            )
+
+        def turn_b(i):
+            bank = turned.tile([P, GS, 2, P], F32, name="bank")
+            live["bb", i] = bank
+            words = b_raw[i][:].bitcast(F32)
+            for g in range(GS):
+                for u in range(2):
+                    if ("xb", i) in live:
+                        rows = live["xb", i][:, g, u, :]
+                    else:
+                        rows = words[:, 256 * g + u : 256 * (g + 1) : 2]
+                    nc.tensor.transpose(bank[:, g, u, :], rows, ident[:])
+
+        def take_b(i, on_scalar):
+            c, j = divmod(i, 4)
+            if j == 0:
+                live["gb", c] = work.tile([P, GS, CHUNK, 2], F32, name="b_grouped", align_bytes=64)
+            dst = live["gb", c][:, :, P * j : P * (j + 1), :]
+            src = live["bb", i][:].rearrange("p g u r -> p g r u")
+            if on_scalar:
+                nc.scalar.copy(out=dst, in_=src)
+            else:
+                nc.vector.tensor_copy(out=dst, in_=src)
+
+        def quant_b(c):
+            for g in range(GS):
+                nc.vector.quantize_mx(
+                    out=b_codes[:, c, g, :].bitcast(FP8X4),
+                    scales=b_scales[:, c, g, :],
+                    in_=live["gb", c][:, g].rearrange("p r u -> p (r u)").bitcast(BF16),
+                )
+
+        def passes_s(m, n, acc, lo, hi, first, last):
+            codes, scales = live["cs", m]
+            for g in range(GS):
+                nc.tensor.matmul_mx(
+                    out=acc,
+                    lhsT=codes[:, g, :].bitcast(FP8X4),
+                    lhsT_scale=scales[:, g, :],
+                    rhs=b_codes[:, n, g, lo:hi].bitcast(FP8X4),
+                    rhs_scale=b_scales[:, n, g, lo:hi],
+                    start=first and g == 0,
+                    stop=last and g == GS - 1,
+                )
+
+        def passes_t(m, n, acc, lo, hi, first, last):
+            codes, scales = live["ct", m]
+            for g in range(GT):
+                nc.tensor.matmul_mx(
+                    out=acc,
+                    lhsT=codes[:, g, :].bitcast(FP8X4),
+                    lhsT_scale=scales[:, g, :],
+                    rhs=tb_words[n][:, g, 2 * lo : 2 * hi].bitcast(FP4X4),
+                    rhs_scale=tb_scales[:, g, CHUNK * n + lo : CHUNK * n + hi],
+                    start=first and g == 0,
+                    stop=last and g == GT - 1,
+                )
+
+        def multiply(m, n, t_first=False, lo=0, hi=CHUNK):
+            acc = sums_pool.tile([P, CHUNK], F32, name="acc")
+            live["acc", m, n, lo] = acc
+            view = acc[:, : hi - lo]
+            if t_first:
+                passes_t(m, n, view, lo, hi, True, False)
+                passes_s(m, n, view, lo, hi, False, True)
+            else:
+                passes_s(m, n, view, lo, hi, True, False)
+                passes_t(m, n, view, lo, hi, False, True)
+
+        def open_group(m, n):
+            acc = sums_pool.tile([P, CHUNK], F32, name="acc")
+            live["acc", m, n, 0] = acc
+            passes_t(m, n, acc[:], 0, CHUNK, True, False)
+
+        def close_group(m, n):
+            passes_s(m, n, live["acc", m, n, 0][:], 0, CHUNK, False, True)
+
+        def square(m, n, lo=0, hi=CHUNK):
+            sq = work.tile([P, CHUNK], F32, name="sq")
+            live["sq", m, n, lo] = sq
+            nc.scalar.activation(out=sq[:, : hi - lo], in_=live["acc", m, n, lo][:, : hi - lo], func=SQUARE)
+
+        def weigh(m, n, lo=0, hi=CHUNK, part=None, queue=None):
+            res = outs.tile([P, CHUNK], F32, name="res")
+            cols = slice(CHUNK * n + lo, CHUNK * n + hi)
+            nc.vector.scalar_tensor_tensor(
+                out=res[:, : hi - lo],
+                in0=live["sq", m, n, lo][:, : hi - lo],
+                scalar=1.0,
+                in1=trust_all[:, cols],
+                op0=MULT,
+                op1=MULT,
+                accum_out=parts[:, m, n : n + 1] if part is None else part,
+            )
+            (queue or nc.sync).dma_start(out=o_view[:, m, cols], in_=res[:, : hi - lo])
+
+        def group(m, n):
+            multiply(m, n)
+            square(m, n)
+            weigh(m, n)
+
+        with tc.manual_schedule():
+            nc.scalar.dma_start(out=scale[:], in_=teacher_scale.rearrange("(p m) c -> p m c", m=TILES))
+            load_t(0)
+            load_s(0)
+            load_b(0)
+            nc.sync.dma_start(out=trust_row[0:1, :], in_=trust.rearrange("(o n) -> o n", o=1))
+            for q in range(4):
+                nc.sync.dma_start(
+                    out=tb_scales[32 * q : 32 * q + 4, :, :].bitcast(I32),
+                    in_=tbank_scales[:, 4 * q : 4 * q + 4, :].rearrange("g q n -> q g n").bitcast(I32),
+                )
+            load_words(0)
+            load_t(1)
+            load_s(1)
+            load_b(1)
+            load_words(1)
+            load_t(2)
+            load_s(2)
+            load_b(2)
+            load_words(2)
+            for m in range(3, TILES):
+                load_t(m)
+                load_s(m)
+
+            trust_banks = []
+            for n in range(CHUNKS):
+                bank = sums_pool.tile([P, CHUNK], F32, name="acc")
+                trust_banks.append(bank)
+
+            def spread_trust(n):
+                cols = slice(CHUNK * n, CHUNK * (n + 1))
+                nc.tensor.matmul(trust_banks[n][:], ones[:], trust_row[:, cols], start=True, stop=True)
+
+            def take_trust(n):
+                cols = slice(CHUNK * n, CHUNK * (n + 1))
+                nc.scalar.copy(out=trust_all[:, cols], in_=trust_banks[n][:])
+
+            def stir(n):
+                for i in range(n):
+                    bank = turned.tile([P, CHUNK], F32, name="bank")
+                    nc.tensor.matmul(bank[:], warm[:, :P], warm[:], start=True, stop=True)
+
+            nc.vector.tensor_scalar(out=neg[:], in0=scale[:], scalar1=-1.0, scalar2=None, op0=MULT)
+            stir(6)
+            widen(0, 0, 16)
+            turn_s(0)
+            take_s(0)
+            turn_b(0)
+            take_b(0, True)
+            turn_b(1)
+            take_b(1, True)
+            turn_t(0)
+            take_t(0, 0)
+            take_t(0, 1, False)
+            spread_trust(0)
+            quant_s(0)
+            turn_b(2)
+            take_b(2, True)
+            spread_trust(1)
+            turn_b(3)
+            spread_trust(2)
+            quant_t(0)
+            take_b(3, True)
+            widen(1, 0, 8)
+            quant_b(0)
+            widen(1, 8, 16)
+            open_group(0, 0)
+            turn_s(1)
+            take_s(1)
+            take_trust(0)
+            turn_b(4)
+            take_b(4, True)
+            close_group(0, 0)
+            quant_s(1)
+            perm_b(6)
+            perm_b(7)
+            turn_t(1)
+            take_t(1, 0)
+            take_t(1, 1)
+            turn_b(5)
+            take_b(5, False)
+            square(0, 0)
+            turn_b(6)
+            take_b(6, True)
+            quant_t(1)
+            weigh(0, 0)
+            perm_s(2)
+            turn_b(7)
+            take_b(7, True)
+            multiply(1, 0)
+            widen(2, 0, 16)
+            quant_b(1)
+            take_trust(1)
+            turn_s(2)
+            turn_t(2)
+            take_s(2)
+            take_trust(2)
+            square(1, 0)
+            take_t(2, 0)
+            take_t(2, 1)
+            weigh(1, 0)
+            multiply(0, 1, True)
+            quant_s(2)
+            quant_t(2)
+            perm_b(8)
+            square(0, 1)
+            perm_b(9)
+            multiply(1, 1)
+            perm_b(10)
+            weigh(0, 1)
+            perm_b(11)
+            for i in range(8, 12):
+                turn_b(i)
+                take_b(i, True)
+            square(1, 1)
+            perm_s(3)
+            widen(3, 0, 8)
+            multiply(2, 0)
+            weigh(1, 1)
+            widen(3, 8, 16)
+            square(2, 0)
+            quant_b(2)
+            multiply(2, 1)
+            weigh(2, 0)
+            turn_s(3)
+            turn_t(3)
+            square(2, 1)
+            take_s(3)
+            take_t(3, 0)
+            take_t(3, 1)
+            multiply(0, 2, True)
+            weigh(2, 1)
+            perm_s(4)
+            widen(4, 0, 4)
+            quant_s(3)
+            quant_t(3)
+            square(0, 2)
+            multiply(1, 2)
+            widen(4, 4, 12)
+            weigh(0, 2)
+            square(1, 2)
+            multiply(2, 2)
+            widen(4, 12, 16)
+            weigh(1, 2)
+            pending = (2, 2)
+            for m in range(3, TILES):
+                ahead = m + 1 < TILES
+                further = m + 2 < TILES
+                if ahead:
+                    turn_s(m + 1)
+                    turn_t(m + 1)
+                multiply(m, 0)
+                square(*pending)
+                if ahead:
+                    take_s(m + 1)
+                    take_t(m + 1, 0)
+                    take_t(m + 1, 1)
+                if further:
+                    widen(m + 2, 0, 6)
+                weigh(*pending)
+                if further:
+                    perm_s(m + 2)
+                if ahead:
+                    quant_s(m + 1)
+                    quant_t(m + 1)
+                multiply(m, 1)
+                square(m, 0)
+                if further:
+                    widen(m + 2, 6, 11)
+                weigh(m, 0)
+                if m < TILES - 1:
+                    multiply(m, 2)
+                square(m, 1)
+                if further:
+                    widen(m + 2, 11, 16)
+                weigh(m, 1)
+                pending = (m, 2)
+            last = TILES - 1
+            half = CHUNK // 2
+            quarter = CHUNK // 4
+            total = const.tile([P, TILES], F32, name="total")
+            rest = const.tile([P, 1], F32, name="rest")
+            for h in range(2):
+                acc = sums_pool.tile([P, CHUNK], F32, name="acc")
+                live["acc", last, 2, half * h] = acc
+                for j in range(2):
+                    lo = half * h + quarter * j
+                    view = acc[:, quarter * j : quarter * (j + 1)]
+                    passes_s(last, 2, view, lo, lo + quarter, True, False)
+                    passes_t(last, 2, view, lo, lo + quarter, False, True)
+                square(last, 2, half * h, half * (h + 1))
+                if h == 0:
+                    weigh(last, 2, 0, half, part=parts[:, last, 2:3])
+                    nc.vector.reduce_sum(out=total[:], in_=parts[:], axis=mybir.AxisListType.X)
+                    nc.vector.tensor_scalar(out=means[:, :last], in0=total[:, :last], scalar1=1.0 / N, scalar2=None, op0=MULT)
+            weigh(last, 2, half, CHUNK, part=rest[:, 0:1])
+            nc.vector.tensor_scalar(
+                out=means[:, last:],
+                in0=total[:, last:],
+                scalar1=rest[:, 0:1],
+                scalar2=1.0 / N,
+                op0=mybir.AluOpType.add,
+                op1=MULT,
+            )
+            nc.scalar.dma_start(out=out_1.rearrange("(p m) -> p m", m=TILES), in_=means[:])

@@ -23,6 +23,7 @@ CHUNK = 512
 CHUNKS = N // CHUNK
 GT = K // 512
 GS = J // 512
+BANKS = 8
 
 
 def tile_bank_relation_distill_d6_kernel(
@@ -35,21 +36,14 @@ def tile_bank_relation_distill_d6_kernel(
         keep = ctx.enter_context(tc.tile_pool(name="keep", bufs=6))
         outs = ctx.enter_context(tc.tile_pool(name="outs", bufs=6))
         wide = ctx.enter_context(tc.tile_pool(name="wide", bufs=4))
-        turned = ctx.enter_context(tc.psum_pool(name="turned", bufs=4))
-        sums_pool = ctx.enter_context(tc.psum_pool(name="acc", bufs=4))
+        psum = ctx.enter_context(tc.psum_pool(name="psum", bufs=1))
 
-        warm = const.tile([P, CHUNK], BF16, name="warm")
-        nc.gpsimd.memset(warm[:].bitcast(I32), 0)
         ident = const.tile([P, P], F32, name="ident")
-        make_identity(nc, ident[:])
-        ones = const.tile([P, P], BF16, name="ones")
+        ones = const.tile([P, CHUNK], BF16, name="ones")
         trust_row = const.tile([P, N], BF16, name="trust_row")
-        nc.vector.memset(trust_row[:].bitcast(I32), 0)
-        nc.gpsimd.memset(ones[:], 1.0)
-        trust_all = const.tile([P, N], F32, name="trust_all")
+        trust_all = const.tile([P, N], BF16, name="trust_all")
         tb_words = [const.tile([P, GT, 2 * CHUNK], U8, name="tb_words%d" % n, align_bytes=64) for n in range(CHUNKS)]
-        tb_scales = const.tile([P, GT, N], U8, name="tb_scales", align_bytes=64)
-        nc.vector.memset(tb_scales[:].rearrange("p g n -> p (g n)").bitcast(I32), 0)
+        tb_scales = [const.tile([P, GT, CHUNK], U8, name="tb_scales%d" % n, align_bytes=64) for n in range(CHUNKS)]
         scale = const.tile([P, TILES, K // P], F32, name="scale")
         neg = const.tile([P, TILES, K // P], F32, name="neg")
         parts = const.tile([P, TILES, CHUNKS], F32, name="parts")
@@ -62,8 +56,8 @@ def tile_bank_relation_distill_d6_kernel(
         t_raw = [const.tile([P, K], U8, name="t_raw%d" % m, align_bytes=64) for m in range(TILES)]
         s_raw = [const.tile([P, J], BF16, name="s_raw%d" % m, align_bytes=64) for m in range(TILES)]
         b_raw = [const.tile([P, J], BF16, name="b_raw%d" % i, align_bytes=64) for i in range(N // P)]
-        b_codes = const.tile([P, CHUNKS, GS, CHUNK], U32, name="b_codes", align_bytes=64)
-        b_scales = const.tile([P, CHUNKS, GS, CHUNK], U8, name="b_scales", align_bytes=64)
+        b_codes = [const.tile([P, GS, CHUNK], U32, name="b_codes%d" % n, align_bytes=64) for n in range(CHUNKS)]
+        b_scales = [const.tile([P, GS, CHUNK], U8, name="b_scales%d" % n, align_bytes=64) for n in range(CHUNKS)]
 
         def load_s(m):
             nc.sync.dma_start(out=s_raw[m][:], in_=s_view[:, m, :])
@@ -71,8 +65,8 @@ def tile_bank_relation_distill_d6_kernel(
         def load_t(m):
             nc.sync.dma_start(out=t_raw[m][:], in_=t_view[:, m, :])
 
-        def load_b(c):
-            for i in range(4 * c, 4 * c + 4):
+        def load_b(lo, hi):
+            for i in range(lo, hi):
                 nc.sync.dma_start(out=b_raw[i][:], in_=sbank[P * i : P * (i + 1), :])
 
         def load_words(c):
@@ -82,31 +76,66 @@ def tile_bank_relation_distill_d6_kernel(
                 in_=tbank_words[:, :, cols].rearrange("g p w -> p g w").bitcast(I32),
             )
 
+        def clear_scales(c):
+            nc.vector.memset(tb_scales[c][:].rearrange("p g n -> p (g n)").bitcast(I32), 0)
+
+        def load_scales(c):
+            cols = slice(CHUNK * c, CHUNK * (c + 1))
+            for r in range(4):
+                nc.sync.dma_start(
+                    out=tb_scales[c][r:P:32, :, :].bitcast(I32),
+                    in_=tbank_scales[:, r:16:4, cols].rearrange("g q n -> q g n").bitcast(I32),
+                )
+
         live = {}
+        idle = list(range(BANKS))
 
-        def perm_s(m):
-            xs = work.tile([P, GS, 2, P], F32, name="xs")
-            live["xs", m] = xs
-            nc.vector.tensor_copy(
-                out=xs[:], in_=s_raw[m][:].bitcast(F32).rearrange("p (g w u) -> p g u w", g=GS, u=2)
-            )
+        def claim(shape, dtype):
+            b = idle.pop(0)
+            return b, psum.tile(shape, dtype, name="bank%d" % b)
 
-        def turn_s(m):
-            bank = turned.tile([P, GS, 2, P], F32, name="bank")
-            live["bs", m] = bank
-            words = s_raw[m][:].bitcast(F32)
+        def perm(key, raw, on_scalar):
+            x = wide.tile([P, GS, 2, P], F32, name="x")
+            live[key] = x
+            src = raw[:].bitcast(F32).rearrange("p (g q u r) -> p g u q r", g=GS, u=2, r=8)
+            dst = x[:].rearrange("p g u (q r) -> p g u q r", r=8)
+            if on_scalar:
+                nc.scalar.copy(out=dst, in_=src)
+            else:
+                nc.vector.tensor_copy(out=dst, in_=src)
+
+        def perm_s(m, on_scalar=False):
+            perm(("xs", m), s_raw[m], on_scalar)
+
+        def perm_b(i, on_scalar=False):
+            perm(("xb", i), b_raw[i], on_scalar)
+
+        def turn(key):
+            b, bank = claim([P, GS, 2, P], F32)
             for g in range(GS):
                 for u in range(2):
-                    if ("xs", m) in live:
-                        rows = live["xs", m][:, g, u, :]
-                    else:
-                        rows = words[:, 256 * g + u : 256 * (g + 1) : 2]
-                    nc.tensor.transpose(bank[:, g, u, :], rows, ident[:])
+                    nc.tensor.transpose(bank[:, g, u, :], live[key][:, g, u, :], ident[:])
+            return b, bank
 
-        def take_s(m):
+        def turn_s(m):
+            live["bs", m] = turn(("xs", m))
+
+        def turn_b(i):
+            live["bb", i] = turn(("xb", i))
+
+        def take(dst, claimed, on_scalar):
+            b, bank = claimed
+            idle.append(b)
+            src = bank[:].rearrange("p g u r -> p g r u")
+            if on_scalar:
+                nc.scalar.copy(out=dst, in_=src)
+            else:
+                nc.vector.tensor_copy(out=dst, in_=src)
+
+        def take_s(m, on_scalar=True):
             grouped = work.tile([P, GS, P, 2], F32, name="s_grouped", align_bytes=64)
             live["gs", m] = grouped
-            nc.scalar.copy(out=grouped[:], in_=live["bs", m][:].rearrange("p g u r -> p g r u"))
+            take(grouped[:], live["bs", m], on_scalar)
 
         def quant_s(m):
             codes = keep.tile([P, GS, P], U32, name="s_codes", align_bytes=64)
@@ -132,72 +161,44 @@ def tile_bank_relation_distill_d6_kernel(
                     op0=MULT,
                 )
 
-        def turn_t(m):
+        def turn_t(m, h):
             words = live["xt", m][:].rearrange("p g u w e -> p (g u w e)").bitcast(F32)
-            for h in range(2):
-                bank = turned.tile([P, 2, 2, P], F32, name="bank")
-                live["bt", m, h] = bank
-                for g in range(2):
-                    for u in range(2):
-                        at = P * (2 * (2 * h + g) + u)
-                        nc.tensor.transpose(bank[:, g, u, :], words[:, at : at + P], ident[:])
+            b, bank = claim([P, 2, 2, P], F32)
+            live["bt", m, h] = (b, bank)
+            for g in range(2):
+                for u in range(2):
+                    at = P * (2 * (2 * h + g) + u)
+                    nc.tensor.transpose(bank[:, g, u, :], words[:, at : at + P], ident[:])
 
         def take_t(m, h, on_scalar=True):
             if h == 0:
                 live["gt", m] = work.tile([P, GT, P, 2], F32, name="t_grouped", align_bytes=64)
-            dst = live["gt", m][:, 2 * h : 2 * h + 2]
-            src = live["bt", m, h][:].rearrange("p g u r -> p g r u")
-            if on_scalar:
-                nc.scalar.copy(out=dst, in_=src)
-            else:
-                nc.vector.tensor_copy(out=dst, in_=src)
+            take(live["gt", m][:, 2 * h : 2 * h + 2], live["bt", m, h], on_scalar)
 
-        def quant_t(m):
-            codes = keep.tile([P, GT, P], U32, name="t_codes", align_bytes=64)
-            scales = keep.tile([P, GT, P], U8, name="t_scales", align_bytes=64)
-            live["ct", m] = (codes, scales)
+        def quant_t(m, lo=0, hi=GT):
+            if lo == 0:
+                codes = keep.tile([P, GT, P], U32, name="t_codes", align_bytes=64)
+                scales = keep.tile([P, GT, P], U8, name="t_scales", align_bytes=64)
+                live["ct", m] = (codes, scales)
+            codes, scales = live["ct", m]
             nc.vector.quantize_mx(
-                out=codes[:].rearrange("p g r -> p (g r)").bitcast(FP8X4),
-                scales=scales[:].rearrange("p g r -> p (g r)"),
-                in_=live["gt", m][:].rearrange("p g r u -> p (g r u)").bitcast(BF16),
+                out=codes[:, lo:hi].rearrange("p g r -> p (g r)").bitcast(FP8X4),
+                scales=scales[:, lo:hi].rearrange("p g r -> p (g r)"),
+                in_=live["gt", m][:, lo:hi].rearrange("p g r u -> p (g r u)").bitcast(BF16),
             )
 
-        def perm_b(i):
-            xb = wide.tile([P, GS, 2, P], F32, name="xb")
-            live["xb", i] = xb
-            nc.vector.tensor_copy(
-                out=xb[:], in_=b_raw[i][:].bitcast(F32).rearrange("p (g w u) -> p g u w", g=GS, u=2)
-            )
-
-        def turn_b(i):
-            bank = turned.tile([P, GS, 2, P], F32, name="bank")
-            live["bb", i] = bank
-            words = b_raw[i][:].bitcast(F32)
-            for g in range(GS):
-                for u in range(2):
-                    if ("xb", i) in live:
-                        rows = live["xb", i][:, g, u, :]
-                    else:
-                        rows = words[:, 256 * g + u : 256 * (g + 1) : 2]
-                    nc.tensor.transpose(bank[:, g, u, :], rows, ident[:])
-
-        def take_b(i, on_scalar):
+        def take_b(i, on_scalar=True):
             c, j = divmod(i, 4)
             if j == 0:
-                live["gb", c] = work.tile([P, GS, CHUNK, 2], F32, name="b_grouped", align_bytes=64)
-            dst = live["gb", c][:, :, P * j : P * (j + 1), :]
-            src = live["bb", i][:].rearrange("p g u r -> p g r u")
-            if on_scalar:
-                nc.scalar.copy(out=dst, in_=src)
-            else:
-                nc.vector.tensor_copy(out=dst, in_=src)
+                live["gb", c] = work.tile([P, GS, CHUNK, 2], F32, name="b_grouped", align_bytes=64, bufs=2)
+            take(live["gb", c][:, :, P * j : P * (j + 1), :], live["bb", i], on_scalar)
 
-        def quant_b(c):
+        def quant_b(c, lo=0, hi=CHUNK):
             for g in range(GS):
                 nc.vector.quantize_mx(
-                    out=b_codes[:, c, g, :].bitcast(FP8X4),
-                    scales=b_scales[:, c, g, :],
-                    in_=live["gb", c][:, g].rearrange("p r u -> p (r u)").bitcast(BF16),
+                    out=b_codes[c][:, g, lo:hi].bitcast(FP8X4),
+                    scales=b_scales[c][:, g, lo:hi],
+                    in_=live["gb", c][:, g, lo:hi].rearrange("p r u -> p (r u)").bitcast(BF16),
                 )
 
         def passes_s(m, n, acc, lo, hi, first, last):
@@ -207,50 +208,47 @@ def tile_bank_relation_distill_d6_kernel(
                     out=acc,
                     lhsT=codes[:, g, :].bitcast(FP8X4),
                     lhsT_scale=scales[:, g, :],
-                    rhs=b_codes[:, n, g, lo:hi].bitcast(FP8X4),
-                    rhs_scale=b_scales[:, n, g, lo:hi],
+                    rhs=b_codes[n][:, g, lo:hi].bitcast(FP8X4),
+                    rhs_scale=b_scales[n][:, g, lo:hi],
                     start=first and g == 0,
                     stop=last and g == GS - 1,
                 )
 
-        def passes_t(m, n, acc, lo, hi, first, last):
+        def passes_t(m, n, acc, lo, hi, first, last, g0=0, g1=GT):
             codes, scales = live["ct", m]
-            for g in range(GT):
+            for g in range(g0, g1):
                 nc.tensor.matmul_mx(
                     out=acc,
                     lhsT=codes[:, g, :].bitcast(FP8X4),
                     lhsT_scale=scales[:, g, :],
                     rhs=tb_words[n][:, g, 2 * lo : 2 * hi].bitcast(FP4X4),
-                    rhs_scale=tb_scales[:, g, CHUNK * n + lo : CHUNK * n + hi],
+                    rhs_scale=tb_scales[n][:, g, lo:hi],
                     start=first and g == 0,
                     stop=last and g == GT - 1,
                 )
 
-        def multiply(m, n, t_first=False, lo=0, hi=CHUNK):
-            acc = sums_pool.tile([P, CHUNK], F32, name="acc")
-            live["acc", m, n, lo] = acc
-            view = acc[:, : hi - lo]
-            if t_first:
-                passes_t(m, n, view, lo, hi, True, False)
-                passes_s(m, n, view, lo, hi, False, True)
-            else:
-                passes_s(m, n, view, lo, hi, True, False)
-                passes_t(m, n, view, lo, hi, False, True)
+        def multiply(m, n, lo=0, hi=CHUNK):
+            live["acc", m, n, lo] = claim([P, CHUNK], F32)
+            view = live["acc", m, n, lo][1][:, : hi - lo]
+            passes_t(m, n, view, lo, hi, True, False)
+            passes_s(m, n, view, lo, hi, False, True)
 
-        def open_group(m, n):
-            acc = sums_pool.tile([P, CHUNK], F32, name="acc")
-            live["acc", m, n, 0] = acc
-            passes_t(m, n, acc[:], 0, CHUNK, True, False)
+        def open_group(m, n, g0=0, g1=GT):
+            if g0 == 0:
+                live["acc", m, n, 0] = claim([P, CHUNK], F32)
+            passes_t(m, n, live["acc", m, n, 0][1][:], 0, CHUNK, True, False, g0, g1)
 
         def close_group(m, n):
-            passes_s(m, n, live["acc", m, n, 0][:], 0, CHUNK, False, True)
+            passes_s(m, n, live["acc", m, n, 0][1][:], 0, CHUNK, False, True)
 
         def square(m, n, lo=0, hi=CHUNK):
-            sq = work.tile([P, CHUNK], F32, name="sq")
+            sq = work.tile([P, CHUNK], F32, name="sq", bufs=5)
             live["sq", m, n, lo] = sq
-            nc.scalar.activation(out=sq[:, : hi - lo], in_=live["acc", m, n, lo][:, : hi - lo], func=SQUARE)
+            b, acc = live["acc", m, n, lo]
+            idle.append(b)
+            nc.scalar.activation(out=sq[:, : hi - lo], in_=acc[:, : hi - lo], func=SQUARE)
 
-        def weigh(m, n, lo=0, hi=CHUNK, part=None, queue=None):
+        def weigh(m, n, lo=0, hi=CHUNK, part=None):
             res = outs.tile([P, CHUNK], F32, name="res")
             cols = slice(CHUNK * n + lo, CHUNK * n + hi)
             nc.vector.scalar_tensor_tensor(
@@ -262,164 +260,187 @@ def tile_bank_relation_distill_d6_kernel(
                 op1=MULT,
                 accum_out=parts[:, m, n : n + 1] if part is None else part,
             )
-            (queue or nc.sync).dma_start(out=o_view[:, m, cols], in_=res[:, : hi - lo])
+            nc.sync.dma_start(out=o_view[:, m, cols], in_=res[:, : hi - lo])
 
-        def group(m, n):
-            multiply(m, n)
-            square(m, n)
-            weigh(m, n)
+        def spread_trust(n):
+            b, bank = claim([P, CHUNK], BF16)
+            live["trust", n] = (b, bank)
+            nc.tensor.matmul(bank[:], ones[:, :P], trust_row[:, CHUNK * n : CHUNK * (n + 1)], start=True, stop=True)
+
+        def stir(count):
+            for i in range(count):
+                b, bank = claim([P, CHUNK], F32)
+                idle.append(b)
+                nc.tensor.matmul(bank[:], ones[:, :P], ones[:], start=True, stop=True)
+
+        def take_trust(n):
+            b, bank = live["trust", n]
+            idle.append(b)
+            nc.scalar.copy(out=trust_all[:, CHUNK * n : CHUNK * (n + 1)], in_=bank[:])
 
         with tc.manual_schedule():
-            nc.scalar.dma_start(out=scale[:], in_=teacher_scale.rearrange("(p m) c -> p m c", m=TILES))
+            nc.vector.memset(ones[:], 1.0)
+            nc.vector.memset(trust_row[:].bitcast(I32), 0)
+            clear_scales(0)
+            make_identity(nc, ident[:])
+            clear_scales(1)
+            clear_scales(2)
+            nc.sync.dma_start(out=scale[:], in_=teacher_scale.rearrange("(p m) c -> p m c", m=TILES))
             load_t(0)
-            load_s(0)
-            load_b(0)
             nc.sync.dma_start(out=trust_row[0:1, :], in_=trust.rearrange("(o n) -> o n", o=1))
-            for q in range(4):
-                nc.sync.dma_start(
-                    out=tb_scales[32 * q : 32 * q + 4, :, :].bitcast(I32),
-                    in_=tbank_scales[:, 4 * q : 4 * q + 4, :].rearrange("g q n -> q g n").bitcast(I32),
-                )
+            load_scales(0)
             load_words(0)
             load_t(1)
-            load_s(1)
-            load_b(1)
+            load_scales(1)
             load_words(1)
+            load_b(0, 4)
+            load_s(0)
+            load_s(1)
             load_t(2)
             load_s(2)
-            load_b(2)
+            load_b(4, 8)
+            load_t(3)
+            load_s(3)
+            load_scales(2)
             load_words(2)
-            for m in range(3, TILES):
+            load_b(8, 12)
+            for m in range(4, TILES):
                 load_t(m)
                 load_s(m)
-
-            trust_banks = []
-            for n in range(CHUNKS):
-                bank = sums_pool.tile([P, CHUNK], F32, name="acc")
-                trust_banks.append(bank)
-
-            def spread_trust(n):
-                cols = slice(CHUNK * n, CHUNK * (n + 1))
-                nc.tensor.matmul(trust_banks[n][:], ones[:], trust_row[:, cols], start=True, stop=True)
-
-            def take_trust(n):
-                cols = slice(CHUNK * n, CHUNK * (n + 1))
-                nc.scalar.copy(out=trust_all[:, cols], in_=trust_banks[n][:])
-
-            def stir(n):
-                for i in range(n):
-                    bank = turned.tile([P, CHUNK], F32, name="bank")
-                    nc.tensor.matmul(bank[:], warm[:, :P], warm[:], start=True, stop=True)
-
             nc.vector.tensor_scalar(out=neg[:], in0=scale[:], scalar1=-1.0, scalar2=None, op0=MULT)
-            stir(6)
+            stir(4)
             widen(0, 0, 16)
+            turn_t(0, 0)
+            take_t(0, 0)
+            turn_t(0, 1)
+            take_t(0, 1)
+            spread_trust(0)
+            take_trust(0)
+            spread_trust(1)
+            take_trust(1)
+            quant_t(0, 0, 2)
+            quant_t(0, 2, 4)
+            open_group(0, 0)
+            widen(1, 0, 16)
+            spread_trust(2)
+            take_trust(2)
+            turn_t(1, 0)
+            take_t(1, 0)
+            turn_t(1, 1)
+            take_t(1, 1)
+            open_group(0, 1)
+            perm_b(0)
+            perm_b(1)
+            quant_t(1)
+            turn_b(0)
+            take_b(0)
+            turn_b(1)
+            take_b(1)
+            perm_b(2)
+            perm_b(3)
+            open_group(1, 0)
+            perm_s(0)
+            quant_b(0, 0, 256)
+            perm_s(1)
+            turn_b(2)
+            take_b(2)
+            turn_b(3)
+            take_b(3)
             turn_s(0)
             take_s(0)
-            turn_b(0)
-            take_b(0, True)
-            turn_b(1)
-            take_b(1, True)
-            turn_t(0)
-            take_t(0, 0)
-            take_t(0, 1, False)
-            spread_trust(0)
-            quant_s(0)
-            turn_b(2)
-            take_b(2, True)
-            spread_trust(1)
-            turn_b(3)
-            spread_trust(2)
-            quant_t(0)
-            take_b(3, True)
-            widen(1, 0, 8)
-            quant_b(0)
-            widen(1, 8, 16)
-            open_group(0, 0)
             turn_s(1)
             take_s(1)
-            take_trust(0)
-            turn_b(4)
-            take_b(4, True)
-            close_group(0, 0)
-            quant_s(1)
-            perm_b(6)
-            perm_b(7)
-            turn_t(1)
-            take_t(1, 0)
-            take_t(1, 1)
-            turn_b(5)
-            take_b(5, False)
-            square(0, 0)
-            turn_b(6)
-            take_b(6, True)
-            quant_t(1)
-            weigh(0, 0)
-            perm_s(2)
-            turn_b(7)
-            take_b(7, True)
-            multiply(1, 0)
             widen(2, 0, 16)
-            quant_b(1)
-            take_trust(1)
-            turn_s(2)
-            turn_t(2)
-            take_s(2)
-            take_trust(2)
-            square(1, 0)
+            perm_s(2)
+            open_group(1, 1)
+            quant_b(0, 256, 512)
+            quant_s(0)
+            quant_s(1)
+            turn_t(2, 0)
             take_t(2, 0)
+            turn_t(2, 1)
             take_t(2, 1)
-            weigh(1, 0)
-            multiply(0, 1, True)
-            quant_s(2)
+            turn_s(2)
+            take_s(2)
+            close_group(0, 0)
+            close_group(1, 0)
+            square(0, 0)
+            square(1, 0)
+            for i in range(4, 8):
+                perm_b(i)
             quant_t(2)
-            perm_b(8)
-            square(0, 1)
-            perm_b(9)
-            multiply(1, 1)
-            perm_b(10)
-            weigh(0, 1)
-            perm_b(11)
+            quant_s(2)
+            for i in range(4, 8):
+                turn_b(i)
+                take_b(i)
+            widen(3, 0, 16)
+            perm_s(3)
+            multiply(2, 0)
+            open_group(2, 1)
+            weigh(0, 0)
+            weigh(1, 0)
+            quant_b(1)
+            square(2, 0)
+            turn_t(3, 0)
+            take_t(3, 0)
+            turn_t(3, 1)
+            take_t(3, 1)
+            turn_s(3)
+            take_s(3)
+            for i in range(8, 12):
+                perm_b(i)
+            for m in range(3):
+                close_group(m, 1)
+                square(m, 1)
+            open_group(0, 2)
+            weigh(2, 0)
+            quant_t(3)
+            quant_s(3)
             for i in range(8, 12):
                 turn_b(i)
-                take_b(i, True)
-            square(1, 1)
-            perm_s(3)
-            widen(3, 0, 8)
-            multiply(2, 0)
-            weigh(1, 1)
-            widen(3, 8, 16)
-            square(2, 0)
-            quant_b(2)
-            multiply(2, 1)
-            weigh(2, 0)
-            turn_s(3)
-            turn_t(3)
-            square(2, 1)
-            take_s(3)
-            take_t(3, 0)
-            take_t(3, 1)
-            multiply(0, 2, True)
-            weigh(2, 1)
+                take_b(i)
+            weigh(0, 1)
+            widen(4, 0, 16)
             perm_s(4)
-            widen(4, 0, 4)
-            quant_s(3)
-            quant_t(3)
+            multiply(3, 0)
+            square(3, 0)
+            multiply(3, 1)
+            weigh(1, 1)
+            quant_b(2)
+            open_group(1, 2)
+            weigh(2, 1)
+            square(3, 1)
+            turn_s(4)
+            take_s(4)
+            turn_t(4, 0)
+            take_t(4, 0)
+            turn_t(4, 1)
+            take_t(4, 1)
+            weigh(3, 0)
+            widen(5, 0, 8)
+            close_group(0, 2)
+            close_group(1, 2)
             square(0, 2)
-            multiply(1, 2)
-            widen(4, 4, 12)
-            weigh(0, 2)
             square(1, 2)
             multiply(2, 2)
-            widen(4, 12, 16)
+            quant_s(4)
+            quant_t(4)
+            widen(5, 8, 16)
+            perm_s(5)
+            square(2, 2)
+            multiply(3, 2)
+            weigh(3, 1)
+            weigh(0, 2)
             weigh(1, 2)
-            pending = (2, 2)
-            for m in range(3, TILES):
+            weigh(2, 2)
+            pending = (3, 2)
+            for m in range(4, TILES):
                 ahead = m + 1 < TILES
                 further = m + 2 < TILES
                 if ahead:
                     turn_s(m + 1)
-                    turn_t(m + 1)
+                    turn_t(m + 1, 0)
+                    turn_t(m + 1, 1)
                 multiply(m, 0)
                 square(*pending)
                 if ahead:
@@ -441,34 +462,32 @@ def tile_bank_relation_distill_d6_kernel(
                 weigh(m, 0)
                 if m < TILES - 1:
                     multiply(m, 2)
-                square(m, 1)
-                if further:
-                    widen(m + 2, 11, 16)
-                weigh(m, 1)
+                    square(m, 1)
+                    if further:
+                        widen(m + 2, 11, 16)
+                    weigh(m, 1)
                 pending = (m, 2)
             last = TILES - 1
-            half = CHUNK // 2
-            quarter = CHUNK // 4
             total = const.tile([P, TILES], F32, name="total")
-            rest = const.tile([P, 1], F32, name="rest")
-            for h in range(2):
-                acc = sums_pool.tile([P, CHUNK], F32, name="acc")
-                live["acc", last, 2, half * h] = acc
-                for j in range(2):
-                    lo = half * h + quarter * j
-                    view = acc[:, quarter * j : quarter * (j + 1)]
-                    passes_s(last, 2, view, lo, lo + quarter, True, False)
-                    passes_t(last, 2, view, lo, lo + quarter, False, True)
-                square(last, 2, half * h, half * (h + 1))
-                if h == 0:
-                    weigh(last, 2, 0, half, part=parts[:, last, 2:3])
-                    nc.vector.reduce_sum(out=total[:], in_=parts[:], axis=mybir.AxisListType.X)
-                    nc.vector.tensor_scalar(out=means[:, :last], in0=total[:, :last], scalar1=1.0 / N, scalar2=None, op0=MULT)
-            weigh(last, 2, half, CHUNK, part=rest[:, 0:1])
+            rest = const.tile([P, 2], F32, name="rest")
+            multiply(last, 2, 0, 256)
+            square(last, 1)
+            weigh(last, 1)
+            multiply(last, 2, 256, 384)
+            square(last, 2, 0, 256)
+            multiply(last, 2, 384, 512)
+            weigh(last, 2, 0, 256)
+            square(last, 2, 256, 384)
+            nc.vector.reduce_sum(out=total[:], in_=parts[:], axis=mybir.AxisListType.X)
+            weigh(last, 2, 256, 384, part=rest[:, 0:1])
+            square(last, 2, 384, 512)
+            nc.vector.tensor_scalar(out=means[:, :last], in0=total[:, :last], scalar1=1.0 / N, scalar2=None, op0=MULT)
+            nc.vector.tensor_tensor(out=total[:, last:], in0=total[:, last:], in1=rest[:, 0:1], op=mybir.AluOpType.add)
+            weigh(last, 2, 384, 512, part=rest[:, 1:2])
             nc.vector.tensor_scalar(
                 out=means[:, last:],
                 in0=total[:, last:],
-                scalar1=rest[:, 0:1],
+                scalar1=rest[:, 1:2],
                 scalar2=1.0 / N,
                 op0=mybir.AluOpType.add,
                 op1=MULT,

@@ -47,6 +47,8 @@ def tile_bank_relation_distill_d6_kernel(
         scale = const.tile([P, TILES, K // P], F32, name="scale")
         neg = const.tile([P, TILES, K // P], F32, name="neg")
         parts = const.tile([P, TILES, CHUNKS], F32, name="parts")
+        ends = const.tile([P, 5], F32, name="ends")
+        shares = const.tile([P, 5], F32, name="shares")
         means = const.tile([P, TILES], F32, name="means")
 
         t_view = teacher_bytes.rearrange("(p m) k -> p m k", m=TILES)
@@ -61,6 +63,13 @@ def tile_bank_relation_distill_d6_kernel(
 
         def load_s(m):
             nc.sync.dma_start(out=s_raw[m][:], in_=s_view[:, m, :])
+
+        def load_s_quadrants(m):
+            rows = student.rearrange("(s i m) (a k) -> m a i s k", s=4, i=32, a=4)[m]
+            for a in range(4):
+                nc.sync.dma_start(
+                    out=s_raw[m][32 * a : 32 * (a + 1), :].rearrange("p (s k) -> p s k", s=4), in_=rows[a]
+                )
 
         def load_t(m):
             nc.sync.dma_start(out=t_raw[m][:], in_=t_view[:, m, :])
@@ -95,9 +104,9 @@ def tile_bank_relation_distill_d6_kernel(
             return b, psum.tile(shape, dtype, name="bank%d" % b)
 
         def perm(key, raw, on_scalar):
-            x = wide.tile([P, GS, 2, P], F32, name="x")
+            x = wide.tile([P, GS, 2, P], F32, name="x", align_bytes=64)
             live[key] = x
-            src = raw[:].bitcast(F32).rearrange("p (g q u r) -> p g u q r", g=GS, u=2, r=8)
+            src = raw[:].bitcast(F32).rearrange("p (q g u r) -> p g u q r", g=GS, u=2, r=8)
             dst = x[:].rearrange("p g u (q r) -> p g u q r", r=8)
             if on_scalar:
                 nc.scalar.copy(out=dst, in_=src)
@@ -136,6 +145,18 @@ def tile_bank_relation_distill_d6_kernel(
             grouped = work.tile([P, GS, P, 2], F32, name="s_grouped", align_bytes=64)
             live["gs", m] = grouped
             take(grouped[:], live["bs", m], on_scalar)
+
+        def flip_s(m):
+            y = work.tile([P, GS, 2, P], F32, name="y", align_bytes=64, bufs=2)
+            live["ys", m] = y
+            nc.vector.transpose(
+                out=y[:].rearrange("p g u r -> p (g u r)"), in_=live["xs", m][:].rearrange("p g u r -> p (g u r)")
+            )
+
+        def weave_s(m):
+            grouped = work.tile([P, GS, P, 2], F32, name="s_grouped", align_bytes=64)
+            live["gs", m] = grouped
+            nc.scalar.copy(out=grouped[:], in_=live["ys", m][:].rearrange("p g u r -> p g r u"))
 
         def quant_s(m):
             codes = keep.tile([P, GS, P], U32, name="s_codes", align_bytes=64)
@@ -306,7 +327,8 @@ def tile_bank_relation_distill_d6_kernel(
             load_b(8, 12)
             for m in range(4, TILES):
                 load_t(m)
-                load_s(m)
+            for m in range(4, TILES):
+                load_s_quadrants(m)
             nc.vector.tensor_scalar(out=neg[:], in0=scale[:], scalar1=-1.0, scalar2=None, op0=MULT)
             stir(4)
             widen(0, 0, 16)
@@ -399,97 +421,108 @@ def tile_bank_relation_distill_d6_kernel(
             for i in range(8, 12):
                 turn_b(i)
                 take_b(i)
-            weigh(0, 1)
             widen(4, 0, 16)
-            perm_s(4)
             multiply(3, 0)
             square(3, 0)
             multiply(3, 1)
-            weigh(1, 1)
+            weigh(0, 1)
             quant_b(2)
+            widen(5, 0, 16)
             open_group(1, 2)
-            weigh(2, 1)
             square(3, 1)
-            turn_s(4)
-            take_s(4)
-            turn_t(4, 0)
-            take_t(4, 0)
-            turn_t(4, 1)
-            take_t(4, 1)
-            weigh(3, 0)
-            widen(5, 0, 8)
+            perm_s(4, True)
+            for m in (4, 5):
+                for h in range(2):
+                    turn_t(m, h)
+                    take_t(m, h)
+            weigh(1, 1)
+            flip_s(4)
+            weigh(2, 1)
             close_group(0, 2)
             close_group(1, 2)
             square(0, 2)
+            weave_s(4)
             square(1, 2)
+            perm_s(5, True)
             multiply(2, 2)
-            quant_s(4)
             quant_t(4)
-            widen(5, 8, 16)
-            perm_s(5)
+            weigh(3, 0)
+            quant_t(5)
+            quant_s(4)
+            weigh(3, 1)
             square(2, 2)
             multiply(3, 2)
-            weigh(3, 1)
+            flip_s(5)
             weigh(0, 2)
+            widen(6, 0, 16)
+            weave_s(5)
+            square(3, 2)
+            multiply(4, 0)
             weigh(1, 2)
+            quant_s(5)
             weigh(2, 2)
-            pending = (3, 2)
-            for m in range(4, TILES):
-                ahead = m + 1 < TILES
-                further = m + 2 < TILES
-                if ahead:
-                    turn_s(m + 1)
-                    turn_t(m + 1, 0)
-                    turn_t(m + 1, 1)
-                multiply(m, 0)
-                square(*pending)
-                if ahead:
-                    take_s(m + 1)
-                    take_t(m + 1, 0)
-                    take_t(m + 1, 1)
-                if further:
-                    widen(m + 2, 0, 6)
-                weigh(*pending)
-                if further:
-                    perm_s(m + 2)
-                if ahead:
-                    quant_s(m + 1)
-                    quant_t(m + 1)
-                multiply(m, 1)
-                square(m, 0)
-                if further:
-                    widen(m + 2, 6, 11)
-                weigh(m, 0)
-                if m < TILES - 1:
-                    multiply(m, 2)
-                    square(m, 1)
-                    if further:
-                        widen(m + 2, 11, 16)
-                    weigh(m, 1)
-                pending = (m, 2)
+            square(4, 0)
+            perm_s(6, True)
+            multiply(4, 1)
+            widen(7, 0, 16)
+            square(4, 1)
+            multiply(4, 2)
+            weigh(3, 2)
+            flip_s(6)
+            for m in (6, 7):
+                for h in range(2):
+                    turn_t(m, h)
+            square(4, 2)
+            for m in (6, 7):
+                for h in range(2):
+                    take_t(m, h)
+            multiply(5, 0)
+            weigh(4, 0)
+            weigh(4, 1)
+            weave_s(6)
+            square(5, 0)
+            perm_s(7, True)
+            multiply(5, 1)
+            weigh(4, 2)
+            quant_t(6)
+            quant_s(6)
+            quant_t(7)
+            square(5, 1)
+            multiply(5, 2)
+            flip_s(7)
+            weigh(5, 0)
+            weave_s(7)
+            square(5, 2)
+            multiply(6, 0)
+            weigh(5, 1)
+            quant_s(7)
+            weigh(5, 2)
+            square(6, 0)
+            multiply(6, 1)
+            weigh(6, 0)
+            multiply(6, 2)
+            square(6, 1)
+            weigh(6, 1)
             last = TILES - 1
-            total = const.tile([P, TILES], F32, name="total")
-            rest = const.tile([P, 2], F32, name="rest")
+            total = const.tile([P, last], F32, name="total")
+            multiply(last, 0)
+            square(last - 1, 2)
+            weigh(last - 1, 2)
+            multiply(last, 1)
+            square(last, 0)
+            nc.vector.reduce_sum(out=total[:], in_=parts[:, :last, :], axis=mybir.AxisListType.X)
+            weigh(last, 0, part=ends[:, 0:1])
+            nc.vector.tensor_scalar(out=means[:, :last], in0=total[:], scalar1=1.0 / N, scalar2=None, op0=MULT)
             multiply(last, 2, 0, 256)
             square(last, 1)
-            weigh(last, 1)
+            weigh(last, 1, part=ends[:, 1:2])
             multiply(last, 2, 256, 384)
             square(last, 2, 0, 256)
+            weigh(last, 2, 0, 256, part=ends[:, 2:3])
             multiply(last, 2, 384, 512)
-            weigh(last, 2, 0, 256)
             square(last, 2, 256, 384)
-            nc.vector.reduce_sum(out=total[:], in_=parts[:], axis=mybir.AxisListType.X)
-            weigh(last, 2, 256, 384, part=rest[:, 0:1])
+            weigh(last, 2, 256, 384, part=ends[:, 3:4])
             square(last, 2, 384, 512)
-            nc.vector.tensor_scalar(out=means[:, :last], in0=total[:, :last], scalar1=1.0 / N, scalar2=None, op0=MULT)
-            nc.vector.tensor_tensor(out=total[:, last:], in0=total[:, last:], in1=rest[:, 0:1], op=mybir.AluOpType.add)
-            weigh(last, 2, 384, 512, part=rest[:, 1:2])
-            nc.vector.tensor_scalar(
-                out=means[:, last:],
-                in0=total[:, last:],
-                scalar1=rest[:, 1:2],
-                scalar2=1.0 / N,
-                op0=mybir.AluOpType.add,
-                op1=MULT,
-            )
+            weigh(last, 2, 384, 512, part=ends[:, 4:5])
+            nc.vector.tensor_scalar(out=shares[:], in0=ends[:], scalar1=1.0 / N, scalar2=None, op0=MULT, op1=mybir.AluOpType.add, accum_out=means[:, last:])
             nc.scalar.dma_start(out=out_1.rearrange("(p m) -> p m", m=TILES), in_=means[:])

@@ -34,7 +34,6 @@ def tile_bank_relation_distill_d6_kernel(
         const = ctx.enter_context(tc.tile_pool(name="const", bufs=1))
         work = ctx.enter_context(tc.tile_pool(name="work", bufs=3))
         keep = ctx.enter_context(tc.tile_pool(name="keep", bufs=6))
-        outs = ctx.enter_context(tc.tile_pool(name="outs", bufs=6))
         wide = ctx.enter_context(tc.tile_pool(name="wide", bufs=4))
         psum = ctx.enter_context(tc.psum_pool(name="psum", bufs=1))
 
@@ -64,12 +63,17 @@ def tile_bank_relation_distill_d6_kernel(
         def load_s(m):
             nc.sync.dma_start(out=s_raw[m][:], in_=s_view[:, m, :])
 
+        def load_quadrants(raw, rows):
+            for a in (0, 2, 1, 3):
+                nc.sync.dma_start(out=raw[32 * a : 32 * (a + 1), :].rearrange("p (s k) -> p s k", s=4), in_=rows[a])
+
         def load_s_quadrants(m):
             rows = student.rearrange("(s i m) (a k) -> m a i s k", s=4, i=32, a=4)[m]
-            for a in range(4):
-                nc.sync.dma_start(
-                    out=s_raw[m][32 * a : 32 * (a + 1), :].rearrange("p (s k) -> p s k", s=4), in_=rows[a]
-                )
+            load_quadrants(s_raw[m], rows)
+
+        def load_b_quadrants(i):
+            rows = sbank[P * i : P * (i + 1), :].rearrange("(s i) (a k) -> a i s k", s=4, a=4)
+            load_quadrants(b_raw[i], rows)
 
         def load_t(m):
             nc.sync.dma_start(out=t_raw[m][:], in_=t_view[:, m, :])
@@ -146,17 +150,36 @@ def tile_bank_relation_distill_d6_kernel(
             live["gs", m] = grouped
             take(grouped[:], live["bs", m], on_scalar)
 
-        def flip_s(m):
-            y = work.tile([P, GS, 2, P], F32, name="y", align_bytes=64, bufs=2)
-            live["ys", m] = y
+        def flip(key):
+            y = work.tile([P, GS, 2, P], F32, name="y", align_bytes=64, bufs=3)
             nc.vector.transpose(
-                out=y[:].rearrange("p g u r -> p (g u r)"), in_=live["xs", m][:].rearrange("p g u r -> p (g u r)")
+                out=y[:].rearrange("p g u r -> p (g u r)"), in_=live[key][:].rearrange("p g u r -> p (g u r)")
             )
+            return y
 
-        def weave_s(m):
+        def flip_s(m):
+            live["ys", m] = flip(("xs", m))
+
+        def flip_b(i):
+            live["yb", i] = flip(("xb", i))
+
+        def weave(dst, y, on_scalar):
+            src = y[:].rearrange("p g u r -> p g r u")
+            if on_scalar:
+                nc.scalar.copy(out=dst, in_=src)
+            else:
+                nc.vector.tensor_copy(out=dst, in_=src)
+
+        def weave_s(m, on_scalar=True):
             grouped = work.tile([P, GS, P, 2], F32, name="s_grouped", align_bytes=64)
             live["gs", m] = grouped
-            nc.scalar.copy(out=grouped[:], in_=live["ys", m][:].rearrange("p g u r -> p g r u"))
+            weave(grouped[:], live["ys", m], on_scalar)
+
+        def weave_b(i, on_scalar=True):
+            c, j = divmod(i, 4)
+            if j == 0:
+                live["gb", c] = work.tile([P, GS, CHUNK, 2], F32, name="b_grouped", align_bytes=64, bufs=2)
+            weave(live["gb", c][:, :, P * j : P * (j + 1), :], live["yb", i], on_scalar)
 
         def quant_s(m):
             codes = keep.tile([P, GS, P], U32, name="s_codes", align_bytes=64)
@@ -263,14 +286,14 @@ def tile_bank_relation_distill_d6_kernel(
             passes_s(m, n, live["acc", m, n, 0][1][:], 0, CHUNK, False, True)
 
         def square(m, n, lo=0, hi=CHUNK):
-            sq = work.tile([P, CHUNK], F32, name="sq", bufs=5)
+            sq = work.tile([P, CHUNK], F32, name="sq", bufs=14)
             live["sq", m, n, lo] = sq
             b, acc = live["acc", m, n, lo]
             idle.append(b)
             nc.scalar.activation(out=sq[:, : hi - lo], in_=acc[:, : hi - lo], func=SQUARE)
 
         def weigh(m, n, lo=0, hi=CHUNK, part=None):
-            res = outs.tile([P, CHUNK], F32, name="res")
+            res = live["sq", m, n, lo]
             cols = slice(CHUNK * n + lo, CHUNK * n + hi)
             nc.vector.scalar_tensor_tensor(
                 out=res[:, : hi - lo],
@@ -321,14 +344,19 @@ def tile_bank_relation_distill_d6_kernel(
             load_s(2)
             load_b(4, 8)
             load_t(3)
-            load_s(3)
             load_scales(2)
             load_words(2)
-            load_b(8, 12)
-            for m in range(4, TILES):
-                load_t(m)
-            for m in range(4, TILES):
-                load_s_quadrants(m)
+            load_s_quadrants(3)
+            load_b_quadrants(8)
+            load_b_quadrants(9)
+            load_t(4)
+            load_b_quadrants(10)
+            load_b_quadrants(11)
+            load_t(5)
+            load_s_quadrants(4)
+            load_t(6)
+            load_s_quadrants(5)
+            load_t(7)
             nc.vector.tensor_scalar(out=neg[:], in0=scale[:], scalar1=-1.0, scalar2=None, op0=MULT)
             stir(4)
             widen(0, 0, 16)
@@ -396,78 +424,85 @@ def tile_bank_relation_distill_d6_kernel(
                 turn_b(i)
                 take_b(i)
             widen(3, 0, 16)
-            perm_s(3)
             multiply(2, 0)
             open_group(2, 1)
-            weigh(0, 0)
-            weigh(1, 0)
+            perm_s(3, True)
             quant_b(1)
             square(2, 0)
             turn_t(3, 0)
             take_t(3, 0)
             turn_t(3, 1)
             take_t(3, 1)
-            turn_s(3)
-            take_s(3)
-            for i in range(8, 12):
-                perm_b(i)
+            flip_s(3)
+            perm_b(8)
+            perm_b(9)
             for m in range(3):
                 close_group(m, 1)
-                square(m, 1)
+            weave_s(3)
+            square(0, 1)
             open_group(0, 2)
-            weigh(2, 0)
             quant_t(3)
+            flip_b(8)
             quant_s(3)
-            for i in range(8, 12):
-                turn_b(i)
-                take_b(i)
+            square(1, 1)
+            weave_b(8)
+            square(2, 1)
+            flip_b(9)
             widen(4, 0, 16)
             multiply(3, 0)
+            perm_b(10, True)
+            weave_b(9)
+            perm_b(11, True)
+            flip_b(10)
             square(3, 0)
             multiply(3, 1)
-            weigh(0, 1)
-            quant_b(2)
+            quant_b(2, 0, 256)
+            flip_b(11)
+            weave_b(10)
+            weave_b(11)
             widen(5, 0, 16)
             open_group(1, 2)
             square(3, 1)
-            perm_s(4, True)
+            perm_s(4)
+            quant_b(2, 256, 512)
+            weigh(0, 0)
+            load_s_quadrants(6)
             for m in (4, 5):
                 for h in range(2):
                     turn_t(m, h)
                     take_t(m, h)
-            weigh(1, 1)
             flip_s(4)
-            weigh(2, 1)
+            weigh(1, 0)
             close_group(0, 2)
             close_group(1, 2)
-            square(0, 2)
             weave_s(4)
+            square(0, 2)
             square(1, 2)
-            perm_s(5, True)
             multiply(2, 2)
             quant_t(4)
-            weigh(3, 0)
-            quant_t(5)
+            weigh(2, 0)
+            load_s_quadrants(7)
             quant_s(4)
-            weigh(3, 1)
+            quant_t(5)
+            perm_s(5, True)
             square(2, 2)
             multiply(3, 2)
+            weigh(0, 1)
             flip_s(5)
-            weigh(0, 2)
             widen(6, 0, 16)
             weave_s(5)
             square(3, 2)
             multiply(4, 0)
-            weigh(1, 2)
+            weigh(1, 1)
             quant_s(5)
-            weigh(2, 2)
+            weigh(2, 1)
             square(4, 0)
             perm_s(6, True)
             multiply(4, 1)
             widen(7, 0, 16)
             square(4, 1)
             multiply(4, 2)
-            weigh(3, 2)
+            weigh(3, 0)
             flip_s(6)
             for m in (6, 7):
                 for h in range(2):
@@ -477,31 +512,36 @@ def tile_bank_relation_distill_d6_kernel(
                 for h in range(2):
                     take_t(m, h)
             multiply(5, 0)
-            weigh(4, 0)
-            weigh(4, 1)
+            weigh(3, 1)
+            weigh(0, 2)
             weave_s(6)
             square(5, 0)
             perm_s(7, True)
             multiply(5, 1)
-            weigh(4, 2)
+            weigh(1, 2)
             quant_t(6)
             quant_s(6)
             quant_t(7)
             square(5, 1)
             multiply(5, 2)
             flip_s(7)
-            weigh(5, 0)
+            weigh(2, 2)
             weave_s(7)
             square(5, 2)
             multiply(6, 0)
-            weigh(5, 1)
+            weigh(3, 2)
             quant_s(7)
-            weigh(5, 2)
+            weigh(4, 0)
+            weigh(4, 1)
             square(6, 0)
             multiply(6, 1)
-            weigh(6, 0)
-            multiply(6, 2)
+            weigh(4, 2)
+            weigh(5, 0)
+            weigh(5, 1)
             square(6, 1)
+            multiply(6, 2)
+            weigh(5, 2)
+            weigh(6, 0)
             weigh(6, 1)
             last = TILES - 1
             total = const.tile([P, last], F32, name="total")

@@ -34,7 +34,7 @@ def tile_bank_relation_distill_d6_kernel(
         const = ctx.enter_context(tc.tile_pool(name="const", bufs=1))
         work = ctx.enter_context(tc.tile_pool(name="work", bufs=3))
         keep = ctx.enter_context(tc.tile_pool(name="keep", bufs=6))
-        wide = ctx.enter_context(tc.tile_pool(name="wide", bufs=4))
+        wide = ctx.enter_context(tc.tile_pool(name="wide", bufs=6))
         psum = ctx.enter_context(tc.psum_pool(name="psum", bufs=1))
 
         ident = const.tile([P, P], F32, name="ident")
@@ -45,7 +45,8 @@ def tile_bank_relation_distill_d6_kernel(
         tb_scales = [const.tile([P, GT, CHUNK], U8, name="tb_scales%d" % n, align_bytes=64) for n in range(CHUNKS)]
         scale = const.tile([P, TILES, K // P], F32, name="scale")
         neg = const.tile([P, TILES, K // P], F32, name="neg")
-        parts = const.tile([P, TILES, CHUNKS], F32, name="parts")
+        total = const.tile([P, TILES - 1], F32, name="total")
+        sixth = const.tile([P, CHUNKS], F32, name="sixth")
         ends = const.tile([P, 5], F32, name="ends")
         shares = const.tile([P, 5], F32, name="shares")
         means = const.tile([P, TILES], F32, name="means")
@@ -82,11 +83,11 @@ def tile_bank_relation_distill_d6_kernel(
             for i in range(lo, hi):
                 nc.sync.dma_start(out=b_raw[i][:], in_=sbank[P * i : P * (i + 1), :])
 
-        def load_words(c):
+        def load_words(c, g0=0, g1=GT):
             cols = slice(2 * CHUNK * c, 2 * CHUNK * (c + 1))
             nc.sync.dma_start(
-                out=tb_words[c][:].bitcast(I32),
-                in_=tbank_words[:, :, cols].rearrange("g p w -> p g w").bitcast(I32),
+                out=tb_words[c][:, g0:g1].bitcast(I32),
+                in_=tbank_words[g0:g1, :, cols].rearrange("g p w -> p g w").bitcast(I32),
             )
 
         def clear_scales(c):
@@ -205,6 +206,24 @@ def tile_bank_relation_distill_d6_kernel(
                     op0=MULT,
                 )
 
+        def widen_flat(m, lo, hi):
+            if lo == 0:
+                live["flat", m] = work.tile([P, K], BF16, name="flat", align_bytes=64, bufs=1)
+            for c in range(lo, hi):
+                nc.scalar.activation(
+                    out=live["flat", m][:, P * c : P * (c + 1)],
+                    in_=t_raw[m][:, P * c : P * (c + 1)].bitcast(FP8),
+                    func=mybir.ActivationFunctionType.Copy,
+                    scale=neg[:, m, c : c + 1],
+                )
+
+        def part_t(m):
+            live["xt", m] = work.tile([P, GT, 2, P, 2], BF16, name="xt", align_bytes=64)
+            nc.vector.tensor_copy(
+                out=live["xt", m][:].rearrange("p g u w e -> p (g u w e)").bitcast(F32).rearrange("p (g u w) -> p g u w", g=GT, u=2),
+                in_=live["flat", m][:].bitcast(F32).rearrange("p (g w u) -> p g u w", g=GT, u=2),
+            )
+
         def turn_t(m, h):
             words = live["xt", m][:].rearrange("p g u w e -> p (g u w e)").bitcast(F32)
             b, bank = claim([P, 2, 2, P], F32)
@@ -286,25 +305,26 @@ def tile_bank_relation_distill_d6_kernel(
             passes_s(m, n, live["acc", m, n, 0][1][:], 0, CHUNK, False, True)
 
         def square(m, n, lo=0, hi=CHUNK):
-            sq = work.tile([P, CHUNK], F32, name="sq", bufs=14)
-            live["sq", m, n, lo] = sq
+            if ("sq", m) not in live:
+                live["sq", m] = work.tile([P, N], F32, name="sq", bufs=6)
             b, acc = live["acc", m, n, lo]
             idle.append(b)
-            nc.scalar.activation(out=sq[:, : hi - lo], in_=acc[:, : hi - lo], func=SQUARE)
+            nc.scalar.activation(
+                out=live["sq", m][:, CHUNK * n + lo : CHUNK * n + hi], in_=acc[:, : hi - lo], func=SQUARE
+            )
 
-        def weigh(m, n, lo=0, hi=CHUNK, part=None):
-            res = live["sq", m, n, lo]
-            cols = slice(CHUNK * n + lo, CHUNK * n + hi)
+        def weigh(m, lo=0, hi=N, part=None):
+            res = live["sq", m][:, lo:hi]
             nc.vector.scalar_tensor_tensor(
-                out=res[:, : hi - lo],
-                in0=live["sq", m, n, lo][:, : hi - lo],
+                out=res,
+                in0=res,
                 scalar=1.0,
-                in1=trust_all[:, cols],
+                in1=trust_all[:, lo:hi],
                 op0=MULT,
                 op1=MULT,
-                accum_out=parts[:, m, n : n + 1] if part is None else part,
+                accum_out=total[:, m : m + 1] if part is None else part,
             )
-            nc.sync.dma_start(out=o_view[:, m, cols], in_=res[:, : hi - lo])
+            nc.sync.dma_start(out=o_view[:, m, lo:hi], in_=res)
 
         def spread_trust(n):
             b, bank = claim([P, CHUNK], BF16)
@@ -323,8 +343,8 @@ def tile_bank_relation_distill_d6_kernel(
             nc.scalar.copy(out=trust_all[:, CHUNK * n : CHUNK * (n + 1)], in_=bank[:])
 
         with tc.manual_schedule():
-            nc.vector.memset(ones[:], 1.0)
             nc.vector.memset(trust_row[:].bitcast(I32), 0)
+            nc.vector.memset(ones[:], 1.0)
             clear_scales(0)
             make_identity(nc, ident[:])
             clear_scales(1)
@@ -333,125 +353,122 @@ def tile_bank_relation_distill_d6_kernel(
             load_t(0)
             nc.sync.dma_start(out=trust_row[0:1, :], in_=trust.rearrange("(o n) -> o n", o=1))
             load_scales(0)
-            load_words(0)
+            load_words(0, 0, 2)
             load_t(1)
+            load_words(0, 2, 4)
+            load_t(2)
             load_scales(1)
-            load_words(1)
+            load_words(1, 0, 2)
+            load_words(1, 2, 4)
             load_b(0, 4)
             load_s(0)
             load_s(1)
-            load_t(2)
             load_s(2)
             load_b(4, 8)
             load_t(3)
+            load_s(3)
+            load_t(4)
             load_scales(2)
             load_words(2)
-            load_s_quadrants(3)
             load_b_quadrants(8)
             load_b_quadrants(9)
-            load_t(4)
+            load_t(5)
             load_b_quadrants(10)
             load_b_quadrants(11)
-            load_t(5)
             load_s_quadrants(4)
             load_t(6)
             load_s_quadrants(5)
             load_t(7)
+            load_s_quadrants(6)
+            load_s_quadrants(7)
             nc.vector.tensor_scalar(out=neg[:], in0=scale[:], scalar1=-1.0, scalar2=None, op0=MULT)
             stir(4)
             widen(0, 0, 16)
+            spread_trust(0)
+            take_trust(0)
             turn_t(0, 0)
             take_t(0, 0)
             turn_t(0, 1)
             take_t(0, 1)
-            spread_trust(0)
-            take_trust(0)
             spread_trust(1)
             take_trust(1)
-            quant_t(0, 0, 2)
-            quant_t(0, 2, 4)
-            open_group(0, 0)
-            widen(1, 0, 16)
             spread_trust(2)
             take_trust(2)
+            quant_t(0, 0, 2)
+            widen(1, 0, 4)
+            quant_t(0, 2, 4)
+            open_group(0, 0)
+            widen(1, 4, 16)
             turn_t(1, 0)
             take_t(1, 0)
             turn_t(1, 1)
             take_t(1, 1)
-            open_group(0, 1)
-            perm_b(0)
-            perm_b(1)
-            quant_t(1)
-            turn_b(0)
-            take_b(0)
-            turn_b(1)
-            take_b(1)
-            perm_b(2)
-            perm_b(3)
-            open_group(1, 0)
-            perm_s(0)
-            quant_b(0, 0, 256)
-            perm_s(1)
-            turn_b(2)
-            take_b(2)
-            turn_b(3)
-            take_b(3)
-            turn_s(0)
-            take_s(0)
-            turn_s(1)
-            take_s(1)
             widen(2, 0, 16)
-            perm_s(2)
-            open_group(1, 1)
-            quant_b(0, 256, 512)
-            quant_s(0)
-            quant_s(1)
+            open_group(0, 1)
+            quant_t(1)
             turn_t(2, 0)
             take_t(2, 0)
             turn_t(2, 1)
             take_t(2, 1)
-            turn_s(2)
-            take_s(2)
-            close_group(0, 0)
-            close_group(1, 0)
-            square(0, 0)
-            square(1, 0)
-            for i in range(4, 8):
+            for i in range(4):
                 perm_b(i)
+            open_group(1, 0)
             quant_t(2)
+            for i in range(4):
+                turn_b(i)
+                take_b(i)
+            for m in range(3):
+                perm_s(m)
+            open_group(1, 1)
+            quant_b(0, 0, 256)
+            for m in range(3):
+                turn_s(m)
+                take_s(m)
+            perm_b(4)
+            perm_b(5)
+            quant_b(0, 256, 512)
+            open_group(2, 0)
+            perm_b(6)
+            quant_s(0)
+            perm_b(7)
+            quant_s(1)
             quant_s(2)
+            for m in range(3):
+                close_group(m, 0)
+                square(m, 0)
             for i in range(4, 8):
                 turn_b(i)
                 take_b(i)
             widen(3, 0, 16)
-            multiply(2, 0)
+            perm_s(3)
+            widen(4, 0, 16)
             open_group(2, 1)
-            perm_s(3, True)
-            quant_b(1)
-            square(2, 0)
+            open_group(0, 2)
+            quant_b(1, 0, 256)
+            quant_b(1, 256, 512)
             turn_t(3, 0)
             take_t(3, 0)
             turn_t(3, 1)
             take_t(3, 1)
-            flip_s(3)
+            turn_s(3)
+            take_s(3)
             perm_b(8)
             perm_b(9)
+            flip_b(8)
             for m in range(3):
                 close_group(m, 1)
-            weave_s(3)
-            square(0, 1)
-            open_group(0, 2)
             quant_t(3)
-            flip_b(8)
             quant_s(3)
-            square(1, 1)
+            square(0, 1)
             weave_b(8)
-            square(2, 1)
+            open_group(1, 2)
             flip_b(9)
-            widen(4, 0, 16)
-            multiply(3, 0)
+            widen(5, 0, 16)
+            square(1, 1)
             perm_b(10, True)
+            square(2, 1)
             weave_b(9)
+            multiply(3, 0)
             perm_b(11, True)
             flip_b(10)
             square(3, 0)
@@ -460,109 +477,94 @@ def tile_bank_relation_distill_d6_kernel(
             flip_b(11)
             weave_b(10)
             weave_b(11)
-            widen(5, 0, 16)
-            open_group(1, 2)
             square(3, 1)
-            perm_s(4)
-            quant_b(2, 256, 512)
-            weigh(0, 0)
-            load_s_quadrants(6)
+            open_group(2, 2)
             for m in (4, 5):
                 for h in range(2):
                     turn_t(m, h)
-                    take_t(m, h)
+            perm_s(4)
+            quant_b(2, 256, 512)
             flip_s(4)
-            weigh(1, 0)
-            close_group(0, 2)
-            close_group(1, 2)
+            take_t(4, 0)
+            take_t(4, 1)
             weave_s(4)
-            square(0, 2)
-            square(1, 2)
-            multiply(2, 2)
+            take_t(5, 0)
+            take_t(5, 1)
+            perm_s(5)
+            for m in range(3):
+                close_group(m, 2)
+                square(m, 2)
             quant_t(4)
-            weigh(2, 0)
-            load_s_quadrants(7)
+            flip_s(5)
             quant_s(4)
             quant_t(5)
-            perm_s(5, True)
-            square(2, 2)
             multiply(3, 2)
-            weigh(0, 1)
-            flip_s(5)
-            widen(6, 0, 16)
             weave_s(5)
+            weigh(0)
             square(3, 2)
             multiply(4, 0)
-            weigh(1, 1)
             quant_s(5)
-            weigh(2, 1)
+            widen(6, 0, 16)
+            widen_flat(7, 0, 8)
             square(4, 0)
             perm_s(6, True)
             multiply(4, 1)
-            widen(7, 0, 16)
+            weigh(1)
+            widen_flat(7, 8, 16)
             square(4, 1)
             multiply(4, 2)
-            weigh(3, 0)
             flip_s(6)
+            part_t(7)
+            square(4, 2)
+            weave_s(6)
+            perm_s(7, True)
+            multiply(5, 0)
+            weigh(2)
             for m in (6, 7):
                 for h in range(2):
                     turn_t(m, h)
-            square(4, 2)
+            square(5, 0)
             for m in (6, 7):
                 for h in range(2):
                     take_t(m, h)
-            multiply(5, 0)
-            weigh(3, 1)
-            weigh(0, 2)
-            weave_s(6)
-            square(5, 0)
-            perm_s(7, True)
             multiply(5, 1)
-            weigh(1, 2)
-            quant_t(6)
             quant_s(6)
-            quant_t(7)
+            flip_s(7)
+            quant_t(6)
+            weave_s(7)
             square(5, 1)
             multiply(5, 2)
-            flip_s(7)
-            weigh(2, 2)
-            weave_s(7)
+            quant_t(7)
+            weigh(3)
+            quant_s(7)
+            weigh(4)
             square(5, 2)
             multiply(6, 0)
-            weigh(3, 2)
-            quant_s(7)
-            weigh(4, 0)
-            weigh(4, 1)
+            weigh(5)
             square(6, 0)
             multiply(6, 1)
-            weigh(4, 2)
-            weigh(5, 0)
-            weigh(5, 1)
             square(6, 1)
+            weigh(6, 0, 1024, part=sixth[:, 0:1])
             multiply(6, 2)
-            weigh(5, 2)
-            weigh(6, 0)
-            weigh(6, 1)
             last = TILES - 1
-            total = const.tile([P, last], F32, name="total")
             multiply(last, 0)
             square(last - 1, 2)
-            weigh(last - 1, 2)
+            weigh(last - 1, 1024, 1536, part=sixth[:, 1:2])
             multiply(last, 1)
             square(last, 0)
-            nc.vector.reduce_sum(out=total[:], in_=parts[:, :last, :], axis=mybir.AxisListType.X)
-            weigh(last, 0, part=ends[:, 0:1])
+            nc.vector.tensor_tensor(out=total[:, last - 1 :], in0=sixth[:, 0:1], in1=sixth[:, 1:2], op=mybir.AluOpType.add)
+            weigh(last, 0, 512, part=ends[:, 0:1])
             nc.vector.tensor_scalar(out=means[:, :last], in0=total[:], scalar1=1.0 / N, scalar2=None, op0=MULT)
             multiply(last, 2, 0, 256)
             square(last, 1)
-            weigh(last, 1, part=ends[:, 1:2])
+            weigh(last, 512, 1024, part=ends[:, 1:2])
             multiply(last, 2, 256, 384)
             square(last, 2, 0, 256)
-            weigh(last, 2, 0, 256, part=ends[:, 2:3])
+            weigh(last, 1024, 1280, part=ends[:, 2:3])
             multiply(last, 2, 384, 512)
             square(last, 2, 256, 384)
-            weigh(last, 2, 256, 384, part=ends[:, 3:4])
+            weigh(last, 1280, 1408, part=ends[:, 3:4])
             square(last, 2, 384, 512)
-            weigh(last, 2, 384, 512, part=ends[:, 4:5])
+            weigh(last, 1408, 1536, part=ends[:, 4:5])
             nc.vector.tensor_scalar(out=shares[:], in0=ends[:], scalar1=1.0 / N, scalar2=None, op0=MULT, op1=mybir.AluOpType.add, accum_out=means[:, last:])
             nc.scalar.dma_start(out=out_1.rearrange("(p m) -> p m", m=TILES), in_=means[:])

@@ -38,7 +38,7 @@ def tile_bank_relation_distill_d6_kernel(
         psum = ctx.enter_context(tc.psum_pool(name="psum", bufs=1))
 
         ident = const.tile([P, P], F32, name="ident")
-        ones = const.tile([P, CHUNK], BF16, name="ones")
+        ones = const.tile([P, P], BF16, name="ones")
         trust_row = const.tile([P, N], BF16, name="trust_row")
         trust_all = const.tile([P, N], BF16, name="trust_all")
         tb_words = [const.tile([P, GT, 2 * CHUNK], U8, name="tb_words%d" % n, align_bytes=64) for n in range(CHUNKS)]
@@ -46,9 +46,9 @@ def tile_bank_relation_distill_d6_kernel(
         scale = const.tile([P, TILES, K // P], F32, name="scale")
         neg = const.tile([P, TILES, K // P], F32, name="neg")
         total = const.tile([P, TILES - 1], F32, name="total")
-        sixth = const.tile([P, CHUNKS], F32, name="sixth")
-        ends = const.tile([P, 5], F32, name="ends")
-        shares = const.tile([P, 5], F32, name="shares")
+        early = const.tile([P, 2], F32, name="early")
+        ends = const.tile([P, 6], F32, name="ends")
+        shares = const.tile([P, 6], F32, name="shares")
         means = const.tile([P, TILES], F32, name="means")
 
         t_view = teacher_bytes.rearrange("(p m) k -> p m k", m=TILES)
@@ -313,7 +313,7 @@ def tile_bank_relation_distill_d6_kernel(
                 out=live["sq", m][:, CHUNK * n + lo : CHUNK * n + hi], in_=acc[:, : hi - lo], func=SQUARE
             )
 
-        def weigh(m, lo=0, hi=N, part=None):
+        def weigh(m, lo=0, hi=N, part=None, queue=nc.sync):
             res = live["sq", m][:, lo:hi]
             nc.vector.scalar_tensor_tensor(
                 out=res,
@@ -324,18 +324,18 @@ def tile_bank_relation_distill_d6_kernel(
                 op1=MULT,
                 accum_out=total[:, m : m + 1] if part is None else part,
             )
-            nc.sync.dma_start(out=o_view[:, m, lo:hi], in_=res)
+            queue.dma_start(out=o_view[:, m, lo:hi], in_=res)
 
         def spread_trust(n):
             b, bank = claim([P, CHUNK], BF16)
             live["trust", n] = (b, bank)
-            nc.tensor.matmul(bank[:], ones[:, :P], trust_row[:, CHUNK * n : CHUNK * (n + 1)], start=True, stop=True)
+            nc.tensor.matmul(bank[:], ones[:], trust_row[:, CHUNK * n : CHUNK * (n + 1)], start=True, stop=True)
 
         def stir(count):
             for i in range(count):
                 b, bank = claim([P, CHUNK], F32)
                 idle.append(b)
-                nc.tensor.matmul(bank[:], ones[:, :P], ones[:], start=True, stop=True)
+                nc.tensor.matmul(bank[:], ones[:], ones[:].unsqueeze(1).to_broadcast([P, CHUNK // P, P]), start=True, stop=True)
 
         def take_trust(n):
             b, bank = live["trust", n]
@@ -343,8 +343,8 @@ def tile_bank_relation_distill_d6_kernel(
             nc.scalar.copy(out=trust_all[:, CHUNK * n : CHUNK * (n + 1)], in_=bank[:])
 
         with tc.manual_schedule():
-            nc.vector.memset(trust_row[:].bitcast(I32), 0)
             nc.vector.memset(ones[:], 1.0)
+            nc.vector.memset(trust_row[:].bitcast(I32), 0)
             clear_scales(0)
             make_identity(nc, ident[:])
             clear_scales(1)
@@ -356,25 +356,23 @@ def tile_bank_relation_distill_d6_kernel(
             load_words(0, 0, 2)
             load_t(1)
             load_words(0, 2, 4)
-            load_t(2)
             load_scales(1)
             load_words(1, 0, 2)
             load_words(1, 2, 4)
+            load_t(2)
             load_b(0, 4)
             load_s(0)
             load_s(1)
             load_s(2)
             load_b(4, 8)
             load_t(3)
-            load_s(3)
-            load_t(4)
+            load_b(8, 10)
             load_scales(2)
             load_words(2)
-            load_b_quadrants(8)
-            load_b_quadrants(9)
+            load_t(4)
+            load_b(10, 12)
+            load_s_quadrants(3)
             load_t(5)
-            load_b_quadrants(10)
-            load_b_quadrants(11)
             load_s_quadrants(4)
             load_t(6)
             load_s_quadrants(5)
@@ -382,7 +380,7 @@ def tile_bank_relation_distill_d6_kernel(
             load_s_quadrants(6)
             load_s_quadrants(7)
             nc.vector.tensor_scalar(out=neg[:], in0=scale[:], scalar1=-1.0, scalar2=None, op0=MULT)
-            stir(4)
+            stir(5)
             widen(0, 0, 16)
             spread_trust(0)
             take_trust(0)
@@ -402,169 +400,180 @@ def tile_bank_relation_distill_d6_kernel(
             turn_t(1, 0)
             take_t(1, 0)
             turn_t(1, 1)
-            take_t(1, 1)
-            widen(2, 0, 16)
+            take_t(1, 1, False)
             open_group(0, 1)
-            quant_t(1)
+            quant_t(1, 0, 2)
+            quant_t(1, 2, 4)
+            widen(2, 0, 16)
+            open_group(1, 0)
             turn_t(2, 0)
             take_t(2, 0)
             turn_t(2, 1)
             take_t(2, 1)
             for i in range(4):
                 perm_b(i)
-            open_group(1, 0)
+            open_group(1, 1)
             quant_t(2)
+            perm_s(0)
+            perm_s(1)
             for i in range(4):
                 turn_b(i)
-                take_b(i)
-            for m in range(3):
-                perm_s(m)
-            open_group(1, 1)
+                take_b(i, i != 1)
+            perm_s(2)
+            open_group(2, 0)
             quant_b(0, 0, 256)
-            for m in range(3):
-                turn_s(m)
-                take_s(m)
             perm_b(4)
             perm_b(5)
             quant_b(0, 256, 512)
-            open_group(2, 0)
             perm_b(6)
-            quant_s(0)
+            for m in range(3):
+                turn_s(m)
+                take_s(m)
             perm_b(7)
+            open_group(2, 1)
+            quant_s(0)
+            widen(3, 0, 4)
             quant_s(1)
+            widen(3, 4, 8)
             quant_s(2)
             for m in range(3):
                 close_group(m, 0)
                 square(m, 0)
-            for i in range(4, 8):
-                turn_b(i)
-                take_b(i)
-            widen(3, 0, 16)
-            perm_s(3)
-            widen(4, 0, 16)
-            open_group(2, 1)
-            open_group(0, 2)
-            quant_b(1, 0, 256)
-            quant_b(1, 256, 512)
-            turn_t(3, 0)
-            take_t(3, 0)
-            turn_t(3, 1)
-            take_t(3, 1)
-            turn_s(3)
-            take_s(3)
+            widen(3, 8, 16)
             perm_b(8)
             perm_b(9)
-            flip_b(8)
+            for i in range(4, 8):
+                turn_b(i)
+                take_b(i, i != 5)
+            open_group(0, 2)
+            quant_b(1, 0, 256)
+            widen(4, 0, 8)
+            quant_b(1, 256, 512)
+            widen(4, 8, 16)
+            turn_t(3, 0)
+            turn_t(3, 1)
+            turn_b(8)
+            turn_b(9)
+            take_t(3, 0)
+            take_t(3, 1)
+            perm_b(10)
+            perm_b(11)
+            take_b(8)
+            take_b(9)
+            perm_s(3)
             for m in range(3):
                 close_group(m, 1)
             quant_t(3)
-            quant_s(3)
+            flip_s(3)
             square(0, 1)
-            weave_b(8)
-            open_group(1, 2)
-            flip_b(9)
-            widen(5, 0, 16)
             square(1, 1)
-            perm_b(10, True)
-            square(2, 1)
-            weave_b(9)
-            multiply(3, 0)
-            perm_b(11, True)
-            flip_b(10)
-            square(3, 0)
-            multiply(3, 1)
+            turn_b(10)
+            turn_b(11)
+            turn_t(4, 0)
+            turn_t(4, 1)
+            weave_s(3)
             quant_b(2, 0, 256)
-            flip_b(11)
-            weave_b(10)
-            weave_b(11)
-            square(3, 1)
-            open_group(2, 2)
-            for m in (4, 5):
-                for h in range(2):
-                    turn_t(m, h)
+            open_group(1, 2)
+            widen(5, 0, 8)
+            quant_s(3)
+            take_b(10)
+            take_b(11)
+            square(2, 1)
+            multiply(3, 0)
+            widen(5, 8, 16)
             perm_s(4)
             quant_b(2, 256, 512)
-            flip_s(4)
             take_t(4, 0)
             take_t(4, 1)
-            weave_s(4)
-            take_t(5, 0)
-            take_t(5, 1)
-            perm_s(5)
-            for m in range(3):
-                close_group(m, 2)
-                square(m, 2)
+            square(3, 0)
+            multiply(3, 1)
+            flip_s(4)
+            weigh(0, 0, 1024, part=early[:, 0:1])
             quant_t(4)
-            flip_s(5)
-            quant_s(4)
-            quant_t(5)
-            multiply(3, 2)
-            weave_s(5)
-            weigh(0)
-            square(3, 2)
-            multiply(4, 0)
-            quant_s(5)
+            weave_s(4)
+            square(3, 1)
+            perm_s(5, True)
+            close_group(0, 2)
+            close_group(1, 2)
             widen(6, 0, 16)
-            widen_flat(7, 0, 8)
-            square(4, 0)
-            perm_s(6, True)
-            multiply(4, 1)
+            quant_s(4)
+            square(0, 2)
+            square(1, 2)
+            multiply(2, 2)
+            flip_s(5)
+            weigh(0, 1024, 1536)
+            weave_s(5)
+            square(2, 2)
+            multiply(3, 2)
             weigh(1)
-            widen_flat(7, 8, 16)
+            quant_s(5)
+            for m in (5, 6):
+                for h in range(2):
+                    turn_t(m, h)
+            square(3, 2)
+            for m in (5, 6):
+                for h in range(2):
+                    take_t(m, h)
+            multiply(4, 0)
+            weigh(2)
+            perm_s(6, True)
+            square(4, 0)
+            multiply(4, 1)
+            quant_t(5)
+            widen(7, 0, 16)
+            quant_t(6)
             square(4, 1)
             multiply(4, 2)
             flip_s(6)
-            part_t(7)
-            square(4, 2)
+            weigh(3)
             weave_s(6)
+            square(4, 2)
             perm_s(7, True)
             multiply(5, 0)
-            weigh(2)
-            for m in (6, 7):
-                for h in range(2):
-                    turn_t(m, h)
-            square(5, 0)
-            for m in (6, 7):
-                for h in range(2):
-                    take_t(m, h)
-            multiply(5, 1)
             quant_s(6)
+            turn_t(7, 0)
+            turn_t(7, 1)
+            square(5, 0)
+            take_t(7, 0)
+            take_t(7, 1)
+            multiply(5, 1)
             flip_s(7)
-            quant_t(6)
+            weigh(4)
             weave_s(7)
             square(5, 1)
             multiply(5, 2)
             quant_t(7)
-            weigh(3)
             quant_s(7)
-            weigh(4)
             square(5, 2)
             multiply(6, 0)
             weigh(5)
             square(6, 0)
             multiply(6, 1)
             square(6, 1)
-            weigh(6, 0, 1024, part=sixth[:, 0:1])
+            weigh(6, 0, 1024, part=early[:, 1:2])
             multiply(6, 2)
             last = TILES - 1
             multiply(last, 0)
             square(last - 1, 2)
-            weigh(last - 1, 1024, 1536, part=sixth[:, 1:2])
-            multiply(last, 1)
+            weigh(last - 1, 1024, 1536)
+            multiply(last, 1, 0, 256)
             square(last, 0)
-            nc.vector.tensor_tensor(out=total[:, last - 1 :], in0=sixth[:, 0:1], in1=sixth[:, 1:2], op=mybir.AluOpType.add)
+            nc.vector.tensor_tensor(out=total[:, :: last - 1], in0=total[:, :: last - 1], in1=early[:], op=mybir.AluOpType.add)
             weigh(last, 0, 512, part=ends[:, 0:1])
             nc.vector.tensor_scalar(out=means[:, :last], in0=total[:], scalar1=1.0 / N, scalar2=None, op0=MULT)
+            multiply(last, 1, 256, 512)
+            square(last, 1, 0, 256)
+            weigh(last, 512, 768, part=ends[:, 1:2])
             multiply(last, 2, 0, 256)
-            square(last, 1)
-            weigh(last, 512, 1024, part=ends[:, 1:2])
+            square(last, 1, 256, 512)
+            weigh(last, 768, 1024, part=ends[:, 2:3])
             multiply(last, 2, 256, 384)
             square(last, 2, 0, 256)
-            weigh(last, 1024, 1280, part=ends[:, 2:3])
+            weigh(last, 1024, 1280, part=ends[:, 3:4])
             multiply(last, 2, 384, 512)
             square(last, 2, 256, 384)
-            weigh(last, 1280, 1408, part=ends[:, 3:4])
+            weigh(last, 1280, 1408, part=ends[:, 4:5])
             square(last, 2, 384, 512)
-            weigh(last, 1408, 1536, part=ends[:, 4:5])
-            nc.vector.tensor_scalar(out=shares[:], in0=ends[:], scalar1=1.0 / N, scalar2=None, op0=MULT, op1=mybir.AluOpType.add, accum_out=means[:, last:])
+            weigh(last, 1408, 1536, part=ends[:, 5:6])
+            nc.scalar.activation(out=shares[:], in_=ends[:], func=mybir.ActivationFunctionType.Copy, scale=1.0 / N, accum_out=means[:, last:])
             nc.scalar.dma_start(out=out_1.rearrange("(p m) -> p m", m=TILES), in_=means[:])

@@ -233,6 +233,19 @@ def tile_bank_relation_distill_d6_kernel(
                     at = P * (2 * (2 * h + g) + u)
                     nc.tensor.transpose(bank[:, g, u, :], words[:, at : at + P], ident[:])
 
+        def turn_pass(m, g):
+            words = live["xt", m][:].rearrange("p g u w e -> p (g u w e)").bitcast(F32)
+            b, bank = claim([P, 1, 2, P], F32)
+            live["bt", m, g] = (b, bank)
+            for u in range(2):
+                at = P * (2 * g + u)
+                nc.tensor.transpose(bank[:, 0, u, :], words[:, at : at + P], ident[:])
+
+        def take_pass(m, g):
+            if g == 0:
+                live["gt", m] = work.tile([P, GT, P, 2], F32, name="t_grouped", align_bytes=64)
+            take(live["gt", m][:, g : g + 1], live["bt", m, g], True)
+
         def take_t(m, h, on_scalar=True):
             if h == 0:
                 live["gt", m] = work.tile([P, GT, P, 2], F32, name="t_grouped", align_bytes=64)
@@ -359,19 +372,21 @@ def tile_bank_relation_distill_d6_kernel(
             load_scales(1)
             load_words(1, 0, 2)
             load_words(1, 2, 4)
+            load_b(0, 2)
             load_t(2)
-            load_b(0, 4)
+            load_b(2, 4)
             load_s(0)
             load_s(1)
             load_s(2)
             load_b(4, 8)
             load_t(3)
-            load_b(8, 10)
             load_scales(2)
             load_words(2)
+            load_b(8, 10)
             load_t(4)
-            load_b(10, 12)
             load_s_quadrants(3)
+            load_b_quadrants(10)
+            load_b_quadrants(11)
             load_t(5)
             load_s_quadrants(4)
             load_t(6)
@@ -381,171 +396,190 @@ def tile_bank_relation_distill_d6_kernel(
             load_s_quadrants(7)
             nc.vector.tensor_scalar(out=neg[:], in0=scale[:], scalar1=-1.0, scalar2=None, op0=MULT)
             stir(5)
-            widen(0, 0, 16)
             spread_trust(0)
-            take_trust(0)
-            turn_t(0, 0)
-            take_t(0, 0)
-            turn_t(0, 1)
-            take_t(0, 1)
-            spread_trust(1)
-            take_trust(1)
-            spread_trust(2)
-            take_trust(2)
-            quant_t(0, 0, 2)
-            widen(1, 0, 4)
-            quant_t(0, 2, 4)
+            widen(0, 0, 16)
+            for g in range(GT):
+                turn_pass(0, g)
+                take_pass(0, g)
+                if g % 2:
+                    spread_trust((g + 1) // 2)
+            quant_t(0, 0, 1)
+            widen(1, 0, 2)
+            quant_t(0, 1, 2)
+            widen(1, 2, 6)
+            quant_t(0, 2, 3)
+            widen(1, 6, 8)
+            quant_t(0, 3, 4)
+            widen(1, 8, 16)
+            for n in range(CHUNKS):
+                take_trust(n)
             open_group(0, 0)
-            widen(1, 4, 16)
             turn_t(1, 0)
             take_t(1, 0)
-            turn_t(1, 1)
-            take_t(1, 1, False)
             open_group(0, 1)
+            perm_b(0)
             quant_t(1, 0, 2)
+            perm_b(1)
+            widen(2, 0, 12)
+            turn_t(1, 1)
+            take_t(1, 1)
+            turn_b(0)
+            take_b(0)
+            widen(2, 12, 16)
+            perm_b(2)
             quant_t(1, 2, 4)
-            widen(2, 0, 16)
-            open_group(1, 0)
+            open_group(1, 0, 0, 2)
+            open_group(1, 1, 0, 2)
+            perm_b(3)
             turn_t(2, 0)
             take_t(2, 0)
+            turn_b(1)
             turn_t(2, 1)
             take_t(2, 1)
-            for i in range(4):
-                perm_b(i)
-            open_group(1, 1)
-            quant_t(2)
+            turn_b(2)
+            take_b(2)
             perm_s(0)
             perm_s(1)
-            for i in range(4):
-                turn_b(i)
-                take_b(i, i != 1)
+            take_b(1, False)
+            open_group(1, 0, 2, 4)
+            open_group(1, 1, 2, 4)
             perm_s(2)
-            open_group(2, 0)
+            quant_t(2)
             quant_b(0, 0, 256)
+            turn_b(3)
+            take_b(3)
+            turn_s(0)
+            take_s(0)
+            turn_s(1)
+            take_s(1)
             perm_b(4)
             perm_b(5)
+            open_group(2, 0)
             quant_b(0, 256, 512)
-            perm_b(6)
-            for m in range(3):
-                turn_s(m)
-                take_s(m)
-            perm_b(7)
-            open_group(2, 1)
             quant_s(0)
             widen(3, 0, 4)
             quant_s(1)
-            widen(3, 4, 8)
+            turn_s(2)
+            take_s(2)
+            turn_b(4)
+            take_b(4)
+            turn_b(5)
+            take_b(5)
+            widen(3, 4, 12)
+            close_group(0, 0)
+            close_group(1, 0)
             quant_s(2)
-            for m in range(3):
-                close_group(m, 0)
-                square(m, 0)
-            widen(3, 8, 16)
+            widen(3, 12, 16)
+            perm_b(6)
+            perm_b(7)
+            square(0, 0)
+            square(1, 0)
+            open_group(2, 1, 0, 2)
+            close_group(2, 0)
+            open_group(2, 1, 2, 4)
+            quant_b(1, 0, 256)
             perm_b(8)
             perm_b(9)
-            for i in range(4, 8):
-                turn_b(i)
-                take_b(i, i != 5)
-            open_group(0, 2)
-            quant_b(1, 0, 256)
-            widen(4, 0, 8)
-            quant_b(1, 256, 512)
-            widen(4, 8, 16)
+            widen(4, 0, 16)
+            turn_b(6)
+            turn_b(7)
             turn_t(3, 0)
             turn_t(3, 1)
-            turn_b(8)
-            turn_b(9)
+            square(2, 0)
+            take_b(6)
+            take_b(7)
             take_t(3, 0)
             take_t(3, 1)
+            perm_s(3)
+            quant_b(1, 256, 512)
+            open_group(0, 2)
+            open_group(1, 2)
+            flip_s(3)
+            quant_t(3)
+            weave_s(3)
             perm_b(10)
             perm_b(11)
-            take_b(8)
-            take_b(9)
-            perm_s(3)
+            flip_b(10)
+            quant_s(3)
+            flip_b(11)
             for m in range(3):
                 close_group(m, 1)
-            quant_t(3)
-            flip_s(3)
-            square(0, 1)
-            square(1, 1)
-            turn_b(10)
-            turn_b(11)
+                square(m, 1)
+            turn_b(8)
+            turn_b(9)
             turn_t(4, 0)
             turn_t(4, 1)
-            weave_s(3)
+            take_b(8)
+            take_b(9)
+            weave_b(10)
+            weave_b(11)
+            widen(5, 0, 16)
             quant_b(2, 0, 256)
-            open_group(1, 2)
-            widen(5, 0, 8)
-            quant_s(3)
-            take_b(10)
-            take_b(11)
-            square(2, 1)
-            multiply(3, 0)
-            widen(5, 8, 16)
             perm_s(4)
             quant_b(2, 256, 512)
+            multiply(3, 0)
+            multiply(3, 1)
+            open_group(2, 2)
             take_t(4, 0)
             take_t(4, 1)
-            square(3, 0)
-            multiply(3, 1)
             flip_s(4)
             weigh(0, 0, 1024, part=early[:, 0:1])
-            quant_t(4)
+            square(3, 0)
             weave_s(4)
             square(3, 1)
-            perm_s(5, True)
-            close_group(0, 2)
-            close_group(1, 2)
+            quant_t(4)
             widen(6, 0, 16)
             quant_s(4)
-            square(0, 2)
-            square(1, 2)
-            multiply(2, 2)
+            perm_s(5, True)
+            for m in range(3):
+                close_group(m, 2)
+                square(m, 2)
+            multiply(3, 2)
             flip_s(5)
             weigh(0, 1024, 1536)
-            weave_s(5)
-            square(2, 2)
-            multiply(3, 2)
             weigh(1)
-            quant_s(5)
+            weave_s(5)
+            square(3, 2)
+            multiply(4, 0)
             for m in (5, 6):
                 for h in range(2):
                     turn_t(m, h)
-            square(3, 2)
-            for m in (5, 6):
-                for h in range(2):
-                    take_t(m, h)
-            multiply(4, 0)
-            weigh(2)
-            perm_s(6, True)
             square(4, 0)
+            take_t(5, 0)
+            take_t(5, 1)
+            quant_s(5)
+            weigh(2)
             multiply(4, 1)
+            perm_s(6, True)
+            take_t(6, 0)
+            take_t(6, 1)
             quant_t(5)
-            widen(7, 0, 16)
-            quant_t(6)
             square(4, 1)
             multiply(4, 2)
             flip_s(6)
+            widen(7, 0, 16)
+            quant_t(6)
             weigh(3)
-            weave_s(6)
             square(4, 2)
-            perm_s(7, True)
+            weave_s(6)
             multiply(5, 0)
             quant_s(6)
-            turn_t(7, 0)
-            turn_t(7, 1)
+            perm_s(7, True)
             square(5, 0)
-            take_t(7, 0)
-            take_t(7, 1)
             multiply(5, 1)
             flip_s(7)
             weigh(4)
-            weave_s(7)
+            turn_t(7, 0)
+            turn_t(7, 1)
             square(5, 1)
+            weave_s(7)
+            take_t(7, 0)
+            take_t(7, 1)
             multiply(5, 2)
-            quant_t(7)
             quant_s(7)
             square(5, 2)
             multiply(6, 0)
+            quant_t(7)
             weigh(5)
             square(6, 0)
             multiply(6, 1)
@@ -575,5 +609,5 @@ def tile_bank_relation_distill_d6_kernel(
             weigh(last, 1280, 1408, part=ends[:, 4:5])
             square(last, 2, 384, 512)
             weigh(last, 1408, 1536, part=ends[:, 5:6])
-            nc.scalar.activation(out=shares[:], in_=ends[:], func=mybir.ActivationFunctionType.Copy, scale=1.0 / N, accum_out=means[:, last:])
+            nc.vector.tensor_scalar(out=shares[:], in0=ends[:], scalar1=1.0 / N, scalar2=None, op0=MULT, op1=mybir.AluOpType.add, accum_out=means[:, last:])
             nc.scalar.dma_start(out=out_1.rearrange("(p m) -> p m", m=TILES), in_=means[:])

@@ -382,11 +382,9 @@ def tile_bank_relation_distill_d6_kernel(
             load_t(3)
             load_scales(2)
             load_words(2)
-            load_b(8, 10)
+            load_b(8, 12)
             load_t(4)
             load_s_quadrants(3)
-            load_b_quadrants(10)
-            load_b_quadrants(11)
             load_t(5)
             load_s_quadrants(4)
             load_t(6)
@@ -419,7 +417,7 @@ def tile_bank_relation_distill_d6_kernel(
             open_group(0, 1)
             perm_b(0)
             quant_t(1, 0, 2)
-            perm_b(1)
+            perm_b(1, True)
             widen(2, 0, 12)
             turn_t(1, 1)
             take_t(1, 1)
@@ -430,7 +428,7 @@ def tile_bank_relation_distill_d6_kernel(
             quant_t(1, 2, 4)
             open_group(1, 0, 0, 2)
             open_group(1, 1, 0, 2)
-            perm_b(3)
+            perm_b(3, True)
             turn_t(2, 0)
             take_t(2, 0)
             turn_b(1)
@@ -480,7 +478,9 @@ def tile_bank_relation_distill_d6_kernel(
             quant_b(1, 0, 256)
             perm_b(8)
             perm_b(9)
-            widen(4, 0, 16)
+            perm_b(10)
+            perm_b(11)
+            widen(4, 0, 12)
             turn_b(6)
             turn_b(7)
             turn_t(3, 0)
@@ -490,96 +490,89 @@ def tile_bank_relation_distill_d6_kernel(
             take_b(7)
             take_t(3, 0)
             take_t(3, 1)
-            perm_s(3)
             quant_b(1, 256, 512)
+            perm_s(3)
             open_group(0, 2)
             open_group(1, 2)
+            widen(4, 12, 16)
             flip_s(3)
             quant_t(3)
-            weave_s(3)
-            perm_b(10)
-            perm_b(11)
-            flip_b(10)
-            quant_s(3)
-            flip_b(11)
+            widen(5, 0, 16)
             for m in range(3):
                 close_group(m, 1)
-                square(m, 1)
-            turn_b(8)
-            turn_b(9)
-            turn_t(4, 0)
-            turn_t(4, 1)
-            take_b(8)
-            take_b(9)
-            weave_b(10)
-            weave_b(11)
-            widen(5, 0, 16)
+            square(0, 1)
+            square(1, 1)
+            weave_s(3)
+            square(2, 1)
+            for i in range(8, 12):
+                turn_b(i)
+                take_b(i)
+            quant_s(3)
+            weigh(0, 0, 1024, part=early[:, 0:1])
             quant_b(2, 0, 256)
             perm_s(4)
-            quant_b(2, 256, 512)
             multiply(3, 0)
             multiply(3, 1)
-            open_group(2, 2)
-            take_t(4, 0)
-            take_t(4, 1)
+            quant_b(2, 256, 512)
             flip_s(4)
-            weigh(0, 0, 1024, part=early[:, 0:1])
+            widen(6, 0, 16)
             square(3, 0)
+            perm_s(5, True)
             weave_s(4)
             square(3, 1)
-            quant_t(4)
-            widen(6, 0, 16)
-            quant_s(4)
-            perm_s(5, True)
-            for m in range(3):
-                close_group(m, 2)
-                square(m, 2)
-            multiply(3, 2)
-            flip_s(5)
-            weigh(0, 1024, 1536)
-            weigh(1)
-            weave_s(5)
-            square(3, 2)
-            multiply(4, 0)
-            for m in (5, 6):
+            for m in (4, 5):
                 for h in range(2):
                     turn_t(m, h)
-            square(4, 0)
-            take_t(5, 0)
-            take_t(5, 1)
-            quant_s(5)
-            weigh(2)
-            multiply(4, 1)
-            perm_s(6, True)
-            take_t(6, 0)
-            take_t(6, 1)
+                    take_t(m, h)
+            flip_s(5)
+            quant_s(4)
+            widen(7, 0, 8)
+            close_group(0, 2)
+            close_group(1, 2)
+            quant_t(4)
+            square(0, 2)
+            weave_s(5)
+            square(1, 2)
+            multiply(2, 2)
+            widen(7, 8, 16)
             quant_t(5)
-            square(4, 1)
-            multiply(4, 2)
+            weigh(0, 1024, 1536)
+            quant_s(5)
+            perm_s(6, True)
+            square(2, 2)
+            multiply(3, 2)
+            weigh(1)
             flip_s(6)
-            widen(7, 0, 16)
-            quant_t(6)
-            weigh(3)
-            square(4, 2)
-            weave_s(6)
-            multiply(5, 0)
-            quant_s(6)
             perm_s(7, True)
-            square(5, 0)
-            multiply(5, 1)
+            square(3, 2)
+            multiply(4, 0)
+            weigh(2)
+            weave_s(6)
+            square(4, 0)
+            multiply(4, 1)
             flip_s(7)
-            weigh(4)
-            turn_t(7, 0)
-            turn_t(7, 1)
-            square(5, 1)
+            quant_s(6)
+            weigh(3)
+            for m in (6, 7):
+                for h in range(2):
+                    turn_t(m, h)
+            square(4, 1)
             weave_s(7)
-            take_t(7, 0)
-            take_t(7, 1)
-            multiply(5, 2)
+            for m in (6, 7):
+                for h in range(2):
+                    take_t(m, h)
+            multiply(4, 2)
             quant_s(7)
+            square(4, 2)
+            multiply(5, 0)
+            quant_t(6)
+            quant_t(7)
+            weigh(4)
+            for n in range(1, CHUNKS):
+                square(5, n - 1)
+                multiply(5, n)
             square(5, 2)
             multiply(6, 0)
-            quant_t(7)
             weigh(5)
             square(6, 0)
             multiply(6, 1)

@@ -46,7 +46,7 @@ def tile_bank_relation_distill_d6_kernel(
         scale = const.tile([P, TILES, K // P], F32, name="scale")
         neg = const.tile([P, TILES, K // P], F32, name="neg")
         total = const.tile([P, TILES - 1], F32, name="total")
-        early = const.tile([P, 2], F32, name="early")
+        early = const.tile([P, 1], F32, name="early")
         ends = const.tile([P, 6], F32, name="ends")
         shares = const.tile([P, 6], F32, name="shares")
         means = const.tile([P, TILES], F32, name="means")
@@ -382,10 +382,13 @@ def tile_bank_relation_distill_d6_kernel(
             load_t(3)
             load_scales(2)
             load_words(2)
-            load_b(8, 12)
-            load_t(4)
             load_s_quadrants(3)
+            load_b_quadrants(8)
+            load_t(4)
+            load_b_quadrants(9)
+            load_b_quadrants(10)
             load_t(5)
+            load_b_quadrants(11)
             load_s_quadrants(4)
             load_t(6)
             load_s_quadrants(5)
@@ -476,11 +479,7 @@ def tile_bank_relation_distill_d6_kernel(
             close_group(2, 0)
             open_group(2, 1, 2, 4)
             quant_b(1, 0, 256)
-            perm_b(8)
-            perm_b(9)
-            perm_b(10)
-            perm_b(11)
-            widen(4, 0, 12)
+            perm_s(3)
             turn_b(6)
             turn_b(7)
             turn_t(3, 0)
@@ -490,94 +489,104 @@ def tile_bank_relation_distill_d6_kernel(
             take_b(7)
             take_t(3, 0)
             take_t(3, 1)
+            flip_s(3)
+            perm_b(8)
+            widen(4, 0, 8)
             quant_b(1, 256, 512)
-            perm_s(3)
+            flip_b(8)
             open_group(0, 2)
             open_group(1, 2)
-            widen(4, 12, 16)
-            flip_s(3)
+            weave_s(3)
+            weave_b(8)
+            perm_b(9)
             quant_t(3)
-            widen(5, 0, 16)
+            flip_b(9)
+            quant_s(3)
+            widen(4, 8, 16)
             for m in range(3):
                 close_group(m, 1)
             square(0, 1)
+            perm_b(10, True)
             square(1, 1)
-            weave_s(3)
+            weave_b(9)
+            flip_b(10)
+            widen(5, 0, 8)
+            perm_b(11, True)
             square(2, 1)
-            for i in range(8, 12):
-                turn_b(i)
-                take_b(i)
-            quant_s(3)
-            weigh(0, 0, 1024, part=early[:, 0:1])
-            quant_b(2, 0, 256)
-            perm_s(4)
+            weave_b(10)
             multiply(3, 0)
-            multiply(3, 1)
-            quant_b(2, 256, 512)
-            flip_s(4)
-            widen(6, 0, 16)
+            quant_b(2, 0, 256)
+            flip_b(11)
+            widen(5, 8, 16)
             square(3, 0)
-            perm_s(5, True)
-            weave_s(4)
+            multiply(3, 1)
+            open_group(2, 2)
+            perm_s(4)
             square(3, 1)
+            weave_b(11)
+            flip_s(4)
+            quant_b(2, 256, 512)
             for m in (4, 5):
                 for h in range(2):
                     turn_t(m, h)
-                    take_t(m, h)
+            perm_s(5, True)
+            take_t(4, 0)
+            take_t(4, 1)
+            weave_s(4)
+            take_t(5, 0)
+            take_t(5, 1)
+            open_group(3, 2)
             flip_s(5)
-            quant_s(4)
-            widen(7, 0, 8)
-            close_group(0, 2)
-            close_group(1, 2)
             quant_t(4)
-            square(0, 2)
+            widen(6, 0, 4)
+            quant_s(4)
+            widen(6, 4, 16)
             weave_s(5)
-            square(1, 2)
-            multiply(2, 2)
-            widen(7, 8, 16)
+            for m in range(4):
+                close_group(m, 2)
+                square(m, 2)
             quant_t(5)
-            weigh(0, 1024, 1536)
             quant_s(5)
-            perm_s(6, True)
-            square(2, 2)
-            multiply(3, 2)
-            weigh(1)
-            flip_s(6)
-            perm_s(7, True)
-            square(3, 2)
+            weigh(0)
             multiply(4, 0)
-            weigh(2)
-            weave_s(6)
+            widen(7, 0, 16)
+            perm_s(6, True)
+            perm_s(7, True)
             square(4, 0)
             multiply(4, 1)
+            flip_s(6)
             flip_s(7)
+            weigh(1)
+            square(4, 1)
+            multiply(4, 2)
+            weave_s(6)
+            weave_s(7)
+            square(4, 2)
+            multiply(5, 0)
             quant_s(6)
-            weigh(3)
+            quant_s(7)
+            weigh(2)
             for m in (6, 7):
                 for h in range(2):
                     turn_t(m, h)
-            square(4, 1)
-            weave_s(7)
+            square(5, 0)
             for m in (6, 7):
                 for h in range(2):
                     take_t(m, h)
-            multiply(4, 2)
-            quant_s(7)
-            square(4, 2)
-            multiply(5, 0)
+            multiply(5, 1)
             quant_t(6)
+            weigh(3)
             quant_t(7)
+            square(5, 1)
+            multiply(5, 2)
             weigh(4)
-            for n in range(1, CHUNKS):
-                square(5, n - 1)
-                multiply(5, n)
             square(5, 2)
             multiply(6, 0)
             weigh(5)
             square(6, 0)
             multiply(6, 1)
             square(6, 1)
-            weigh(6, 0, 1024, part=early[:, 1:2])
+            weigh(6, 0, 1024, part=early[:, 0:1])
             multiply(6, 2)
             last = TILES - 1
             multiply(last, 0)
@@ -585,7 +594,7 @@ def tile_bank_relation_distill_d6_kernel(
             weigh(last - 1, 1024, 1536)
             multiply(last, 1, 0, 256)
             square(last, 0)
-            nc.vector.tensor_tensor(out=total[:, :: last - 1], in0=total[:, :: last - 1], in1=early[:], op=mybir.AluOpType.add)
+            nc.vector.tensor_tensor(out=total[:, last - 1 :], in0=total[:, last - 1 :], in1=early[:], op=mybir.AluOpType.add)
             weigh(last, 0, 512, part=ends[:, 0:1])
             nc.vector.tensor_scalar(out=means[:, :last], in0=total[:], scalar1=1.0 / N, scalar2=None, op0=MULT)
             multiply(last, 1, 256, 512)

@@ -41,8 +41,10 @@ def tile_bank_relation_distill_d6_kernel(
         ones = const.tile([P, P], BF16, name="ones")
         trust_row = const.tile([P, N], BF16, name="trust_row")
         trust_all = const.tile([P, N], BF16, name="trust_all")
-        tb_words = [const.tile([P, GT, 2 * CHUNK], U8, name="tb_words%d" % n, align_bytes=64) for n in range(CHUNKS)]
-        tb_scales = [const.tile([P, GT, CHUNK], U8, name="tb_scales%d" % n, align_bytes=64) for n in range(CHUNKS)]
+        first_words = [const.tile([P, 4 * CHUNK], U8, name="first_words%d" % g, align_bytes=64) for g in range(GT)]
+        last_words = const.tile([P, GT, 2 * CHUNK], U8, name="last_words", align_bytes=64)
+        first_scales = const.tile([P, GT, 2 * CHUNK], U8, name="first_scales", align_bytes=64)
+        last_scales = const.tile([P, GT, CHUNK], U8, name="last_scales", align_bytes=64)
         scale = const.tile([P, TILES, K // P], F32, name="scale")
         neg = const.tile([P, TILES, K // P], F32, name="neg")
         total = const.tile([P, TILES - 1], F32, name="total")
@@ -56,8 +58,12 @@ def tile_bank_relation_distill_d6_kernel(
         o_view = out_0.rearrange("(p m) n -> p m n", m=TILES)
 
         t_raw = [const.tile([P, K], U8, name="t_raw%d" % m, align_bytes=64) for m in range(TILES)]
-        s_raw = [const.tile([P, J], BF16, name="s_raw%d" % m, align_bytes=64) for m in range(TILES)]
-        b_raw = [const.tile([P, J], BF16, name="b_raw%d" % i, align_bytes=64) for i in range(N // P)]
+        s_pair = const.tile([P, 2, J], BF16, name="s_pair", align_bytes=64)
+        s_raw = [s_pair[:, 0], s_pair[:, 1]]
+        s_raw.extend(const.tile([P, J], BF16, name="s_raw%d" % m, align_bytes=64)[:] for m in range(2, TILES))
+        b_pair = [const.tile([P, 2, J], BF16, name="b_pair%d" % j, align_bytes=64) for j in range(4)]
+        b_raw = [b_pair[i // 2][:, i % 2] for i in range(8)]
+        b_raw.extend(const.tile([P, J], BF16, name="b_raw%d" % i, align_bytes=64)[:] for i in range(8, N // P))
         b_codes = [const.tile([P, GS, CHUNK], U32, name="b_codes%d" % n, align_bytes=64) for n in range(CHUNKS)]
         b_scales = [const.tile([P, GS, CHUNK], U8, name="b_scales%d" % n, align_bytes=64) for n in range(CHUNKS)]
 
@@ -83,23 +89,37 @@ def tile_bank_relation_distill_d6_kernel(
             for i in range(lo, hi):
                 nc.sync.dma_start(out=b_raw[i][:], in_=sbank[P * i : P * (i + 1), :])
 
-        def load_words(c, g0=0, g1=GT):
-            cols = slice(2 * CHUNK * c, 2 * CHUNK * (c + 1))
+        def load_b_pair(j):
+            rows = sbank[2 * P * j : 2 * P * (j + 1), :].rearrange("(e p) k -> p e k", e=2)
+            nc.sync.dma_start(out=b_pair[j][:], in_=rows)
+
+        def load_first_words(g):
+            nc.sync.dma_start(out=first_words[g][:].bitcast(I32), in_=tbank_words[g, :, : 4 * CHUNK].bitcast(I32))
+
+        def load_last_words():
             nc.sync.dma_start(
-                out=tb_words[c][:, g0:g1].bitcast(I32),
-                in_=tbank_words[g0:g1, :, cols].rearrange("g p w -> p g w").bitcast(I32),
+                out=last_words[:].bitcast(I32),
+                in_=tbank_words[:, :, 4 * CHUNK :].rearrange("g p w -> p g w").bitcast(I32),
             )
 
-        def clear_scales(c):
-            nc.vector.memset(tb_scales[c][:].rearrange("p g n -> p (g n)").bitcast(I32), 0)
+        def clear_scales(tile):
+            nc.vector.memset(tile[:].rearrange("p g n -> p (g n)").bitcast(I32), 0)
 
-        def load_scales(c):
-            cols = slice(CHUNK * c, CHUNK * (c + 1))
+        def load_scales(tile, lo, hi):
             for r in range(4):
                 nc.sync.dma_start(
-                    out=tb_scales[c][r:P:32, :, :].bitcast(I32),
-                    in_=tbank_scales[:, r:16:4, cols].rearrange("g q n -> q g n").bitcast(I32),
+                    out=tile[r:P:32, :, :].bitcast(I32),
+                    in_=tbank_scales[:, r:16:4, lo:hi].rearrange("g q n -> q g n").bitcast(I32),
                 )
+
+        def tb_operand(n, g, lo, hi):
+            if n < CHUNKS - 1:
+                lo, hi = CHUNK * n + lo, CHUNK * n + hi
+                return first_words[g][:, 2 * lo : 2 * hi], first_scales[:, g, lo:hi]
+            return last_words[:, g, 2 * lo : 2 * hi], last_scales[:, g, lo:hi]
+
+        def load_s_pair(m):
+            nc.sync.dma_start(out=s_pair[:], in_=s_view[:, m : m + 2, :])
 
         live = {}
         idle = list(range(BANKS))
@@ -293,12 +313,13 @@ def tile_bank_relation_distill_d6_kernel(
         def passes_t(m, n, acc, lo, hi, first, last, g0=0, g1=GT):
             codes, scales = live["ct", m]
             for g in range(g0, g1):
+                words, word_scales = tb_operand(n, g, lo, hi)
                 nc.tensor.matmul_mx(
                     out=acc,
                     lhsT=codes[:, g, :].bitcast(FP8X4),
                     lhsT_scale=scales[:, g, :],
-                    rhs=tb_words[n][:, g, 2 * lo : 2 * hi].bitcast(FP4X4),
-                    rhs_scale=tb_scales[n][:, g, lo:hi],
+                    rhs=words.bitcast(FP4X4),
+                    rhs_scale=word_scales,
                     start=first and g == 0,
                     stop=last and g == GT - 1,
                 )
@@ -358,33 +379,29 @@ def tile_bank_relation_distill_d6_kernel(
         with tc.manual_schedule():
             nc.vector.memset(ones[:], 1.0)
             nc.vector.memset(trust_row[:].bitcast(I32), 0)
-            clear_scales(0)
+            clear_scales(first_scales)
             make_identity(nc, ident[:])
-            clear_scales(1)
-            clear_scales(2)
+            clear_scales(last_scales)
             nc.sync.dma_start(out=scale[:], in_=teacher_scale.rearrange("(p m) c -> p m c", m=TILES))
             load_t(0)
             nc.sync.dma_start(out=trust_row[0:1, :], in_=trust.rearrange("(o n) -> o n", o=1))
-            load_scales(0)
-            load_words(0, 0, 2)
             load_t(1)
-            load_words(0, 2, 4)
-            load_scales(1)
-            load_words(1, 0, 2)
-            load_words(1, 2, 4)
-            load_b(0, 2)
+            load_scales(first_scales, 0, 2 * CHUNK)
+            for g in range(GT):
+                load_first_words(g)
+            load_b_pair(0)
             load_t(2)
-            load_b(2, 4)
-            load_s(0)
-            load_s(1)
+            load_b_pair(1)
+            load_s_pair(0)
             load_s(2)
-            load_b(4, 8)
+            load_b_pair(2)
+            load_b_pair(3)
             load_t(3)
-            load_scales(2)
-            load_words(2)
-            load_s_quadrants(3)
-            load_b_quadrants(8)
+            load_scales(last_scales, 2 * CHUNK, N)
+            load_last_words()
+            load_b(8, 9)
             load_t(4)
+            load_s_quadrants(3)
             load_b_quadrants(9)
             load_b_quadrants(10)
             load_t(5)
@@ -404,141 +421,129 @@ def tile_bank_relation_distill_d6_kernel(
                 take_pass(0, g)
                 if g % 2:
                     spread_trust((g + 1) // 2)
+            widen(1, 0, 8)
             quant_t(0, 0, 1)
-            widen(1, 0, 2)
             quant_t(0, 1, 2)
-            widen(1, 2, 6)
+            widen(1, 8, 12)
             quant_t(0, 2, 3)
-            widen(1, 6, 8)
+            widen(1, 12, 16)
             quant_t(0, 3, 4)
-            widen(1, 8, 16)
-            for n in range(CHUNKS):
-                take_trust(n)
-            open_group(0, 0)
             turn_t(1, 0)
+            take_trust(0)
             take_t(1, 0)
-            open_group(0, 1)
-            perm_b(0)
-            quant_t(1, 0, 2)
-            perm_b(1, True)
-            widen(2, 0, 12)
+            open_group(0, 0, 0, 1)
+            open_group(0, 1, 0, 1)
             turn_t(1, 1)
+            take_trust(1)
             take_t(1, 1)
-            turn_b(0)
-            take_b(0)
-            widen(2, 12, 16)
-            perm_b(2)
+            take_trust(2)
+            for g in range(1, GT):
+                open_group(0, 0, g, g + 1)
+                open_group(0, 1, g, g + 1)
+            quant_t(1, 0, 2)
             quant_t(1, 2, 4)
+            perm_b(0)
+            perm_b(1)
+            widen(2, 0, 16)
             open_group(1, 0, 0, 2)
             open_group(1, 1, 0, 2)
-            perm_b(3, True)
-            turn_t(2, 0)
-            take_t(2, 0)
+            turn_b(0)
+            take_b(0)
             turn_b(1)
-            turn_t(2, 1)
-            take_t(2, 1)
-            turn_b(2)
-            take_b(2)
+            take_b(1)
+            perm_b(2)
+            perm_b(3)
             perm_s(0)
             perm_s(1)
-            take_b(1, False)
             open_group(1, 0, 2, 4)
-            open_group(1, 1, 2, 4)
+            turn_t(2, 0)
+            turn_t(2, 1)
+            turn_b(2)
+            turn_b(3)
+            take_t(2, 0)
+            take_t(2, 1)
+            take_b(2)
+            take_b(3)
             perm_s(2)
             quant_t(2)
             quant_b(0, 0, 256)
-            turn_b(3)
-            take_b(3)
-            turn_s(0)
-            take_s(0)
-            turn_s(1)
-            take_s(1)
+            open_group(1, 1, 2, 4)
+            for m in range(3):
+                turn_s(m)
+                take_s(m)
             perm_b(4)
-            perm_b(5)
-            open_group(2, 0)
             quant_b(0, 256, 512)
+            open_group(2, 0)
+            open_group(2, 1)
             quant_s(0)
-            widen(3, 0, 4)
+            perm_b(5, True)
+            perm_b(6, True)
+            perm_b(7, True)
             quant_s(1)
-            turn_s(2)
-            take_s(2)
-            turn_b(4)
-            take_b(4)
-            turn_b(5)
-            take_b(5)
-            widen(3, 4, 12)
-            close_group(0, 0)
-            close_group(1, 0)
             quant_s(2)
-            widen(3, 12, 16)
-            perm_b(6)
-            perm_b(7)
-            square(0, 0)
-            square(1, 0)
-            open_group(2, 1, 0, 2)
-            close_group(2, 0)
-            open_group(2, 1, 2, 4)
-            quant_b(1, 0, 256)
-            perm_s(3)
-            turn_b(6)
-            turn_b(7)
-            turn_t(3, 0)
-            turn_t(3, 1)
-            square(2, 0)
-            take_b(6)
-            take_b(7)
-            take_t(3, 0)
-            take_t(3, 1)
-            flip_s(3)
+            widen(3, 0, 16)
+            for m in range(3):
+                close_group(m, 0)
+                square(m, 0)
+            for i in range(4, 8):
+                turn_b(i)
+                take_b(i, i >= 6)
             perm_b(8)
-            widen(4, 0, 8)
+            quant_b(1, 0, 256)
+            widen(4, 0, 4)
             quant_b(1, 256, 512)
-            flip_b(8)
             open_group(0, 2)
+            turn_t(3, 0)
+            take_t(3, 0)
+            turn_t(3, 1)
+            take_t(3, 1)
+            turn_b(8)
+            take_b(8)
+            perm_s(3)
+            widen(4, 4, 8)
+            flip_s(3)
+            widen(4, 8, 12)
             open_group(1, 2)
             weave_s(3)
-            weave_b(8)
-            perm_b(9)
             quant_t(3)
-            flip_b(9)
+            perm_b(9)
+            widen(4, 12, 16)
             quant_s(3)
-            widen(4, 8, 16)
+            flip_b(9)
             for m in range(3):
                 close_group(m, 1)
-            square(0, 1)
-            perm_b(10, True)
-            square(1, 1)
+                square(m, 1)
+            perm_b(10)
             weave_b(9)
-            flip_b(10)
             widen(5, 0, 8)
-            perm_b(11, True)
-            square(2, 1)
-            weave_b(10)
+            flip_b(10)
             multiply(3, 0)
+            widen(5, 8, 16)
+            perm_b(11)
+            square(3, 0)
+            weave_b(10)
             quant_b(2, 0, 256)
             flip_b(11)
-            widen(5, 8, 16)
-            square(3, 0)
             multiply(3, 1)
-            open_group(2, 2)
-            perm_s(4)
             square(3, 1)
             weave_b(11)
+            open_group(2, 2)
+            perm_s(4)
+            widen(6, 0, 4)
             flip_s(4)
             quant_b(2, 256, 512)
             for m in (4, 5):
                 for h in range(2):
                     turn_t(m, h)
-            perm_s(5, True)
             take_t(4, 0)
             take_t(4, 1)
             weave_s(4)
             take_t(5, 0)
             take_t(5, 1)
             open_group(3, 2)
-            flip_s(5)
+            perm_s(5)
             quant_t(4)
-            widen(6, 0, 4)
+            flip_s(5)
             quant_s(4)
             widen(6, 4, 16)
             weave_s(5)

@@ -48,7 +48,7 @@ def tile_bank_relation_distill_d6_kernel(
         scale = const.tile([P, TILES, K // P], F32, name="scale")
         neg = const.tile([P, TILES, K // P], F32, name="neg")
         total = const.tile([P, TILES - 1], F32, name="total")
-        early = const.tile([P, 1], F32, name="early")
+        early = const.tile([P, 7], F32, name="early")
         ends = const.tile([P, 6], F32, name="ends")
         shares = const.tile([P, 6], F32, name="shares")
         means = const.tile([P, TILES], F32, name="means")
@@ -397,10 +397,10 @@ def tile_bank_relation_distill_d6_kernel(
             load_b_pair(2)
             load_b_pair(3)
             load_t(3)
+            load_t(4)
             load_scales(last_scales, 2 * CHUNK, N)
             load_last_words()
             load_b(8, 9)
-            load_t(4)
             load_s_quadrants(3)
             load_b_quadrants(9)
             load_b_quadrants(10)
@@ -482,6 +482,7 @@ def tile_bank_relation_distill_d6_kernel(
             quant_s(1)
             quant_s(2)
             widen(3, 0, 16)
+            widen(4, 0, 12)
             for m in range(3):
                 close_group(m, 0)
                 square(m, 0)
@@ -490,7 +491,6 @@ def tile_bank_relation_distill_d6_kernel(
                 take_b(i, i >= 6)
             perm_b(8)
             quant_b(1, 0, 256)
-            widen(4, 0, 4)
             quant_b(1, 256, 512)
             open_group(0, 2)
             turn_t(3, 0)
@@ -500,98 +500,108 @@ def tile_bank_relation_distill_d6_kernel(
             turn_b(8)
             take_b(8)
             perm_s(3)
-            widen(4, 4, 8)
+            widen(4, 12, 16)
             flip_s(3)
-            widen(4, 8, 12)
             open_group(1, 2)
             weave_s(3)
             quant_t(3)
             perm_b(9)
-            widen(4, 12, 16)
             quant_s(3)
             flip_b(9)
+            perm_b(10)
             for m in range(3):
                 close_group(m, 1)
                 square(m, 1)
-            perm_b(10)
             weave_b(9)
-            widen(5, 0, 8)
+            widen(5, 0, 4)
             flip_b(10)
-            multiply(3, 0)
-            widen(5, 8, 16)
+            widen(5, 4, 8)
             perm_b(11)
+            multiply(3, 0)
+            widen(5, 8, 12)
+            flip_b(11)
             square(3, 0)
             weave_b(10)
+            widen(5, 12, 16)
             quant_b(2, 0, 256)
-            flip_b(11)
             multiply(3, 1)
             square(3, 1)
             weave_b(11)
             open_group(2, 2)
             perm_s(4)
             widen(6, 0, 4)
-            flip_s(4)
             quant_b(2, 256, 512)
+            flip_s(4)
             for m in (4, 5):
                 for h in range(2):
                     turn_t(m, h)
             take_t(4, 0)
             take_t(4, 1)
+            perm_s(5, True)
             weave_s(4)
             take_t(5, 0)
             take_t(5, 1)
             open_group(3, 2)
-            perm_s(5)
             quant_t(4)
-            flip_s(5)
+            weigh(0, 0, 1024, part=early[:, 0:1])
             quant_s(4)
+            flip_s(5)
             widen(6, 4, 16)
-            weave_s(5)
             for m in range(4):
                 close_group(m, 2)
-                square(m, 2)
+            square(0, 2)
+            square(1, 2)
+            weave_s(5)
+            square(2, 2)
+            square(3, 2)
             quant_t(5)
+            weigh(1, 0, 1024, part=early[:, 1:2])
             quant_s(5)
-            weigh(0)
             multiply(4, 0)
             widen(7, 0, 16)
             perm_s(6, True)
-            perm_s(7, True)
             square(4, 0)
             multiply(4, 1)
             flip_s(6)
-            flip_s(7)
-            weigh(1)
+            weigh(2, 0, 1024, part=early[:, 2:3])
             square(4, 1)
+            perm_s(7, True)
             multiply(4, 2)
-            weave_s(6)
-            weave_s(7)
+            weigh(0, 1024, 1536)
+            weigh(1, 1024, 1536)
             square(4, 2)
+            weave_s(6)
             multiply(5, 0)
+            weigh(2, 1024, 1536)
             quant_s(6)
-            quant_s(7)
-            weigh(2)
             for m in (6, 7):
                 for h in range(2):
                     turn_t(m, h)
+            take_t(6, 0)
+            take_t(6, 1)
             square(5, 0)
-            for m in (6, 7):
-                for h in range(2):
-                    take_t(m, h)
+            take_t(7, 0)
+            take_t(7, 1)
             multiply(5, 1)
             quant_t(6)
-            weigh(3)
-            quant_t(7)
+            flip_s(7)
+            weigh(3, 0, 1024, part=early[:, 3:4])
+            weigh(3, 1024, 1536)
+            weave_s(7)
             square(5, 1)
             multiply(5, 2)
-            weigh(4)
+            weigh(4, 0, 1024, part=early[:, 4:5])
+            quant_t(7)
+            weigh(4, 1024, 1536)
+            quant_s(7)
             square(5, 2)
             multiply(6, 0)
-            weigh(5)
+            weigh(5, 0, 1024, part=early[:, 5:6])
+            weigh(5, 1024, 1536)
             square(6, 0)
             multiply(6, 1)
             square(6, 1)
-            weigh(6, 0, 1024, part=early[:, 0:1])
+            weigh(6, 0, 1024, part=early[:, 6:7])
             multiply(6, 2)
             last = TILES - 1
             multiply(last, 0)
@@ -599,7 +609,7 @@ def tile_bank_relation_distill_d6_kernel(
             weigh(last - 1, 1024, 1536)
             multiply(last, 1, 0, 256)
             square(last, 0)
-            nc.vector.tensor_tensor(out=total[:, last - 1 :], in0=total[:, last - 1 :], in1=early[:], op=mybir.AluOpType.add)
+            nc.vector.tensor_tensor(out=total[:], in0=total[:], in1=early[:], op=mybir.AluOpType.add)
             weigh(last, 0, 512, part=ends[:, 0:1])
             nc.vector.tensor_scalar(out=means[:, :last], in0=total[:], scalar1=1.0 / N, scalar2=None, op0=MULT)
             multiply(last, 1, 256, 512)

@@ -40,7 +40,7 @@ def tile_bank_relation_distill_d6_kernel(
         ident = const.tile([P, P], F32, name="ident")
         ones = const.tile([P, P], BF16, name="ones")
         trust_row = const.tile([P, N], BF16, name="trust_row")
-        trust_all = const.tile([P, N], BF16, name="trust_all")
+        trust_all = const.tile([P, N + 8], BF16, name="trust_all")
         first_words = [const.tile([P, 4 * CHUNK], U8, name="first_words%d" % g, align_bytes=64) for g in range(GT)]
         last_words = const.tile([P, GT, 2 * CHUNK], U8, name="last_words", align_bytes=64)
         first_scales = const.tile([P, GT, 2 * CHUNK], U8, name="first_scales", align_bytes=64)
@@ -49,8 +49,8 @@ def tile_bank_relation_distill_d6_kernel(
         neg = const.tile([P, TILES, K // P], F32, name="neg")
         total = const.tile([P, TILES - 1], F32, name="total")
         early = const.tile([P, 7], F32, name="early")
-        ends = const.tile([P, 6], F32, name="ends")
-        shares = const.tile([P, 6], F32, name="shares")
+        shares = const.tile([P, P + 5], F32, name="shares")
+        final = const.tile([P, P], F32, name="final")
         means = const.tile([P, TILES], F32, name="means")
 
         t_view = teacher_bytes.rearrange("(p m) k -> p m k", m=TILES)
@@ -227,7 +227,7 @@ def tile_bank_relation_distill_d6_kernel(
                 )
 
         def widen_flat(m, lo, hi):
-            if lo == 0:
+            if ("flat", m) not in live:
                 live["flat", m] = work.tile([P, K], BF16, name="flat", align_bytes=64, bufs=1)
             for c in range(lo, hi):
                 nc.scalar.activation(
@@ -237,12 +237,14 @@ def tile_bank_relation_distill_d6_kernel(
                     scale=neg[:, m, c : c + 1],
                 )
 
-        def part_t(m):
+        def part_t(m, on_scalar=False):
             live["xt", m] = work.tile([P, GT, 2, P, 2], BF16, name="xt", align_bytes=64)
-            nc.vector.tensor_copy(
-                out=live["xt", m][:].rearrange("p g u w e -> p (g u w e)").bitcast(F32).rearrange("p (g u w) -> p g u w", g=GT, u=2),
-                in_=live["flat", m][:].bitcast(F32).rearrange("p (g w u) -> p g u w", g=GT, u=2),
-            )
+            dst = live["xt", m][:].rearrange("p g u w e -> p (g u w e)").bitcast(F32).rearrange("p (g u w) -> p g u w", g=GT, u=2)
+            src = live["flat", m][:].bitcast(F32).rearrange("p (g w u) -> p g u w", g=GT, u=2)
+            if on_scalar:
+                nc.scalar.copy(out=dst, in_=src)
+            else:
+                nc.vector.tensor_copy(out=dst, in_=src)
 
         def turn_t(m, h):
             words = live["xt", m][:].rearrange("p g u w e -> p (g u w e)").bitcast(F32)
@@ -252,6 +254,15 @@ def tile_bank_relation_distill_d6_kernel(
                 for u in range(2):
                     at = P * (2 * (2 * h + g) + u)
                     nc.tensor.transpose(bank[:, g, u, :], words[:, at : at + P], ident[:])
+
+        def turn_flat(m, h):
+            words = live["flat", m][:].bitcast(F32)
+            b, bank = claim([P, 2, 2, P], F32)
+            live["bt", m, h] = (b, bank)
+            for g in range(2):
+                for u in range(2):
+                    at = 2 * P * (2 * h + g)
+                    nc.tensor.transpose(bank[:, g, u, :], words[:, at + u : at + 2 * P : 2], ident[:])
 
         def turn_pass(m, g):
             words = live["xt", m][:].rearrange("p g u w e -> p (g u w e)").bitcast(F32)
@@ -340,7 +351,7 @@ def tile_bank_relation_distill_d6_kernel(
 
         def square(m, n, lo=0, hi=CHUNK):
             if ("sq", m) not in live:
-                live["sq", m] = work.tile([P, N], F32, name="sq", bufs=6)
+                live["sq", m] = work.tile([P, N + 8], F32, name="sq", bufs=6)
             b, acc = live["acc", m, n, lo]
             idle.append(b)
             nc.scalar.activation(
@@ -361,9 +372,16 @@ def tile_bank_relation_distill_d6_kernel(
             queue.dma_start(out=o_view[:, m, lo:hi], in_=res)
 
         def spread_trust(n):
-            b, bank = claim([P, CHUNK], BF16)
-            live["trust", n] = (b, bank)
-            nc.tensor.matmul(bank[:], ones[:], trust_row[:, CHUNK * n : CHUNK * (n + 1)], start=True, stop=True)
+            if n % 2 == 0:
+                live["trust", n // 2] = claim([P, min(2 * CHUNK, N - CHUNK * n)], BF16)
+            bank = live["trust", n // 2][1]
+            nc.tensor.matmul(
+                bank[:, CHUNK * (n % 2) : CHUNK * (n % 2 + 1)],
+                ones[:],
+                trust_row[:, CHUNK * n : CHUNK * (n + 1)],
+                start=True,
+                stop=True,
+            )
 
         def stir(count):
             for i in range(count):
@@ -371,17 +389,19 @@ def tile_bank_relation_distill_d6_kernel(
                 idle.append(b)
                 nc.tensor.matmul(bank[:], ones[:], ones[:].unsqueeze(1).to_broadcast([P, CHUNK // P, P]), start=True, stop=True)
 
-        def take_trust(n):
-            b, bank = live["trust", n]
+        def take_trust(lo, hi):
+            b, bank = live["trust", lo // 2]
             idle.append(b)
-            nc.scalar.copy(out=trust_all[:, CHUNK * n : CHUNK * (n + 1)], in_=bank[:])
+            nc.scalar.copy(out=trust_all[:, CHUNK * lo : CHUNK * hi], in_=bank[:])
 
         with tc.manual_schedule():
             nc.vector.memset(ones[:], 1.0)
+            nc.scalar.activation(out=trust_all[:, N:], in_=ones[:, :8], func=SQUARE)
             nc.vector.memset(trust_row[:].bitcast(I32), 0)
             clear_scales(first_scales)
             make_identity(nc, ident[:])
             clear_scales(last_scales)
+            nc.vector.memset(early[:], 0.0)
             nc.sync.dma_start(out=scale[:], in_=teacher_scale.rearrange("(p m) c -> p m c", m=TILES))
             load_t(0)
             nc.sync.dma_start(out=trust_row[0:1, :], in_=trust.rearrange("(o n) -> o n", o=1))
@@ -400,53 +420,45 @@ def tile_bank_relation_distill_d6_kernel(
             load_t(4)
             load_scales(last_scales, 2 * CHUNK, N)
             load_last_words()
-            load_b(8, 9)
             load_s_quadrants(3)
-            load_b_quadrants(9)
-            load_b_quadrants(10)
-            load_t(5)
-            load_b_quadrants(11)
             load_s_quadrants(4)
+            for i in range(8, 12):
+                load_b_quadrants(i)
+            load_t(5)
             load_t(6)
             load_s_quadrants(5)
             load_t(7)
-            load_s_quadrants(6)
-            load_s_quadrants(7)
             nc.vector.tensor_scalar(out=neg[:], in0=scale[:], scalar1=-1.0, scalar2=None, op0=MULT)
-            stir(5)
+            stir(4)
             spread_trust(0)
-            widen(0, 0, 16)
-            for g in range(GT):
-                turn_pass(0, g)
-                take_pass(0, g)
-                if g % 2:
-                    spread_trust((g + 1) // 2)
-            widen(1, 0, 8)
-            quant_t(0, 0, 1)
-            quant_t(0, 1, 2)
-            widen(1, 8, 12)
-            quant_t(0, 2, 3)
-            widen(1, 12, 16)
-            quant_t(0, 3, 4)
-            turn_t(1, 0)
-            take_trust(0)
-            take_t(1, 0)
-            open_group(0, 0, 0, 1)
-            open_group(0, 1, 0, 1)
-            turn_t(1, 1)
-            take_trust(1)
-            take_t(1, 1)
-            take_trust(2)
-            for g in range(1, GT):
-                open_group(0, 0, g, g + 1)
-                open_group(0, 1, g, g + 1)
+            widen(0, 0, 8)
+            widen_flat(0, 8, 16)
+            turn_t(0, 0)
+            take_t(0, 0)
+            spread_trust(1)
+            widen(1, 0, 16)
+            turn_flat(0, 1)
+            take_t(0, 1)
+            spread_trust(2)
+            quant_t(0, 0, 2)
+            for h in range(2):
+                turn_t(1, h)
+                take_t(1, h)
+            quant_t(0, 2, 4)
             quant_t(1, 0, 2)
             quant_t(1, 2, 4)
+            take_trust(0, 2)
+            take_trust(2, 3)
+            for g in range(3):
+                open_group(0, 0, g, g + 1)
+                open_group(0, 1, g, g + 1)
+            open_group(1, 0, 0, 2)
+            open_group(1, 1, 0, 2)
             perm_b(0)
             perm_b(1)
             widen(2, 0, 16)
-            open_group(1, 0, 0, 2)
-            open_group(1, 1, 0, 2)
+            open_group(0, 0, 3, 4)
+            open_group(0, 1, 3, 4)
             turn_b(0)
             take_b(0)
             turn_b(1)
@@ -482,122 +494,116 @@ def tile_bank_relation_distill_d6_kernel(
             quant_s(1)
             quant_s(2)
             widen(3, 0, 16)
-            widen(4, 0, 12)
+            widen(4, 0, 16)
             for m in range(3):
                 close_group(m, 0)
                 square(m, 0)
             for i in range(4, 8):
                 turn_b(i)
-                take_b(i, i >= 6)
-            perm_b(8)
+                take_b(i, i != 5)
+            open_group(0, 2)
             quant_b(1, 0, 256)
             quant_b(1, 256, 512)
-            open_group(0, 2)
-            turn_t(3, 0)
-            take_t(3, 0)
-            turn_t(3, 1)
-            take_t(3, 1)
-            turn_b(8)
-            take_b(8)
-            perm_s(3)
-            widen(4, 12, 16)
+            perm_s(3, True)
             flip_s(3)
-            open_group(1, 2)
+            for m in (3, 4):
+                for h in range(2):
+                    turn_t(m, h)
+            take_t(3, 0)
+            take_t(3, 1)
             weave_s(3)
+            perm_s(4)
             quant_t(3)
-            perm_b(9)
+            flip_s(4)
             quant_s(3)
-            flip_b(9)
-            perm_b(10)
+            take_t(4, 0)
+            take_t(4, 1)
             for m in range(3):
                 close_group(m, 1)
                 square(m, 1)
-            weave_b(9)
-            widen(5, 0, 4)
-            flip_b(10)
-            widen(5, 4, 8)
-            perm_b(11)
+            open_group(1, 2)
+            perm_b(8)
+            quant_t(4)
+            flip_b(8)
+            weave_s(4)
+            perm_b(9)
+            quant_s(4)
+            flip_b(9)
             multiply(3, 0)
-            widen(5, 8, 12)
-            flip_b(11)
+            weave_b(8)
             square(3, 0)
-            weave_b(10)
-            widen(5, 12, 16)
-            quant_b(2, 0, 256)
+            perm_b(10, True)
+            weigh(0, 0, 1024, part=early[:, 0:1])
+            load_s_quadrants(6)
+            load_s_quadrants(7)
             multiply(3, 1)
+            weave_b(9)
+            flip_b(10)
             square(3, 1)
+            perm_b(11, True)
+            widen(5, 0, 16)
+            multiply(4, 0)
+            weave_b(10)
+            flip_b(11)
+            square(4, 0)
+            quant_b(2, 0, 256)
+            multiply(4, 1)
             weave_b(11)
+            widen(6, 0, 16)
+            square(4, 1)
             open_group(2, 2)
-            perm_s(4)
-            widen(6, 0, 4)
+            open_group(3, 2)
             quant_b(2, 256, 512)
-            flip_s(4)
-            for m in (4, 5):
+            weigh(1, 0, 1024, part=early[:, 1:2])
+            perm_s(5, True)
+            for m in (5, 6):
                 for h in range(2):
                     turn_t(m, h)
-            take_t(4, 0)
-            take_t(4, 1)
-            perm_s(5, True)
-            weave_s(4)
+            flip_s(5)
+            weigh(2, 0, 1024, part=early[:, 2:3])
             take_t(5, 0)
             take_t(5, 1)
-            open_group(3, 2)
-            quant_t(4)
-            weigh(0, 0, 1024, part=early[:, 0:1])
-            quant_s(4)
-            flip_s(5)
-            widen(6, 4, 16)
+            weave_s(5)
             for m in range(4):
                 close_group(m, 2)
+            quant_t(5)
             square(0, 2)
             square(1, 2)
-            weave_s(5)
-            square(2, 2)
-            square(3, 2)
-            quant_t(5)
-            weigh(1, 0, 1024, part=early[:, 1:2])
             quant_s(5)
-            multiply(4, 0)
-            widen(7, 0, 16)
-            perm_s(6, True)
-            square(4, 0)
-            multiply(4, 1)
-            flip_s(6)
-            weigh(2, 0, 1024, part=early[:, 2:3])
-            square(4, 1)
-            perm_s(7, True)
-            multiply(4, 2)
             weigh(0, 1024, 1536)
             weigh(1, 1024, 1536)
-            square(4, 2)
-            weave_s(6)
-            multiply(5, 0)
-            weigh(2, 1024, 1536)
-            quant_s(6)
-            for m in (6, 7):
-                for h in range(2):
-                    turn_t(m, h)
             take_t(6, 0)
             take_t(6, 1)
+            multiply(4, 2)
+            square(2, 2)
+            square(3, 2)
+            widen(7, 0, 16)
+            weigh(2, 1024, 1536)
+            multiply(5, 0)
+            square(4, 2)
+            perm_s(6, True)
+            quant_t(6)
+            flip_s(6)
+            multiply(5, 1)
             square(5, 0)
+            weave_s(6)
+            weigh(3, 0, 1536)
+            for h in range(2):
+                turn_t(7, h)
+            square(5, 1)
+            perm_s(7, True)
+            quant_s(6)
+            weigh(4, 0, 1536)
+            multiply(5, 2)
             take_t(7, 0)
             take_t(7, 1)
-            multiply(5, 1)
-            quant_t(6)
             flip_s(7)
-            weigh(3, 0, 1024, part=early[:, 3:4])
-            weigh(3, 1024, 1536)
-            weave_s(7)
-            square(5, 1)
-            multiply(5, 2)
-            weigh(4, 0, 1024, part=early[:, 4:5])
-            quant_t(7)
-            weigh(4, 1024, 1536)
-            quant_s(7)
             square(5, 2)
             multiply(6, 0)
-            weigh(5, 0, 1024, part=early[:, 5:6])
-            weigh(5, 1024, 1536)
+            weave_s(7)
+            quant_t(7)
+            weigh(5, 0, 1536)
+            quant_s(7)
             square(6, 0)
             multiply(6, 1)
             square(6, 1)
@@ -610,21 +616,30 @@ def tile_bank_relation_distill_d6_kernel(
             multiply(last, 1, 0, 256)
             square(last, 0)
             nc.vector.tensor_tensor(out=total[:], in0=total[:], in1=early[:], op=mybir.AluOpType.add)
-            weigh(last, 0, 512, part=ends[:, 0:1])
+            weigh(last, 0, 512, part=live["sq", last][:, N + 0 : N + 1])
             nc.vector.tensor_scalar(out=means[:, :last], in0=total[:], scalar1=1.0 / N, scalar2=None, op0=MULT)
             multiply(last, 1, 256, 512)
             square(last, 1, 0, 256)
-            weigh(last, 512, 768, part=ends[:, 1:2])
+            weigh(last, 512, 768, part=live["sq", last][:, N + 1 : N + 2])
             multiply(last, 2, 0, 256)
             square(last, 1, 256, 512)
-            weigh(last, 768, 1024, part=ends[:, 2:3])
+            weigh(last, 768, 1024, part=live["sq", last][:, N + 2 : N + 3])
             multiply(last, 2, 256, 384)
             square(last, 2, 0, 256)
-            weigh(last, 1024, 1280, part=ends[:, 3:4])
+            weigh(last, 1024, 1280, part=live["sq", last][:, N + 3 : N + 4])
             multiply(last, 2, 384, 512)
             square(last, 2, 256, 384)
-            weigh(last, 1280, 1408, part=ends[:, 4:5])
+            weigh(last, 1280, 1408, part=live["sq", last][:, N + 4 : N + 5])
             square(last, 2, 384, 512)
-            weigh(last, 1408, 1536, part=ends[:, 5:6])
-            nc.vector.tensor_scalar(out=shares[:], in0=ends[:], scalar1=1.0 / N, scalar2=None, op0=MULT, op1=mybir.AluOpType.add, accum_out=means[:, last:])
+            nc.vector.tensor_tensor(out=final[:], in0=live["sq", last][:, N - P : N], in1=trust_all[:, N - P : N], op=MULT)
+            nc.sync.dma_start(out=o_view[:, last, N - P : N], in_=final[:])
+            nc.vector.scalar_tensor_tensor(
+                out=shares[:],
+                in0=live["sq", last][:, N - P : N + 5],
+                scalar=1.0 / N,
+                in1=trust_all[:, N - P : N + 5],
+                op0=MULT,
+                op1=MULT,
+                accum_out=means[:, last:],
+            )
             nc.scalar.dma_start(out=out_1.rearrange("(p m) -> p m", m=TILES), in_=means[:])

@@ -105,11 +105,11 @@ def tile_bank_relation_distill_d6_kernel(
         def clear_scales(tile):
             nc.vector.memset(tile[:].rearrange("p g n -> p (g n)").bitcast(I32), 0)
 
-        def load_scales(tile, lo, hi):
+        def load_scales(tile, lo, hi, g0=0, g1=GT):
             for r in range(4):
                 nc.sync.dma_start(
-                    out=tile[r:P:32, :, :].bitcast(I32),
-                    in_=tbank_scales[:, r:16:4, lo:hi].rearrange("g q n -> q g n").bitcast(I32),
+                    out=tile[r:P:32, g0:g1, :].bitcast(I32),
+                    in_=tbank_scales[g0:g1, r:16:4, lo:hi].rearrange("g q n -> q g n").bitcast(I32),
                 )
 
         def tb_operand(n, g, lo, hi):
@@ -255,19 +255,27 @@ def tile_bank_relation_distill_d6_kernel(
                     at = P * (2 * (2 * h + g) + u)
                     nc.tensor.transpose(bank[:, g, u, :], words[:, at : at + P], ident[:])
 
-        def turn_flat(m, h):
+        def turn_flat(m, g):
             words = live["flat", m][:].bitcast(F32)
-            b, bank = claim([P, 2, 2, P], F32)
-            live["bt", m, h] = (b, bank)
-            for g in range(2):
-                for u in range(2):
-                    at = 2 * P * (2 * h + g)
-                    nc.tensor.transpose(bank[:, g, u, :], words[:, at + u : at + 2 * P : 2], ident[:])
+            if g % 2 == 0:
+                live["bt", m, g // 2] = claim([P, 2, 2, P], F32)
+            bank = live["bt", m, g // 2][1]
+            for u in range(2):
+                nc.tensor.transpose(bank[:, g % 2, u, :], words[:, 2 * P * g + u : 2 * P * (g + 1) : 2], ident[:])
+
+        def turn_half(m, g):
+            words = live["xt", m][:].rearrange("p g u w e -> p (g u w e)").bitcast(F32)
+            if g % 2 == 0:
+                live["bt", m, g // 2] = claim([P, 2, 2, P], F32)
+            bank = live["bt", m, g // 2][1]
+            for u in range(2):
+                at = P * (2 * g + u)
+                nc.tensor.transpose(bank[:, g % 2, u, :], words[:, at : at + P], ident[:])
 
         def turn_pass(m, g):
             words = live["xt", m][:].rearrange("p g u w e -> p (g u w e)").bitcast(F32)
             b, bank = claim([P, 1, 2, P], F32)
-            live["bt", m, g] = (b, bank)
+            live["bp", m, g] = (b, bank)
             for u in range(2):
                 at = P * (2 * g + u)
                 nc.tensor.transpose(bank[:, 0, u, :], words[:, at : at + P], ident[:])
@@ -275,10 +283,10 @@ def tile_bank_relation_distill_d6_kernel(
         def take_pass(m, g):
             if g == 0:
                 live["gt", m] = work.tile([P, GT, P, 2], F32, name="t_grouped", align_bytes=64)
-            take(live["gt", m][:, g : g + 1], live["bt", m, g], True)
+            take(live["gt", m][:, g : g + 1], live["bp", m, g], True)
 
         def take_t(m, h, on_scalar=True):
-            if h == 0:
+            if ("gt", m) not in live:
                 live["gt", m] = work.tile([P, GT, P, 2], F32, name="t_grouped", align_bytes=64)
             take(live["gt", m][:, 2 * h : 2 * h + 2], live["bt", m, h], on_scalar)
 
@@ -401,16 +409,16 @@ def tile_bank_relation_distill_d6_kernel(
             clear_scales(first_scales)
             make_identity(nc, ident[:])
             clear_scales(last_scales)
-            nc.vector.memset(early[:], 0.0)
             nc.sync.dma_start(out=scale[:], in_=teacher_scale.rearrange("(p m) c -> p m c", m=TILES))
             load_t(0)
             nc.sync.dma_start(out=trust_row[0:1, :], in_=trust.rearrange("(o n) -> o n", o=1))
             load_t(1)
-            load_scales(first_scales, 0, 2 * CHUNK)
-            for g in range(GT):
+            for g in (0, 2):
+                load_scales(first_scales, 0, 2 * CHUNK, g, g + 2)
                 load_first_words(g)
-            load_b_pair(0)
+                load_first_words(g + 1)
             load_t(2)
+            load_b_pair(0)
             load_b_pair(1)
             load_s_pair(0)
             load_s(2)
@@ -433,59 +441,69 @@ def tile_bank_relation_distill_d6_kernel(
             spread_trust(0)
             widen(0, 0, 8)
             widen_flat(0, 8, 16)
-            turn_t(0, 0)
-            take_t(0, 0)
-            spread_trust(1)
             widen(1, 0, 16)
-            turn_flat(0, 1)
-            take_t(0, 1)
+            turn_pass(0, 0)
+            take_pass(0, 0)
+            spread_trust(1)
+            turn_pass(0, 1)
+            take_pass(0, 1)
+            turn_flat(0, 2)
+            turn_pass(1, 0)
+            take_pass(1, 0)
+            turn_flat(0, 3)
+            turn_pass(1, 1)
+            take_pass(1, 1)
+            turn_half(1, 2)
             spread_trust(2)
-            quant_t(0, 0, 2)
-            for h in range(2):
-                turn_t(1, h)
-                take_t(1, h)
+            turn_half(1, 3)
+            quant_t(0, 0, 1)
+            quant_t(0, 1, 2)
+            take_t(0, 1, False)
+            take_t(1, 1)
+            quant_t(1, 0, 1)
+            quant_t(1, 1, 2)
             quant_t(0, 2, 4)
-            quant_t(1, 0, 2)
             quant_t(1, 2, 4)
             take_trust(0, 2)
             take_trust(2, 3)
-            for g in range(3):
-                open_group(0, 0, g, g + 1)
-                open_group(0, 1, g, g + 1)
-            open_group(1, 0, 0, 2)
-            open_group(1, 1, 0, 2)
+            for m in range(2):
+                for g in range(2):
+                    open_group(m, 0, g, g + 1)
+                    open_group(m, 1, g, g + 1)
+            open_group(0, 0, 2, 4)
+            open_group(0, 1, 2, 4)
+            open_group(1, 0, 2, 4)
+            widen(2, 0, 16)
             perm_b(0)
             perm_b(1)
-            widen(2, 0, 16)
-            open_group(0, 0, 3, 4)
-            open_group(0, 1, 3, 4)
-            turn_b(0)
-            take_b(0)
-            turn_b(1)
-            take_b(1)
-            perm_b(2)
-            perm_b(3)
-            perm_s(0)
-            perm_s(1)
-            open_group(1, 0, 2, 4)
             turn_t(2, 0)
             turn_t(2, 1)
-            turn_b(2)
-            turn_b(3)
+            turn_b(0)
+            turn_b(1)
             take_t(2, 0)
             take_t(2, 1)
-            take_b(2)
-            take_b(3)
-            perm_s(2)
-            quant_t(2)
-            quant_b(0, 0, 256)
+            take_b(0)
+            take_b(1)
             open_group(1, 1, 2, 4)
+            perm_b(2)
+            perm_b(3)
+            quant_t(2, 0, 2)
+            quant_t(2, 2, 4)
+            perm_s(0)
+            perm_s(1)
+            perm_s(2)
+            turn_b(2)
+            take_b(2)
+            turn_b(3)
+            take_b(3)
+            quant_b(0, 0, 256)
+            open_group(2, 0, 0, 2)
             for m in range(3):
                 turn_s(m)
                 take_s(m)
             perm_b(4)
             quant_b(0, 256, 512)
-            open_group(2, 0)
+            open_group(2, 0, 2, 4)
             open_group(2, 1)
             quant_s(0)
             perm_b(5, True)
@@ -554,19 +572,19 @@ def tile_bank_relation_distill_d6_kernel(
             open_group(2, 2)
             open_group(3, 2)
             quant_b(2, 256, 512)
-            weigh(1, 0, 1024, part=early[:, 1:2])
             perm_s(5, True)
             for m in (5, 6):
                 for h in range(2):
                     turn_t(m, h)
             flip_s(5)
-            weigh(2, 0, 1024, part=early[:, 2:3])
             take_t(5, 0)
             take_t(5, 1)
+            weigh(1, 0, 1024, part=early[:, 1:2])
             weave_s(5)
             for m in range(4):
                 close_group(m, 2)
             quant_t(5)
+            weigh(2, 0, 1024, part=early[:, 2:3])
             square(0, 2)
             square(1, 2)
             quant_s(5)
@@ -587,13 +605,14 @@ def tile_bank_relation_distill_d6_kernel(
             multiply(5, 1)
             square(5, 0)
             weave_s(6)
-            weigh(3, 0, 1536)
+            weigh(3, 0, 1024, part=early[:, 3:4])
             for h in range(2):
                 turn_t(7, h)
             square(5, 1)
             perm_s(7, True)
             quant_s(6)
-            weigh(4, 0, 1536)
+            weigh(3, 1024, 1536)
+            weigh(4, 0, 1024, part=early[:, 4:5])
             multiply(5, 2)
             take_t(7, 0)
             take_t(7, 1)
@@ -601,9 +620,11 @@ def tile_bank_relation_distill_d6_kernel(
             square(5, 2)
             multiply(6, 0)
             weave_s(7)
+            weigh(4, 1024, 1536)
             quant_t(7)
-            weigh(5, 0, 1536)
             quant_s(7)
+            weigh(5, 0, 1024, part=early[:, 5:6])
+            weigh(5, 1024, 1536)
             square(6, 0)
             multiply(6, 1)
             square(6, 1)

@@ -40,7 +40,7 @@ def tile_bank_relation_distill_d6_kernel(
         ident = const.tile([P, P], F32, name="ident")
         ones = const.tile([P, P], BF16, name="ones")
         trust_row = const.tile([P, N], BF16, name="trust_row")
-        trust_all = const.tile([P, N + 8], BF16, name="trust_all")
+        trust_all = const.tile([P, N + 5], BF16, name="trust_all")
         first_words = [const.tile([P, 4 * CHUNK], U8, name="first_words%d" % g, align_bytes=64) for g in range(GT)]
         last_words = const.tile([P, GT, 2 * CHUNK], U8, name="last_words", align_bytes=64)
         first_scales = const.tile([P, GT, 2 * CHUNK], U8, name="first_scales", align_bytes=64)
@@ -359,7 +359,7 @@ def tile_bank_relation_distill_d6_kernel(
 
         def square(m, n, lo=0, hi=CHUNK):
             if ("sq", m) not in live:
-                live["sq", m] = work.tile([P, N + 8], F32, name="sq", bufs=6)
+                live["sq", m] = work.tile([P, N + 5], F32, name="sq", bufs=6)
             b, acc = live["acc", m, n, lo]
             idle.append(b)
             nc.scalar.activation(
@@ -404,7 +404,7 @@ def tile_bank_relation_distill_d6_kernel(
 
         with tc.manual_schedule():
             nc.vector.memset(ones[:], 1.0)
-            nc.scalar.activation(out=trust_all[:, N:], in_=ones[:, :8], func=SQUARE)
+            nc.scalar.activation(out=trust_all[:, N:], in_=ones[:, :5], func=SQUARE)
             nc.vector.memset(trust_row[:].bitcast(I32), 0)
             clear_scales(first_scales)
             make_identity(nc, ident[:])

@@ -42,8 +42,8 @@ def tile_bank_relation_distill_d6_kernel(
         trust_row = const.tile([P, N], BF16, name="trust_row")
         trust_all = const.tile([P, N + 5], BF16, name="trust_all")
         first_words = [const.tile([P, 4 * CHUNK], U8, name="first_words%d" % g, align_bytes=64) for g in range(GT)]
-        last_words = const.tile([P, GT, 2 * CHUNK], U8, name="last_words", align_bytes=64)
-        first_scales = const.tile([P, GT, 2 * CHUNK], U8, name="first_scales", align_bytes=64)
+        last_words = [const.tile([P, 2 * CHUNK], U8, name="last_words%d" % g, align_bytes=64) for g in range(GT)]
+        first_scales = [const.tile([P, 2, 2 * CHUNK], U8, name="first_scales%d" % h, align_bytes=64) for h in range(2)]
         last_scales = const.tile([P, GT, CHUNK], U8, name="last_scales", align_bytes=64)
         scale = const.tile([P, TILES, K // P], F32, name="scale")
         neg = const.tile([P, TILES, K // P], F32, name="neg")
@@ -61,9 +61,8 @@ def tile_bank_relation_distill_d6_kernel(
         s_pair = const.tile([P, 2, J], BF16, name="s_pair", align_bytes=64)
         s_raw = [s_pair[:, 0], s_pair[:, 1]]
         s_raw.extend(const.tile([P, J], BF16, name="s_raw%d" % m, align_bytes=64)[:] for m in range(2, TILES))
-        b_pair = [const.tile([P, 2, J], BF16, name="b_pair%d" % j, align_bytes=64) for j in range(4)]
-        b_raw = [b_pair[i // 2][:, i % 2] for i in range(8)]
-        b_raw.extend(const.tile([P, J], BF16, name="b_raw%d" % i, align_bytes=64)[:] for i in range(8, N // P))
+        b_pair = [const.tile([P, 2, J], BF16, name="b_pair%d" % j, align_bytes=64) for j in range(6)]
+        b_raw = [b_pair[i // 2][:, i % 2] for i in range(12)]
         b_codes = [const.tile([P, GS, CHUNK], U32, name="b_codes%d" % n, align_bytes=64) for n in range(CHUNKS)]
         b_scales = [const.tile([P, GS, CHUNK], U8, name="b_scales%d" % n, align_bytes=64) for n in range(CHUNKS)]
 
@@ -78,7 +77,13 @@ def tile_bank_relation_distill_d6_kernel(
             rows = student.rearrange("(s i m) (a k) -> m a i s k", s=4, i=32, a=4)[m]
             load_quadrants(s_raw[m], rows)
 
-        def load_b_quadrants(i):
+        def load_b_quadrants(j):
+            rows = sbank[2 * P * j : 2 * P * (j + 1), :].rearrange("(s i) (a k) -> a i s k", s=8, a=4)
+            for a in (0, 2, 1, 3):
+                out = b_pair[j][32 * a : 32 * (a + 1)].rearrange("p e (s k) -> p (e s) k", s=4)
+                nc.sync.dma_start(out=out, in_=rows[a])
+
+        def load_b_tile_quadrants(i):
             rows = sbank[P * i : P * (i + 1), :].rearrange("(s i) (a k) -> a i s k", s=4, a=4)
             load_quadrants(b_raw[i], rows)
 
@@ -97,10 +102,8 @@ def tile_bank_relation_distill_d6_kernel(
             nc.sync.dma_start(out=first_words[g][:].bitcast(I32), in_=tbank_words[g, :, : 4 * CHUNK].bitcast(I32))
 
         def load_last_words():
-            nc.sync.dma_start(
-                out=last_words[:].bitcast(I32),
-                in_=tbank_words[:, :, 4 * CHUNK :].rearrange("g p w -> p g w").bitcast(I32),
-            )
+            for g in range(GT):
+                nc.sync.dma_start(out=last_words[g][:].bitcast(I32), in_=tbank_words[g, :, 4 * CHUNK :].bitcast(I32))
 
         def clear_scales(tile):
             nc.vector.memset(tile[:].rearrange("p g n -> p (g n)").bitcast(I32), 0)
@@ -108,15 +111,15 @@ def tile_bank_relation_distill_d6_kernel(
         def load_scales(tile, lo, hi, g0=0, g1=GT):
             for r in range(4):
                 nc.sync.dma_start(
-                    out=tile[r:P:32, g0:g1, :].bitcast(I32),
+                    out=tile[r:P:32].bitcast(I32),
                     in_=tbank_scales[g0:g1, r:16:4, lo:hi].rearrange("g q n -> q g n").bitcast(I32),
                 )
 
         def tb_operand(n, g, lo, hi):
             if n < CHUNKS - 1:
                 lo, hi = CHUNK * n + lo, CHUNK * n + hi
-                return first_words[g][:, 2 * lo : 2 * hi], first_scales[:, g, lo:hi]
-            return last_words[:, g, 2 * lo : 2 * hi], last_scales[:, g, lo:hi]
+                return first_words[g][:, 2 * lo : 2 * hi], first_scales[g // 2][:, g % 2, lo:hi]
+            return last_words[g][:, 2 * lo : 2 * hi], last_scales[:, g, lo:hi]
 
         def load_s_pair(m):
             nc.sync.dma_start(out=s_pair[:], in_=s_view[:, m : m + 2, :])
@@ -172,7 +175,7 @@ def tile_bank_relation_distill_d6_kernel(
             take(grouped[:], live["bs", m], on_scalar)
 
         def flip(key):
-            y = work.tile([P, GS, 2, P], F32, name="y", align_bytes=64, bufs=3)
+            y = work.tile([P, GS, 2, P], F32, name="y", align_bytes=64, bufs=5)
             nc.vector.transpose(
                 out=y[:].rearrange("p g u r -> p (g u r)"), in_=live[key][:].rearrange("p g u r -> p (g u r)")
             )
@@ -196,11 +199,14 @@ def tile_bank_relation_distill_d6_kernel(
             live["gs", m] = grouped
             weave(grouped[:], live["ys", m], on_scalar)
 
+        def b_slot(i):
+            j, e = divmod(i, 2)
+            if ("gb", j) not in live:
+                live["gb", j] = work.tile([P, GS, 2 * P, 2], F32, name="b_grouped", align_bytes=64, bufs=4)
+            return live["gb", j][:, :, P * e : P * (e + 1), :]
+
         def weave_b(i, on_scalar=True):
-            c, j = divmod(i, 4)
-            if j == 0:
-                live["gb", c] = work.tile([P, GS, CHUNK, 2], F32, name="b_grouped", align_bytes=64, bufs=2)
-            weave(live["gb", c][:, :, P * j : P * (j + 1), :], live["yb", i], on_scalar)
+            weave(b_slot(i), live["yb", i], on_scalar)
 
         def quant_s(m):
             codes = keep.tile([P, GS, P], U32, name="s_codes", align_bytes=64)
@@ -303,17 +309,14 @@ def tile_bank_relation_distill_d6_kernel(
             )
 
         def take_b(i, on_scalar=True):
-            c, j = divmod(i, 4)
-            if j == 0:
-                live["gb", c] = work.tile([P, GS, CHUNK, 2], F32, name="b_grouped", align_bytes=64, bufs=2)
-            take(live["gb", c][:, :, P * j : P * (j + 1), :], live["bb", i], on_scalar)
+            take(b_slot(i), live["bb", i], on_scalar)
 
         def quant_b(c, lo=0, hi=CHUNK):
             for g in range(GS):
                 nc.vector.quantize_mx(
                     out=b_codes[c][:, g, lo:hi].bitcast(FP8X4),
                     scales=b_scales[c][:, g, lo:hi],
-                    in_=live["gb", c][:, g, lo:hi].rearrange("p r u -> p (r u)").bitcast(BF16),
+                    in_=live["gb", 2 * c + lo // (2 * P)][:, g].rearrange("p r u -> p (r u)").bitcast(BF16),
                 )
 
         def passes_s(m, n, acc, lo, hi, first, last):
@@ -348,6 +351,12 @@ def tile_bank_relation_distill_d6_kernel(
             view = live["acc", m, n, lo][1][:, : hi - lo]
             passes_t(m, n, view, lo, hi, True, False)
             passes_s(m, n, view, lo, hi, False, True)
+
+        def multiply_student_first(m, n):
+            live["acc", m, n, 0] = claim([P, CHUNK], F32)
+            view = live["acc", m, n, 0][1][:]
+            passes_s(m, n, view, 0, CHUNK, True, False)
+            passes_t(m, n, view, 0, CHUNK, False, True)
 
         def open_group(m, n, g0=0, g1=GT):
             if g0 == 0:
@@ -406,7 +415,8 @@ def tile_bank_relation_distill_d6_kernel(
             nc.vector.memset(ones[:], 1.0)
             nc.scalar.activation(out=trust_all[:, N:], in_=ones[:, :5], func=SQUARE)
             nc.vector.memset(trust_row[:].bitcast(I32), 0)
-            clear_scales(first_scales)
+            clear_scales(first_scales[0])
+            clear_scales(first_scales[1])
             make_identity(nc, ident[:])
             clear_scales(last_scales)
             nc.sync.dma_start(out=scale[:], in_=teacher_scale.rearrange("(p m) c -> p m c", m=TILES))
@@ -414,7 +424,7 @@ def tile_bank_relation_distill_d6_kernel(
             nc.sync.dma_start(out=trust_row[0:1, :], in_=trust.rearrange("(o n) -> o n", o=1))
             load_t(1)
             for g in (0, 2):
-                load_scales(first_scales, 0, 2 * CHUNK, g, g + 2)
+                load_scales(first_scales[g // 2], 0, 2 * CHUNK, g, g + 2)
                 load_first_words(g)
                 load_first_words(g + 1)
             load_t(2)
@@ -423,19 +433,22 @@ def tile_bank_relation_distill_d6_kernel(
             load_s_pair(0)
             load_s(2)
             load_b_pair(2)
-            load_b_pair(3)
             load_t(3)
-            load_t(4)
+            load_b_tile_quadrants(6)
+            load_b_tile_quadrants(7)
             load_scales(last_scales, 2 * CHUNK, N)
             load_last_words()
             load_s_quadrants(3)
-            load_s_quadrants(4)
-            for i in range(8, 12):
-                load_b_quadrants(i)
+            load_t(4)
             load_t(5)
-            load_t(6)
+            load_s_quadrants(4)
+            load_b_quadrants(4)
             load_s_quadrants(5)
+            load_b_quadrants(5)
             load_t(7)
+            load_t(6)
+            load_s_quadrants(6)
+            load_s(7)
             nc.vector.tensor_scalar(out=neg[:], in0=scale[:], scalar1=-1.0, scalar2=None, op0=MULT)
             stir(4)
             spread_trust(0)
@@ -507,129 +520,152 @@ def tile_bank_relation_distill_d6_kernel(
             open_group(2, 1)
             quant_s(0)
             perm_b(5, True)
-            perm_b(6, True)
-            perm_b(7, True)
             quant_s(1)
             quant_s(2)
-            widen(3, 0, 16)
-            widen(4, 0, 16)
-            for m in range(3):
-                close_group(m, 0)
-                square(m, 0)
-            for i in range(4, 8):
-                turn_b(i)
-                take_b(i, i != 5)
-            open_group(0, 2)
-            quant_b(1, 0, 256)
-            quant_b(1, 256, 512)
+            perm_b(6, True)
+            widen(3,0,16)
+            close_group(0,0)
+            square(0,0)
+            close_group(1,0)
+            square(1,0)
+            close_group(2,0)
+            square(2,0)
+            turn_b(4)
+            turn_b(5)
+            turn_t(3,0)
+            turn_t(3,1)
+            perm_b(7)
+            flip_b(6)
+            flip_b(7)
+            take_b(4)
+            take_b(5)
+            weave_b(6, False)
+            weave_b(7, False)
+            open_group(0,2,0,2)
+            open_group(1,2,0,2)
+            open_group(0,2,2,4)
+            open_group(1,2,2,4)
+            take_t(3,0)
+            take_t(3,1)
+            quant_b(1,0,256)
+            quant_b(1,256,512)
             perm_s(3, True)
-            flip_s(3)
-            for m in (3, 4):
-                for h in range(2):
-                    turn_t(m, h)
-            take_t(3, 0)
-            take_t(3, 1)
-            weave_s(3)
-            perm_s(4)
             quant_t(3)
-            flip_s(4)
+            flip_s(3)
+            close_group(0,1)
+            square(0,1)
+            close_group(1,1)
+            weave_s(3)
+            square(1,1)
+            close_group(2,1)
+            square(2,1)
+            widen(4,0,16)
             quant_s(3)
-            take_t(4, 0)
-            take_t(4, 1)
-            for m in range(3):
-                close_group(m, 1)
-                square(m, 1)
-            open_group(1, 2)
-            perm_b(8)
-            quant_t(4)
+            widen(5,0,16)
+            perm_s(4, True)
+            open_group(3,0)
+            open_group(3,1)
+            close_group(3,0)
+            square(3,0)
+            close_group(3,1)
+            perm_b(8,True)
+            flip_s(4)
+            weigh(0,0,1024,part=early[:, 0:1])
+            weave_s(4,False)
             flip_b(8)
-            weave_s(4)
-            perm_b(9)
+            turn_t(4,0)
+            turn_t(4,1)
+            turn_t(5,0)
+            turn_t(5,1)
+            take_t(4,0)
+            take_t(4,1)
+            perm_b(9,True)
+            square(3,1)
+            quant_t(4,0,2)
+            quant_t(4,2,4)
             quant_s(4)
             flip_b(9)
-            multiply(3, 0)
+            open_group(2,2)
+            open_group(3,2)
+            take_t(5,0)
+            take_t(5,1)
+            perm_s(5,True)
+            perm_b(10,True)
+            perm_b(11,True)
             weave_b(8)
-            square(3, 0)
-            perm_b(10, True)
-            weigh(0, 0, 1024, part=early[:, 0:1])
-            load_s_quadrants(6)
-            load_s_quadrants(7)
-            multiply(3, 1)
             weave_b(9)
-            flip_b(10)
-            square(3, 1)
-            perm_b(11, True)
-            widen(5, 0, 16)
-            multiply(4, 0)
-            weave_b(10)
-            flip_b(11)
-            square(4, 0)
-            quant_b(2, 0, 256)
-            multiply(4, 1)
-            weave_b(11)
-            widen(6, 0, 16)
-            square(4, 1)
-            open_group(2, 2)
-            open_group(3, 2)
-            quant_b(2, 256, 512)
-            perm_s(5, True)
-            for m in (5, 6):
-                for h in range(2):
-                    turn_t(m, h)
-            flip_s(5)
-            take_t(5, 0)
-            take_t(5, 1)
-            weigh(1, 0, 1024, part=early[:, 1:2])
-            weave_s(5)
-            for m in range(4):
-                close_group(m, 2)
             quant_t(5)
-            weigh(2, 0, 1024, part=early[:, 2:3])
-            square(0, 2)
-            square(1, 2)
+            flip_s(5)
+            flip_b(10)
+            flip_b(11)
+            multiply(4,0)
+            square(4,0)
+            weave_s(5)
+            weave_b(10)
+            quant_b(2,0,256)
             quant_s(5)
-            weigh(0, 1024, 1536)
-            weigh(1, 1024, 1536)
-            take_t(6, 0)
-            take_t(6, 1)
-            multiply(4, 2)
-            square(2, 2)
-            square(3, 2)
-            widen(7, 0, 16)
-            weigh(2, 1024, 1536)
-            multiply(5, 0)
-            square(4, 2)
-            perm_s(6, True)
-            quant_t(6)
+            multiply(4,1)
+            weave_b(11)
+            square(4,1)
+            weigh(1,0,1024,part=early[:, 1:2])
+            quant_b(2,256,512)
+            open_group(5,0)
+            open_group(5,1)
+            widen_flat(7,0,8)
+            close_group(5,0)
+            square(5,0)
+            close_group(5,1)
+            square(5,1)
+            widen(6,0,16)
+            weigh(2,0,1024,part=early[:, 2:3])
+            close_group(0,2)
+            square(0,2)
+            close_group(1,2)
+            widen_flat(7,8,16)
+            square(1,2)
+            close_group(2,2)
+            square(2,2)
+            close_group(3,2)
+            square(3,2)
+            weigh(0,1024,1536)
+            perm_s(6)
+            part_t(7)
+            perm_s(7)
             flip_s(6)
-            multiply(5, 1)
-            square(5, 0)
+            multiply(4,2)
+            turn_t(6,0)
+            turn_t(6,1)
+            turn_t(7,0)
+            turn_t(7,1)
+            turn_s(7)
+            weigh(1,1024,1536)
+            weigh(2,1024,1536)
+            take_t(6,0)
+            take_t(6,1)
             weave_s(6)
-            weigh(3, 0, 1024, part=early[:, 3:4])
-            for h in range(2):
-                turn_t(7, h)
-            square(5, 1)
-            perm_s(7, True)
+            square(4,2)
+            multiply(5,2)
+            quant_t(6,0,2)
+            quant_t(6,2,4)
+            weigh(3,1024,1536)
             quant_s(6)
-            weigh(3, 1024, 1536)
-            weigh(4, 0, 1024, part=early[:, 4:5])
-            multiply(5, 2)
-            take_t(7, 0)
-            take_t(7, 1)
-            flip_s(7)
-            square(5, 2)
-            multiply(6, 0)
-            weave_s(7)
-            weigh(4, 1024, 1536)
+            take_t(7,0)
+            take_t(7,1)
+            take_s(7)
+            square(5,2)
+            weigh(3,0,1024,part=early[:, 3:4])
+            weigh(4,0,1024,part=early[:, 4:5])
+            multiply(6,0)
+            square(6,0)
             quant_t(7)
+            weigh(4,1024,1536)
             quant_s(7)
-            weigh(5, 0, 1024, part=early[:, 5:6])
-            weigh(5, 1024, 1536)
-            square(6, 0)
-            multiply(6, 1)
-            square(6, 1)
-            weigh(6, 0, 1024, part=early[:, 6:7])
-            multiply(6, 2)
+            weigh(5,0,1024,part=early[:, 5:6])
+            weigh(5,1024,1536)
+            multiply(6,1)
+            square(6,1)
+            weigh(6,0,1024,part=early[:, 6:7])
+            multiply(6,2)
             last = TILES - 1
             multiply(last, 0)
             square(last - 1, 2)

@@ -442,13 +442,15 @@ def tile_bank_relation_distill_d6_kernel(
             load_t(4)
             load_t(5)
             load_s_quadrants(4)
-            load_b_quadrants(4)
+            load_b_tile_quadrants(8)
+            load_b_tile_quadrants(9)
             load_s_quadrants(5)
-            load_b_quadrants(5)
+            load_b_tile_quadrants(10)
+            load_b_tile_quadrants(11)
             load_t(7)
             load_t(6)
-            load_s_quadrants(6)
             load_s(7)
+            load_s_quadrants(6)
             nc.vector.tensor_scalar(out=neg[:], in0=scale[:], scalar1=-1.0, scalar2=None, op0=MULT)
             stir(4)
             spread_trust(0)
@@ -579,35 +581,35 @@ def tile_bank_relation_distill_d6_kernel(
             turn_t(5,1)
             take_t(4,0)
             take_t(4,1)
-            perm_b(9,True)
             square(3,1)
+            quant_s(4)
             quant_t(4,0,2)
             quant_t(4,2,4)
-            quant_s(4)
-            flip_b(9)
+            weigh(1,0,1024,part=early[:, 1:2])
             open_group(2,2)
             open_group(3,2)
             take_t(5,0)
             take_t(5,1)
+            perm_b(9,True)
             perm_s(5,True)
             perm_b(10,True)
-            perm_b(11,True)
             weave_b(8)
-            weave_b(9)
             quant_t(5)
+            flip_b(9)
             flip_s(5)
             flip_b(10)
-            flip_b(11)
+            perm_b(11)
             multiply(4,0)
             square(4,0)
             weave_s(5)
-            weave_b(10)
-            quant_b(2,0,256)
+            weave_b(9)
+            flip_b(11)
             quant_s(5)
             multiply(4,1)
-            weave_b(11)
+            weave_b(10)
             square(4,1)
-            weigh(1,0,1024,part=early[:, 1:2])
+            weave_b(11,False)
+            quant_b(2,0,256)
             quant_b(2,256,512)
             open_group(5,0)
             open_group(5,1)

@@ -433,12 +433,11 @@ def tile_bank_relation_distill_d6_kernel(
             load_s_pair(0)
             load_s(2)
             load_b_pair(2)
+            load_b_pair(3)
             load_t(3)
-            load_b_tile_quadrants(6)
-            load_b_tile_quadrants(7)
+            load_s(3)
             load_scales(last_scales, 2 * CHUNK, N)
             load_last_words()
-            load_s_quadrants(3)
             load_t(4)
             load_t(5)
             load_s_quadrants(4)
@@ -447,10 +446,10 @@ def tile_bank_relation_distill_d6_kernel(
             load_s_quadrants(5)
             load_b_tile_quadrants(10)
             load_b_tile_quadrants(11)
-            load_t(7)
             load_t(6)
-            load_s(7)
+            load_t(7)
             load_s_quadrants(6)
+            load_s_quadrants(7)
             nc.vector.tensor_scalar(out=neg[:], in0=scale[:], scalar1=-1.0, scalar2=None, op0=MULT)
             stir(4)
             spread_trust(0)
@@ -516,16 +515,18 @@ def tile_bank_relation_distill_d6_kernel(
             for m in range(3):
                 turn_s(m)
                 take_s(m)
-            perm_b(4)
             quant_b(0, 256, 512)
             open_group(2, 0, 2, 4)
             open_group(2, 1)
             quant_s(0)
             perm_b(5, True)
+            perm_b(6, True)
             quant_s(1)
             quant_s(2)
-            perm_b(6, True)
+            perm_b(4)
+            perm_b(7)
             widen(3,0,16)
+            perm_s(3)
             close_group(0,0)
             square(0,0)
             close_group(1,0)
@@ -534,135 +535,124 @@ def tile_bank_relation_distill_d6_kernel(
             square(2,0)
             turn_b(4)
             turn_b(5)
-            turn_t(3,0)
-            turn_t(3,1)
-            perm_b(7)
-            flip_b(6)
-            flip_b(7)
+            turn_b(6)
+            turn_b(7)
             take_b(4)
-            take_b(5)
-            weave_b(6, False)
-            weave_b(7, False)
-            open_group(0,2,0,2)
-            open_group(1,2,0,2)
-            open_group(0,2,2,4)
-            open_group(1,2,2,4)
-            take_t(3,0)
-            take_t(3,1)
+            take_b(5,False)
+            take_b(6)
+            take_b(7,False)
+            open_group(0,2)
             quant_b(1,0,256)
             quant_b(1,256,512)
-            perm_s(3, True)
-            quant_t(3)
-            flip_s(3)
+            turn_t(3,0)
+            turn_t(3,1)
+            turn_s(3)
+            take_t(3,0)
+            take_t(3,1)
+            take_s(3)
+            widen(4,0,16)
             close_group(0,1)
             square(0,1)
             close_group(1,1)
-            weave_s(3)
             square(1,1)
             close_group(2,1)
             square(2,1)
-            widen(4,0,16)
+            quant_t(3)
             quant_s(3)
             widen(5,0,16)
-            perm_s(4, True)
-            open_group(3,0)
-            open_group(3,1)
-            close_group(3,0)
-            square(3,0)
-            close_group(3,1)
+            open_group(1,2)
+            perm_s(4,True)
             perm_b(8,True)
+            multiply(3,0)
+            square(3,0)
             flip_s(4)
             weigh(0,0,1024,part=early[:, 0:1])
-            weave_s(4,False)
             flip_b(8)
+            multiply(3,1)
+            weave_s(4)
+            perm_b(9,True)
+            square(3,1)
             turn_t(4,0)
             turn_t(4,1)
             turn_t(5,0)
             turn_t(5,1)
             take_t(4,0)
             take_t(4,1)
-            square(3,1)
             quant_s(4)
+            flip_b(9)
             quant_t(4,0,2)
             quant_t(4,2,4)
-            weigh(1,0,1024,part=early[:, 1:2])
             open_group(2,2)
             open_group(3,2)
+            perm_s(5,True)
             take_t(5,0)
             take_t(5,1)
-            perm_b(9,True)
-            perm_s(5,True)
             perm_b(10,True)
             weave_b(8)
-            quant_t(5)
-            flip_b(9)
+            perm_b(11,True)
+            weave_b(9)
+            weigh(1,0,1024,part=early[:, 1:2])
             flip_s(5)
+            quant_t(5)
             flip_b(10)
-            perm_b(11)
+            flip_b(11)
             multiply(4,0)
             square(4,0)
             weave_s(5)
-            weave_b(9)
-            flip_b(11)
-            quant_s(5)
-            multiply(4,1)
             weave_b(10)
-            square(4,1)
-            weave_b(11,False)
             quant_b(2,0,256)
-            quant_b(2,256,512)
-            open_group(5,0)
-            open_group(5,1)
-            widen_flat(7,0,8)
-            close_group(5,0)
-            square(5,0)
-            close_group(5,1)
-            square(5,1)
+            multiply(4,1)
+            weave_b(11)
+            square(4,1)
+            quant_s(5)
             widen(6,0,16)
+            quant_b(2,256,512)
+            multiply(5,0)
+            square(5,0)
+            perm_s(6,True)
             weigh(2,0,1024,part=early[:, 2:3])
+            widen(7,0,16)
+            multiply(5,1)
+            square(5,1)
             close_group(0,2)
             square(0,2)
             close_group(1,2)
-            widen_flat(7,8,16)
             square(1,2)
             close_group(2,2)
             square(2,2)
             close_group(3,2)
             square(3,2)
-            weigh(0,1024,1536)
-            perm_s(6)
-            part_t(7)
-            perm_s(7)
+            weigh(3,0,1024,part=early[:, 3:4])
             flip_s(6)
-            multiply(4,2)
+            weigh(0,1024,1536)
+            weigh(1,1024,1536)
             turn_t(6,0)
             turn_t(6,1)
             turn_t(7,0)
             turn_t(7,1)
-            turn_s(7)
-            weigh(1,1024,1536)
-            weigh(2,1024,1536)
             take_t(6,0)
             take_t(6,1)
             weave_s(6)
-            square(4,2)
-            multiply(5,2)
-            quant_t(6,0,2)
-            quant_t(6,2,4)
-            weigh(3,1024,1536)
+            perm_s(7,True)
+            multiply(4,2)
+            quant_t(6)
+            weigh(2,1024,1536)
             quant_s(6)
+            flip_s(7)
+            weigh(3,1024,1536)
+            square(4,2)
             take_t(7,0)
             take_t(7,1)
-            take_s(7)
+            multiply(5,2)
+            weave_s(7)
             square(5,2)
-            weigh(3,0,1024,part=early[:, 3:4])
             weigh(4,0,1024,part=early[:, 4:5])
-            multiply(6,0)
-            square(6,0)
             quant_t(7)
             weigh(4,1024,1536)
             quant_s(7)
             weigh(5,0,1024,part=early[:, 5:6])
+            multiply(6,0)
+            square(6,0)
             weigh(5,1024,1536)
             multiply(6,1)
             square(6,1)

@@ -42,8 +42,8 @@ def tile_bank_relation_distill_d6_kernel(
         trust_row = const.tile([P, N], BF16, name="trust_row")
         trust_all = const.tile([P, N + 5], BF16, name="trust_all")
         first_words = [const.tile([P, 4 * CHUNK], U8, name="first_words%d" % g, align_bytes=64) for g in range(GT)]
-        last_words = [const.tile([P, 2 * CHUNK], U8, name="last_words%d" % g, align_bytes=64) for g in range(GT)]
-        first_scales = [const.tile([P, 2, 2 * CHUNK], U8, name="first_scales%d" % h, align_bytes=64) for h in range(2)]
+        last_words = [const.tile([P, 2, 2 * CHUNK], U8, name="last_words%d" % h, align_bytes=64) for h in range(2)]
+        first_scales = const.tile([P, GT, 2 * CHUNK], U8, name="first_scales", align_bytes=64)
         last_scales = const.tile([P, GT, CHUNK], U8, name="last_scales", align_bytes=64)
         scale = const.tile([P, TILES, K // P], F32, name="scale")
         neg = const.tile([P, TILES, K // P], F32, name="neg")
@@ -102,8 +102,9 @@ def tile_bank_relation_distill_d6_kernel(
             nc.sync.dma_start(out=first_words[g][:].bitcast(I32), in_=tbank_words[g, :, : 4 * CHUNK].bitcast(I32))
 
         def load_last_words():
-            for g in range(GT):
-                nc.sync.dma_start(out=last_words[g][:].bitcast(I32), in_=tbank_words[g, :, 4 * CHUNK :].bitcast(I32))
+            for h in range(2):
+                rows = tbank_words[2 * h : 2 * h + 2, :, 4 * CHUNK :].rearrange("g p w -> p g w")
+                nc.sync.dma_start(out=last_words[h][:].bitcast(I32), in_=rows.bitcast(I32))
 
         def clear_scales(tile):
             nc.vector.memset(tile[:].rearrange("p g n -> p (g n)").bitcast(I32), 0)
@@ -118,8 +119,8 @@ def tile_bank_relation_distill_d6_kernel(
         def tb_operand(n, g, lo, hi):
             if n < CHUNKS - 1:
                 lo, hi = CHUNK * n + lo, CHUNK * n + hi
-                return first_words[g][:, 2 * lo : 2 * hi], first_scales[g // 2][:, g % 2, lo:hi]
-            return last_words[g][:, 2 * lo : 2 * hi], last_scales[:, g, lo:hi]
+                return first_words[g][:, 2 * lo : 2 * hi], first_scales[:, g, lo:hi]
+            return last_words[g // 2][:, g % 2, 2 * lo : 2 * hi], last_scales[:, g, lo:hi]
 
         def load_s_pair(m):
             nc.sync.dma_start(out=s_pair[:], in_=s_view[:, m : m + 2, :])
@@ -415,20 +416,20 @@ def tile_bank_relation_distill_d6_kernel(
             nc.vector.memset(ones[:], 1.0)
             nc.scalar.activation(out=trust_all[:, N:], in_=ones[:, :5], func=SQUARE)
             nc.vector.memset(trust_row[:].bitcast(I32), 0)
-            clear_scales(first_scales[0])
-            clear_scales(first_scales[1])
+            clear_scales(first_scales)
             make_identity(nc, ident[:])
             clear_scales(last_scales)
             nc.sync.dma_start(out=scale[:], in_=teacher_scale.rearrange("(p m) c -> p m c", m=TILES))
             load_t(0)
             nc.sync.dma_start(out=trust_row[0:1, :], in_=trust.rearrange("(o n) -> o n", o=1))
             load_t(1)
-            for g in (0, 2):
-                load_scales(first_scales[g // 2], 0, 2 * CHUNK, g, g + 2)
-                load_first_words(g)
-                load_first_words(g + 1)
+            load_scales(first_scales, 0, 2 * CHUNK)
+            load_first_words(0)
+            load_first_words(1)
+            load_first_words(2)
             load_t(2)
             load_b_pair(0)
+            load_first_words(3)
             load_b_pair(1)
             load_s_pair(0)
             load_s(2)
@@ -464,6 +465,7 @@ def tile_bank_relation_distill_d6_kernel(
             turn_flat(0, 2)
             turn_pass(1, 0)
             take_pass(1, 0)
+            stir(1)
             turn_flat(0, 3)
             turn_pass(1, 1)
             take_pass(1, 1)
@@ -484,40 +486,46 @@ def tile_bank_relation_distill_d6_kernel(
                 for g in range(2):
                     open_group(m, 0, g, g + 1)
                     open_group(m, 1, g, g + 1)
-            open_group(0, 0, 2, 4)
-            open_group(0, 1, 2, 4)
-            open_group(1, 0, 2, 4)
-            widen(2, 0, 16)
+            open_group(0,0,2,3)
+            open_group(0,1,2,3)
+            open_group(1,0,2,3)
+            open_group(1,1,2,3)
+            widen(2,0,16)
             perm_b(0)
             perm_b(1)
-            turn_t(2, 0)
-            turn_t(2, 1)
+            turn_t(2,0)
+            turn_t(2,1)
             turn_b(0)
             turn_b(1)
-            take_t(2, 0)
-            take_t(2, 1)
+            take_t(2,0)
+            take_t(2,1)
             take_b(0)
             take_b(1)
-            open_group(1, 1, 2, 4)
+            open_group(0,0,3,4)
+            open_group(0,1,3,4)
+            open_group(1,0,3,4)
             perm_b(2)
             perm_b(3)
-            quant_t(2, 0, 2)
-            quant_t(2, 2, 4)
-            perm_s(0)
-            perm_s(1)
-            perm_s(2)
+            quant_t(2,0,4)
             turn_b(2)
             take_b(2)
             turn_b(3)
             take_b(3)
-            quant_b(0, 0, 256)
-            open_group(2, 0, 0, 2)
-            for m in range(3):
-                turn_s(m)
-                take_s(m)
-            quant_b(0, 256, 512)
-            open_group(2, 0, 2, 4)
-            open_group(2, 1)
+            perm_s(0)
+            perm_s(1)
+            quant_b(0,0,256)
+            perm_s(2)
+            open_group(2,0,0,3)
+            turn_s(0)
+            take_s(0)
+            turn_s(1)
+            take_s(1)
+            turn_s(2)
+            take_s(2)
+            quant_b(0,256,512)
+            open_group(1,1,3,4)
+            open_group(2,0,3,4)
+            open_group(2,1)
             quant_s(0)
             perm_b(5, True)
             perm_b(6, True)

@@ -436,10 +436,10 @@ def tile_bank_relation_distill_d6_kernel(
             load_b_pair(2)
             load_b_pair(3)
             load_t(3)
-            load_s(3)
+            load_t(4)
             load_scales(last_scales, 2 * CHUNK, N)
             load_last_words()
-            load_t(4)
+            load_s_quadrants(3)
             load_t(5)
             load_s_quadrants(4)
             load_b_tile_quadrants(8)
@@ -527,14 +527,14 @@ def tile_bank_relation_distill_d6_kernel(
             open_group(2,0,3,4)
             open_group(2,1)
             quant_s(0)
-            perm_b(5, True)
-            perm_b(6, True)
+            perm_b(5,True)
+            perm_b(6,True)
             quant_s(1)
             quant_s(2)
             perm_b(4)
             perm_b(7)
             widen(3,0,16)
-            perm_s(3)
+            widen(4,0,16)
             close_group(0,0)
             square(0,0)
             close_group(1,0)
@@ -542,85 +542,94 @@ def tile_bank_relation_distill_d6_kernel(
             close_group(2,0)
             square(2,0)
             turn_b(4)
-            turn_b(5)
-            turn_b(6)
-            turn_b(7)
             take_b(4)
-            take_b(5,False)
+            turn_b(5)
+            take_b(5)
+            turn_b(6)
             take_b(6)
-            take_b(7,False)
+            turn_b(7)
+            take_b(7)
             open_group(0,2)
+            open_group(1,2)
             quant_b(1,0,256)
             quant_b(1,256,512)
             turn_t(3,0)
             turn_t(3,1)
-            turn_s(3)
+            turn_t(4,0)
+            perm_s(3,True)
             take_t(3,0)
             take_t(3,1)
-            take_s(3)
-            widen(4,0,16)
+            flip_s(3)
+            quant_t(3,0,2)
+            weave_s(3)
+            take_t(4,0)
             close_group(0,1)
             square(0,1)
             close_group(1,1)
             square(1,1)
             close_group(2,1)
             square(2,1)
-            quant_t(3)
+            quant_t(3,2,4)
+            widen(5,0,8)
             quant_s(3)
-            widen(5,0,16)
-            open_group(1,2)
+            widen(5,8,16)
+            quant_t(4,0,2)
             perm_s(4,True)
             perm_b(8,True)
-            multiply(3,0)
+            open_group(3,0,0,2)
+            open_group(3,1,0,2)
+            open_group(3,0,2,4)
+            open_group(3,1,2,4)
+            close_group(3,0)
             square(3,0)
-            flip_s(4)
             weigh(0,0,1024,part=early[:, 0:1])
+            flip_s(4)
             flip_b(8)
-            multiply(3,1)
-            weave_s(4)
-            perm_b(9,True)
+            close_group(3,1)
             square(3,1)
-            turn_t(4,0)
             turn_t(4,1)
             turn_t(5,0)
             turn_t(5,1)
-            take_t(4,0)
             take_t(4,1)
+            weave_s(4)
+            take_t(5,0)
+            take_t(5,1)
+            weigh(1,0,1024,part=early[:, 1:2])
+            quant_t(4,2,4)
+            perm_b(9)
             quant_s(4)
             flip_b(9)
-            quant_t(4,0,2)
-            quant_t(4,2,4)
+            weigh(2,0,1024,part=early[:, 2:3])
             open_group(2,2)
             open_group(3,2)
             perm_s(5,True)
-            take_t(5,0)
-            take_t(5,1)
             perm_b(10,True)
             weave_b(8)
             perm_b(11,True)
-            weave_b(9)
-            weigh(1,0,1024,part=early[:, 1:2])
-            flip_s(5)
             quant_t(5)
+            flip_s(5)
             flip_b(10)
             flip_b(11)
             multiply(4,0)
             square(4,0)
             weave_s(5)
+            weave_b(9)
             weave_b(10)
+            quant_s(5)
             quant_b(2,0,256)
             multiply(4,1)
             weave_b(11)
             square(4,1)
-            quant_s(5)
-            widen(6,0,16)
+            widen(6,0,4)
             quant_b(2,256,512)
-            multiply(5,0)
-            square(5,0)
+            widen(6,4,16)
+            open_group(5,0)
+            open_group(5,1)
+            close_group(5,0)
             perm_s(6,True)
-            weigh(2,0,1024,part=early[:, 2:3])
+            square(5,0)
             widen(7,0,16)
-            multiply(5,1)
+            close_group(5,1)
             square(5,1)
             close_group(0,2)
             square(0,2)
@@ -646,21 +655,21 @@ def tile_bank_relation_distill_d6_kernel(
             quant_t(6)
             weigh(2,1024,1536)
             quant_s(6)
-            flip_s(7)
             weigh(3,1024,1536)
             square(4,2)
             take_t(7,0)
             take_t(7,1)
             multiply(5,2)
-            weave_s(7)
             square(5,2)
             weigh(4,0,1024,part=early[:, 4:5])
-            quant_t(7)
+            flip_s(7)
             weigh(4,1024,1536)
-            quant_s(7)
+            quant_t(7)
             weigh(5,0,1024,part=early[:, 5:6])
             multiply(6,0)
             square(6,0)
+            weave_s(7)
+            quant_s(7)
             weigh(5,1024,1536)
             multiply(6,1)
             square(6,1)

@@ -24,6 +24,7 @@ CHUNKS = N // CHUNK
 GT = K // 512
 GS = J // 512
 BANKS = 8
+PAIRS = (2, 3)
 
 
 def tile_bank_relation_distill_d6_kernel(
@@ -48,7 +49,7 @@ def tile_bank_relation_distill_d6_kernel(
         scale = const.tile([P, TILES, K // P], F32, name="scale")
         neg = const.tile([P, TILES, K // P], F32, name="neg")
         total = const.tile([P, TILES - 1], F32, name="total")
-        early = const.tile([P, 7], F32, name="early")
+        parts = const.tile([P, TILES - 1, CHUNKS], F32, name="parts")
         shares = const.tile([P, P + 5], F32, name="shares")
         final = const.tile([P, P], F32, name="final")
         means = const.tile([P, TILES], F32, name="means")
@@ -57,12 +58,16 @@ def tile_bank_relation_distill_d6_kernel(
         s_view = student.rearrange("(p m) k -> p m k", m=TILES)
         o_view = out_0.rearrange("(p m) n -> p m n", m=TILES)
 
-        t_raw = [const.tile([P, K], U8, name="t_raw%d" % m, align_bytes=64) for m in range(TILES)]
+        t_half = [const.tile([P, K // 2], U8, name="t_half%d" % h, align_bytes=64) for h in range(2)]
+        t_raw = {m: const.tile([P, K], U8, name="t_raw%d" % m, align_bytes=64) for m in range(1, TILES)}
         s_pair = const.tile([P, 2, J], BF16, name="s_pair", align_bytes=64)
         s_raw = [s_pair[:, 0], s_pair[:, 1]]
         s_raw.extend(const.tile([P, J], BF16, name="s_raw%d" % m, align_bytes=64)[:] for m in range(2, TILES))
-        b_pair = [const.tile([P, 2, J], BF16, name="b_pair%d" % j, align_bytes=64) for j in range(6)]
-        b_raw = [b_pair[i // 2][:, i % 2] for i in range(12)]
+        b_pair = {j: const.tile([P, 2, J], BF16, name="b_pair%d" % j, align_bytes=64) for j in PAIRS}
+        b_raw = [
+            b_pair[i // 2][:, i % 2] if i // 2 in PAIRS else const.tile([P, J], BF16, name="b_raw%d" % i, align_bytes=64)[:]
+            for i in range(12)
+        ]
         b_codes = [const.tile([P, GS, CHUNK], U32, name="b_codes%d" % n, align_bytes=64) for n in range(CHUNKS)]
         b_scales = [const.tile([P, GS, CHUNK], U8, name="b_scales%d" % n, align_bytes=64) for n in range(CHUNKS)]
 
@@ -77,18 +82,20 @@ def tile_bank_relation_distill_d6_kernel(
             rows = student.rearrange("(s i m) (a k) -> m a i s k", s=4, i=32, a=4)[m]
             load_quadrants(s_raw[m], rows)
 
-        def load_b_quadrants(j):
-            rows = sbank[2 * P * j : 2 * P * (j + 1), :].rearrange("(s i) (a k) -> a i s k", s=8, a=4)
-            for a in (0, 2, 1, 3):
-                out = b_pair[j][32 * a : 32 * (a + 1)].rearrange("p e (s k) -> p (e s) k", s=4)
-                nc.sync.dma_start(out=out, in_=rows[a])
-
         def load_b_tile_quadrants(i):
             rows = sbank[P * i : P * (i + 1), :].rearrange("(s i) (a k) -> a i s k", s=4, a=4)
             load_quadrants(b_raw[i], rows)
 
         def load_t(m):
             nc.sync.dma_start(out=t_raw[m][:], in_=t_view[:, m, :])
+
+        def load_t_half(h):
+            nc.sync.dma_start(out=t_half[h][:], in_=t_view[:, 0, K // 2 * h : K // 2 * (h + 1)])
+
+        def block(m, c):
+            if m == 0:
+                return t_half[c // 8][:, P * (c % 8) : P * (c % 8 + 1)].bitcast(FP8)
+            return t_raw[m][:, P * c : P * (c + 1)].bitcast(FP8)
 
         def load_b(lo, hi):
             for i in range(lo, hi):
@@ -227,31 +234,21 @@ def tile_bank_relation_distill_d6_kernel(
                 g, q = divmod(c, 4)
                 nc.vector.tensor_scalar(
                     out=xt[:, g, :, 32 * q : 32 * (q + 1), :].rearrange("p u w e -> p w u e"),
-                    in0=t_raw[m][:, P * c : P * (c + 1)].bitcast(FP8).rearrange("p (w u e) -> p w u e", u=2, e=2),
+                    in0=block(m, c).rearrange("p (w u e) -> p w u e", u=2, e=2),
                     scalar1=neg[:, m, c : c + 1],
                     scalar2=None,
                     op0=MULT,
                 )
 
         def widen_flat(m, lo, hi):
-            if ("flat", m) not in live:
-                live["flat", m] = work.tile([P, K], BF16, name="flat", align_bytes=64, bufs=1)
+            live["flat", m] = work.tile([P, P * (hi - lo)], BF16, name="flat", align_bytes=64, bufs=2)
             for c in range(lo, hi):
                 nc.scalar.activation(
-                    out=live["flat", m][:, P * c : P * (c + 1)],
-                    in_=t_raw[m][:, P * c : P * (c + 1)].bitcast(FP8),
+                    out=live["flat", m][:, P * (c - lo) : P * (c - lo + 1)],
+                    in_=block(m, c),
                     func=mybir.ActivationFunctionType.Copy,
                     scale=neg[:, m, c : c + 1],
                 )
-
-        def part_t(m, on_scalar=False):
-            live["xt", m] = work.tile([P, GT, 2, P, 2], BF16, name="xt", align_bytes=64)
-            dst = live["xt", m][:].rearrange("p g u w e -> p (g u w e)").bitcast(F32).rearrange("p (g u w) -> p g u w", g=GT, u=2)
-            src = live["flat", m][:].bitcast(F32).rearrange("p (g w u) -> p g u w", g=GT, u=2)
-            if on_scalar:
-                nc.scalar.copy(out=dst, in_=src)
-            else:
-                nc.vector.tensor_copy(out=dst, in_=src)
 
         def turn_t(m, h):
             words = live["xt", m][:].rearrange("p g u w e -> p (g u w e)").bitcast(F32)
@@ -264,15 +261,15 @@ def tile_bank_relation_distill_d6_kernel(
 
         def turn_flat(m, g):
             words = live["flat", m][:].bitcast(F32)
-            if g % 2 == 0:
+            if ("bt", m, g // 2) not in live:
                 live["bt", m, g // 2] = claim([P, 2, 2, P], F32)
             bank = live["bt", m, g // 2][1]
             for u in range(2):
-                nc.tensor.transpose(bank[:, g % 2, u, :], words[:, 2 * P * g + u : 2 * P * (g + 1) : 2], ident[:])
+                nc.tensor.transpose(bank[:, g % 2, u, :], words[:, u : 2 * P : 2], ident[:])
 
         def turn_half(m, g):
             words = live["xt", m][:].rearrange("p g u w e -> p (g u w e)").bitcast(F32)
-            if g % 2 == 0:
+            if ("bt", m, g // 2) not in live:
                 live["bt", m, g // 2] = claim([P, 2, 2, P], F32)
             bank = live["bt", m, g // 2][1]
             for u in range(2):
@@ -353,12 +350,6 @@ def tile_bank_relation_distill_d6_kernel(
             passes_t(m, n, view, lo, hi, True, False)
             passes_s(m, n, view, lo, hi, False, True)
 
-        def multiply_student_first(m, n):
-            live["acc", m, n, 0] = claim([P, CHUNK], F32)
-            view = live["acc", m, n, 0][1][:]
-            passes_s(m, n, view, 0, CHUNK, True, False)
-            passes_t(m, n, view, 0, CHUNK, False, True)
-
         def open_group(m, n, g0=0, g1=GT):
             if g0 == 0:
                 live["acc", m, n, 0] = claim([P, CHUNK], F32)
@@ -385,7 +376,7 @@ def tile_bank_relation_distill_d6_kernel(
                 in1=trust_all[:, lo:hi],
                 op0=MULT,
                 op1=MULT,
-                accum_out=total[:, m : m + 1] if part is None else part,
+                accum_out=parts[:, m, lo // CHUNK : lo // CHUNK + 1] if part is None else part,
             )
             queue.dma_start(out=o_view[:, m, lo:hi], in_=res)
 
@@ -419,8 +410,10 @@ def tile_bank_relation_distill_d6_kernel(
             clear_scales(first_scales)
             make_identity(nc, ident[:])
             clear_scales(last_scales)
+            nc.vector.memset(parts[:], 0.0)
             nc.sync.dma_start(out=scale[:], in_=teacher_scale.rearrange("(p m) c -> p m c", m=TILES))
-            load_t(0)
+            load_t_half(0)
+            load_t_half(1)
             nc.sync.dma_start(out=trust_row[0:1, :], in_=trust.rearrange("(o n) -> o n", o=1))
             load_t(1)
             load_scales(first_scales, 0, 2 * CHUNK)
@@ -428,14 +421,14 @@ def tile_bank_relation_distill_d6_kernel(
             load_first_words(1)
             load_first_words(2)
             load_t(2)
-            load_b_pair(0)
+            load_b(0, 2)
             load_first_words(3)
-            load_b_pair(1)
+            load_b(2, 4)
             load_s_pair(0)
             load_s(2)
+            load_t(3)
             load_b_pair(2)
             load_b_pair(3)
-            load_t(3)
             load_t(4)
             load_scales(last_scales, 2 * CHUNK, N)
             load_last_words()
@@ -454,24 +447,24 @@ def tile_bank_relation_distill_d6_kernel(
             nc.vector.tensor_scalar(out=neg[:], in0=scale[:], scalar1=-1.0, scalar2=None, op0=MULT)
             stir(4)
             spread_trust(0)
-            widen(0, 0, 8)
-            widen_flat(0, 8, 16)
-            widen(1, 0, 16)
+            widen(0, 0, 12)
+            widen_flat(0, 12, 16)
+            widen(1, 0, 12)
+            widen_flat(1, 12, 16)
             turn_pass(0, 0)
-            take_pass(0, 0)
-            spread_trust(1)
             turn_pass(0, 1)
+            spread_trust(1)
+            take_pass(0, 0)
             take_pass(0, 1)
-            turn_flat(0, 2)
+            turn_flat(0, 3)
+            turn_half(0, 2)
             turn_pass(1, 0)
             take_pass(1, 0)
-            stir(1)
-            turn_flat(0, 3)
+            spread_trust(2)
             turn_pass(1, 1)
             take_pass(1, 1)
+            turn_flat(1, 3)
             turn_half(1, 2)
-            spread_trust(2)
-            turn_half(1, 3)
             quant_t(0, 0, 1)
             quant_t(0, 1, 2)
             take_t(0, 1, False)
@@ -491,30 +484,31 @@ def tile_bank_relation_distill_d6_kernel(
             open_group(1,0,2,3)
             open_group(1,1,2,3)
             widen(2,0,16)
-            perm_b(0)
-            perm_b(1)
+            perm_b(0,True)
+            perm_b(1,True)
             turn_t(2,0)
             turn_t(2,1)
             turn_b(0)
             turn_b(1)
             take_t(2,0)
-            take_t(2,1)
             take_b(0)
             take_b(1)
             open_group(0,0,3,4)
             open_group(0,1,3,4)
             open_group(1,0,3,4)
             perm_b(2)
+            take_t(2,1,False)
             perm_b(3)
-            quant_t(2,0,4)
+            quant_t(2,0,2)
+            quant_t(2,2,4)
             turn_b(2)
             take_b(2)
             turn_b(3)
             take_b(3)
             perm_s(0)
             perm_s(1)
-            quant_b(0,0,256)
             perm_s(2)
+            quant_b(0,0,256)
             open_group(2,0,0,3)
             turn_s(0)
             take_s(0)
@@ -523,20 +517,24 @@ def tile_bank_relation_distill_d6_kernel(
             turn_s(2)
             take_s(2)
             quant_b(0,256,512)
+            widen(3,0,5)
             open_group(1,1,3,4)
             open_group(2,0,3,4)
             open_group(2,1)
             quant_s(0)
+            widen(3,5,7)
             perm_b(5,True)
             perm_b(6,True)
             quant_s(1)
+            widen(3,7,9)
             quant_s(2)
             perm_b(4)
             perm_b(7)
-            widen(3,0,16)
+            widen(3,9,16)
             widen(4,0,16)
             close_group(0,0)
             square(0,0)
+            weigh(0,0,512)
             close_group(1,0)
             square(1,0)
             close_group(2,0)
@@ -552,6 +550,7 @@ def tile_bank_relation_distill_d6_kernel(
             open_group(0,2)
             open_group(1,2)
             quant_b(1,0,256)
+            weigh(1,0,512)
             quant_b(1,256,512)
             turn_t(3,0)
             turn_t(3,1)
@@ -560,6 +559,7 @@ def tile_bank_relation_distill_d6_kernel(
             take_t(3,0)
             take_t(3,1)
             flip_s(3)
+            weigh(2,0,512)
             quant_t(3,0,2)
             weave_s(3)
             take_t(4,0)
@@ -582,7 +582,7 @@ def tile_bank_relation_distill_d6_kernel(
             open_group(3,1,2,4)
             close_group(3,0)
             square(3,0)
-            weigh(0,0,1024,part=early[:, 0:1])
+            weigh(0,512,1024)
             flip_s(4)
             flip_b(8)
             close_group(3,1)
@@ -594,26 +594,26 @@ def tile_bank_relation_distill_d6_kernel(
             weave_s(4)
             take_t(5,0)
             take_t(5,1)
-            weigh(1,0,1024,part=early[:, 1:2])
+            weigh(1,512,1024)
             quant_t(4,2,4)
             perm_b(9)
             quant_s(4)
             flip_b(9)
-            weigh(2,0,1024,part=early[:, 2:3])
+            weigh(2,512,1024)
             open_group(2,2)
             open_group(3,2)
             perm_s(5,True)
             perm_b(10,True)
             weave_b(8)
-            perm_b(11,True)
+            weave_b(9)
             quant_t(5)
             flip_s(5)
+            perm_b(11)
             flip_b(10)
             flip_b(11)
             multiply(4,0)
             square(4,0)
             weave_s(5)
-            weave_b(9)
             weave_b(10)
             quant_s(5)
             quant_b(2,0,256)
@@ -639,10 +639,9 @@ def tile_bank_relation_distill_d6_kernel(
             square(2,2)
             close_group(3,2)
             square(3,2)
-            weigh(3,0,1024,part=early[:, 3:4])
             flip_s(6)
+            weigh(3,0,1024)
             weigh(0,1024,1536)
-            weigh(1,1024,1536)
             turn_t(6,0)
             turn_t(6,1)
             turn_t(7,0)
@@ -653,27 +652,28 @@ def tile_bank_relation_distill_d6_kernel(
             perm_s(7,True)
             multiply(4,2)
             quant_t(6)
-            weigh(2,1024,1536)
             quant_s(6)
+            weigh(1,1024,1536)
+            weigh(2,1024,1536)
+            flip_s(7)
             weigh(3,1024,1536)
             square(4,2)
             take_t(7,0)
             take_t(7,1)
             multiply(5,2)
+            weave_s(7)
             square(5,2)
-            weigh(4,0,1024,part=early[:, 4:5])
-            flip_s(7)
-            weigh(4,1024,1536)
+            weigh(4,0,1024)
             quant_t(7)
-            weigh(5,0,1024,part=early[:, 5:6])
+            weigh(4,1024,1536)
             multiply(6,0)
             square(6,0)
-            weave_s(7)
             quant_s(7)
+            weigh(5,0,1024)
             weigh(5,1024,1536)
             multiply(6,1)
             square(6,1)
-            weigh(6,0,1024,part=early[:, 6:7])
+            weigh(6,0,1024)
             multiply(6,2)
             last = TILES - 1
             multiply(last, 0)
@@ -681,7 +681,7 @@ def tile_bank_relation_distill_d6_kernel(
             weigh(last - 1, 1024, 1536)
             multiply(last, 1, 0, 256)
             square(last, 0)
-            nc.vector.tensor_tensor(out=total[:], in0=total[:], in1=early[:], op=mybir.AluOpType.add)
+            nc.vector.tensor_reduce(out=total[:], in_=parts[:], axis=mybir.AxisListType.X, op=mybir.AluOpType.add)
             weigh(last, 0, 512, part=live["sq", last][:, N + 0 : N + 1])
             nc.vector.tensor_scalar(out=means[:, :last], in0=total[:], scalar1=1.0 / N, scalar2=None, op0=MULT)
             multiply(last, 1, 256, 512)

@@ -240,6 +240,36 @@ def tile_bank_relation_distill_d6_kernel(
                     op0=MULT,
                 )
 
+        def widen_parked(m):
+            xq = work.tile([P, 4, 2, 2, 32, 2], BF16, name="parked", align_bytes=64, bufs=1)
+            for c in range(8, 16):
+                g, q = divmod(c, 4)
+                nc.vector.tensor_scalar(
+                    out=xq[:, q, g - 2].rearrange("p u w e -> p w u e"),
+                    in0=block(m, c).rearrange("p (w u e) -> p w u e", u=2, e=2),
+                    scalar1=neg[:, m, c : c + 1],
+                    scalar2=None,
+                    op0=MULT,
+                )
+            park = o_view[:, m, :CHUNK].bitcast(BF16)
+            nc.sync.dma_start(out=park, in_=xq[:].rearrange("p q g u w e -> p (q g u w e)"))
+            back = work.tile([P, 2 * CHUNK], BF16, name="back", align_bytes=64, bufs=1)
+            live["back", m] = back
+            rows = park.rearrange("(s i) (a w) -> a i s w", s=4, a=4)
+            for a in (0, 2, 1, 3):
+                nc.sync.dma_start(out=back[32 * a : 32 * (a + 1), :].rearrange("p (s w) -> p s w", s=4), in_=rows[a])
+
+        def flip_t(m):
+            y = work.tile([P, CHUNK], F32, name="y", align_bytes=64, bufs=5)
+            live["yt", m] = y
+            nc.vector.transpose(out=y[:], in_=live["back", m][:].bitcast(F32))
+
+        def weave_t(m):
+            nc.scalar.copy(
+                out=live["gt", m][:, 2:].rearrange("p g (s i) u -> p g s i u", s=4),
+                in_=live["yt", m][:].rearrange("p (s g u i) -> p g s i u", s=4, g=2, u=2),
+            )
+
         def widen_flat(m, lo, hi):
             live["flat", m] = work.tile([P, P * (hi - lo)], BF16, name="flat", align_bytes=64, bufs=2)
             for c in range(lo, hi):
@@ -440,8 +470,8 @@ def tile_bank_relation_distill_d6_kernel(
             load_s_quadrants(5)
             load_b_tile_quadrants(10)
             load_b_tile_quadrants(11)
-            load_t(6)
             load_t(7)
+            load_t(6)
             load_s_quadrants(6)
             load_s_quadrants(7)
             nc.vector.tensor_scalar(out=neg[:], in0=scale[:], scalar1=-1.0, scalar2=None, op0=MULT)
@@ -524,13 +554,13 @@ def tile_bank_relation_distill_d6_kernel(
             quant_s(0)
             widen(3,5,7)
             perm_b(5,True)
-            perm_b(6,True)
             quant_s(1)
             widen(3,7,9)
             quant_s(2)
             perm_b(4)
-            perm_b(7)
             widen(3,9,16)
+            perm_b(6)
+            perm_b(7)
             widen(4,0,16)
             close_group(0,0)
             square(0,0)
@@ -622,13 +652,14 @@ def tile_bank_relation_distill_d6_kernel(
             square(4,1)
             widen(6,0,4)
             quant_b(2,256,512)
+            widen_parked(7)
             widen(6,4,16)
             open_group(5,0)
             open_group(5,1)
             close_group(5,0)
             perm_s(6,True)
             square(5,0)
-            widen(7,0,16)
+            widen(7,0,8)
             close_group(5,1)
             square(5,1)
             close_group(0,2)
@@ -645,7 +676,6 @@ def tile_bank_relation_distill_d6_kernel(
             turn_t(6,0)
             turn_t(6,1)
             turn_t(7,0)
-            turn_t(7,1)
             take_t(6,0)
             take_t(6,1)
             weave_s(6)
@@ -656,24 +686,27 @@ def tile_bank_relation_distill_d6_kernel(
             weigh(1,1024,1536)
             weigh(2,1024,1536)
             flip_s(7)
-            weigh(3,1024,1536)
             square(4,2)
             take_t(7,0)
-            take_t(7,1)
             multiply(5,2)
             weave_s(7)
             square(5,2)
+            flip_t(7)
+            weave_t(7)
+            weigh(3,1024,1536)
             weigh(4,0,1024)
-            quant_t(7)
-            weigh(4,1024,1536)
             multiply(6,0)
             square(6,0)
+            quant_t(7)
+            weigh(4,1024,1536)
             quant_s(7)
-            weigh(5,0,1024)
+            weigh(5,0,512)
+            weigh(5,512,1024)
             weigh(5,1024,1536)
             multiply(6,1)
             square(6,1)
-            weigh(6,0,1024)
+            weigh(6,0,512)
+            weigh(6,512,1024)
             multiply(6,2)
             last = TILES - 1
             multiply(last, 0)

@@ -240,34 +240,59 @@ def tile_bank_relation_distill_d6_kernel(
                     op0=MULT,
                 )
 
-        def widen_parked(m):
-            xq = work.tile([P, 4, 2, 2, 32, 2], BF16, name="parked", align_bytes=64, bufs=1)
-            for c in range(8, 16):
+        def widen_parked(m, h):
+            xq = work.tile([P, 4, 2, 2, 32, 2], BF16, name="xt", align_bytes=64)
+            for c in range(8 * h, 8 * h + 8):
                 g, q = divmod(c, 4)
                 nc.vector.tensor_scalar(
-                    out=xq[:, q, g - 2].rearrange("p u w e -> p w u e"),
+                    out=xq[:, q, g % 2].rearrange("p u w e -> p w u e"),
                     in0=block(m, c).rearrange("p (w u e) -> p w u e", u=2, e=2),
                     scalar1=neg[:, m, c : c + 1],
                     scalar2=None,
                     op0=MULT,
                 )
-            park = o_view[:, m, :CHUNK].bitcast(BF16)
+            park = o_view[:, TILES - 1, CHUNK * h : CHUNK * (h + 1)].bitcast(BF16)
             nc.sync.dma_start(out=park, in_=xq[:].rearrange("p q g u w e -> p (q g u w e)"))
-            back = work.tile([P, 2 * CHUNK], BF16, name="back", align_bytes=64, bufs=1)
-            live["back", m] = back
+            live["park", m, h] = park
+
+        def widen_parked_flat(m, h):
+            xq = work.tile([P, 4, 2, P], BF16, name="xt", align_bytes=64)
+            for c in range(8 * h, 8 * h + 8):
+                g, q = divmod(c, 4)
+                nc.scalar.activation(
+                    out=xq[:, q, g % 2],
+                    in_=block(m, c),
+                    func=mybir.ActivationFunctionType.Copy,
+                    scale=neg[:, m, c : c + 1],
+                )
+            park = o_view[:, TILES - 1, CHUNK * h : CHUNK * (h + 1)].bitcast(BF16)
+            nc.sync.dma_start(out=park, in_=xq[:].rearrange("p q g k -> p (q g k)"))
+            live["park", m, h] = park
+
+        def part_t(m, h):
+            x = wide.tile([P, 8, 2, 32], F32, name="x", align_bytes=64)
+            nc.scalar.copy(out=x[:], in_=live["back", m, h].rearrange("p (b j u) -> p b u j", b=8, u=2))
+            live["back", m, h] = x[:].rearrange("p b u j -> p (b u j)")
+
+        def fetch_parked(m, h):
+            park = live["park", m, h]
+            back = wide.tile([P, 2 * CHUNK], BF16, name="x", align_bytes=64)
+            live["back", m, h] = back[:].bitcast(F32)
             rows = park.rearrange("(s i) (a w) -> a i s w", s=4, a=4)
             for a in (0, 2, 1, 3):
                 nc.sync.dma_start(out=back[32 * a : 32 * (a + 1), :].rearrange("p (s w) -> p s w", s=4), in_=rows[a])
 
-        def flip_t(m):
+        def flip_t(m, h):
             y = work.tile([P, CHUNK], F32, name="y", align_bytes=64, bufs=5)
-            live["yt", m] = y
-            nc.vector.transpose(out=y[:], in_=live["back", m][:].bitcast(F32))
+            live["yt", m, h] = y
+            nc.vector.transpose(out=y[:], in_=live["back", m, h])
 
-        def weave_t(m):
+        def weave_t(m, h):
+            if ("gt", m) not in live:
+                live["gt", m] = work.tile([P, GT, P, 2], F32, name="t_grouped", align_bytes=64)
             nc.scalar.copy(
-                out=live["gt", m][:, 2:].rearrange("p g (s i) u -> p g s i u", s=4),
-                in_=live["yt", m][:].rearrange("p (s g u i) -> p g s i u", s=4, g=2, u=2),
+                out=live["gt", m][:, 2 * h : 2 * h + 2].rearrange("p g (s i) u -> p g s i u", s=4),
+                in_=live["yt", m, h][:].rearrange("p (s g u i) -> p g s i u", s=4, g=2, u=2),
             )
 
         def widen_flat(m, lo, hi):
@@ -380,6 +405,13 @@ def tile_bank_relation_distill_d6_kernel(
             passes_t(m, n, view, lo, hi, True, False)
             passes_s(m, n, view, lo, hi, False, True)
 
+        def multiply_late_half(m, n):
+            live["acc", m, n, 0] = claim([P, CHUNK], F32)
+            view = live["acc", m, n, 0][1][:]
+            passes_t(m, n, view, 0, CHUNK, True, False, 0, 2)
+            passes_s(m, n, view, 0, CHUNK, False, False)
+            passes_t(m, n, view, 0, CHUNK, False, True, 2, GT)
+
         def open_group(m, n, g0=0, g1=GT):
             if g0 == 0:
                 live["acc", m, n, 0] = claim([P, CHUNK], F32)
@@ -390,14 +422,17 @@ def tile_bank_relation_distill_d6_kernel(
 
         def square(m, n, lo=0, hi=CHUNK):
             if ("sq", m) not in live:
-                live["sq", m] = work.tile([P, N + 5], F32, name="sq", bufs=6)
+                live["sq", m] = work.tile([P, N + 5], F32, name="sq", bufs=7)
             b, acc = live["acc", m, n, lo]
             idle.append(b)
             nc.scalar.activation(
                 out=live["sq", m][:, CHUNK * n + lo : CHUNK * n + hi], in_=acc[:, : hi - lo], func=SQUARE
             )
 
-        def weigh(m, lo=0, hi=N, part=None, queue=nc.sync):
+        def store(m, lo, hi):
+            nc.sync.dma_start(out=o_view[:, m, lo:hi], in_=live["sq", m][:, lo:hi])
+
+        def weigh(m, lo=0, hi=N, part=None, held=False):
             res = live["sq", m][:, lo:hi]
             nc.vector.scalar_tensor_tensor(
                 out=res,
@@ -408,7 +443,8 @@ def tile_bank_relation_distill_d6_kernel(
                 op1=MULT,
                 accum_out=parts[:, m, lo // CHUNK : lo // CHUNK + 1] if part is None else part,
             )
-            queue.dma_start(out=o_view[:, m, lo:hi], in_=res)
+            if not held:
+                store(m, lo, hi)
 
         def spread_trust(n):
             if n % 2 == 0:
@@ -612,7 +648,7 @@ def tile_bank_relation_distill_d6_kernel(
             open_group(3,1,2,4)
             close_group(3,0)
             square(3,0)
-            weigh(0,512,1024)
+            weigh(0,512,1024,held=True)
             flip_s(4)
             flip_b(8)
             close_group(3,1)
@@ -624,12 +660,12 @@ def tile_bank_relation_distill_d6_kernel(
             weave_s(4)
             take_t(5,0)
             take_t(5,1)
-            weigh(1,512,1024)
+            weigh(1,512,1024,held=True)
             quant_t(4,2,4)
             perm_b(9)
             quant_s(4)
             flip_b(9)
-            weigh(2,512,1024)
+            weigh(2,512,1024,held=True)
             open_group(2,2)
             open_group(3,2)
             perm_s(5,True)
@@ -650,16 +686,20 @@ def tile_bank_relation_distill_d6_kernel(
             multiply(4,1)
             weave_b(11)
             square(4,1)
-            widen(6,0,4)
+            widen_parked(7,0)
+            store(0,512,1024)
             quant_b(2,256,512)
-            widen_parked(7)
-            widen(6,4,16)
+            perm_s(6,True)
+            widen_parked_flat(7,1)
+            store(1,512,1024)
+            store(2,512,1024)
+            fetch_parked(7,0)
+            fetch_parked(7,1)
+            widen(6,0,16)
             open_group(5,0)
             open_group(5,1)
             close_group(5,0)
-            perm_s(6,True)
             square(5,0)
-            widen(7,0,8)
             close_group(5,1)
             square(5,1)
             close_group(0,2)
@@ -673,34 +713,37 @@ def tile_bank_relation_distill_d6_kernel(
             flip_s(6)
             weigh(3,0,1024)
             weigh(0,1024,1536)
+            weigh(4,0,512)
             turn_t(6,0)
             turn_t(6,1)
-            turn_t(7,0)
             take_t(6,0)
             take_t(6,1)
             weave_s(6)
             perm_s(7,True)
             multiply(4,2)
+            weigh(1,1024,1536)
+            weigh(4,512,1024)
             quant_t(6)
             quant_s(6)
-            weigh(1,1024,1536)
             weigh(2,1024,1536)
             flip_s(7)
             square(4,2)
-            take_t(7,0)
-            multiply(5,2)
+            flip_t(7,0)
             weave_s(7)
-            square(5,2)
-            flip_t(7)
-            weave_t(7)
+            part_t(7,1)
+            weave_t(7,0)
+            multiply(5,2)
             weigh(3,1024,1536)
-            weigh(4,0,1024)
+            weigh(4,1024,1536)
+            flip_t(7,1)
+            square(5,2)
+            weave_t(7,1)
+            quant_s(7)
+            quant_t(7,0,2)
             multiply(6,0)
             square(6,0)
-            quant_t(7)
-            weigh(4,1024,1536)
-            quant_s(7)
             weigh(5,0,512)
+            quant_t(7,2,4)
             weigh(5,512,1024)
             weigh(5,1024,1536)
             multiply(6,1)
@@ -709,17 +752,17 @@ def tile_bank_relation_distill_d6_kernel(
             weigh(6,512,1024)
             multiply(6,2)
             last = TILES - 1
-            multiply(last, 0)
+            multiply_late_half(last, 0)
             square(last - 1, 2)
             weigh(last - 1, 1024, 1536)
             multiply(last, 1, 0, 256)
             square(last, 0)
-            nc.vector.tensor_reduce(out=total[:], in_=parts[:], axis=mybir.AxisListType.X, op=mybir.AluOpType.add)
             weigh(last, 0, 512, part=live["sq", last][:, N + 0 : N + 1])
-            nc.vector.tensor_scalar(out=means[:, :last], in0=total[:], scalar1=1.0 / N, scalar2=None, op0=MULT)
+            nc.vector.tensor_reduce(out=total[:], in_=parts[:], axis=mybir.AxisListType.X, op=mybir.AluOpType.add)
             multiply(last, 1, 256, 512)
             square(last, 1, 0, 256)
             weigh(last, 512, 768, part=live["sq", last][:, N + 1 : N + 2])
+            nc.vector.tensor_scalar(out=means[:, :last], in0=total[:], scalar1=1.0 / N, scalar2=None, op0=MULT)
             multiply(last, 2, 0, 256)
             square(last, 1, 256, 512)
             weigh(last, 768, 1024, part=live["sq", last][:, N + 2 : N + 3])

@@ -458,12 +458,6 @@ def tile_bank_relation_distill_d6_kernel(
                 stop=True,
             )
 
-        def stir(count):
-            for i in range(count):
-                b, bank = claim([P, CHUNK], F32)
-                idle.append(b)
-                nc.tensor.matmul(bank[:], ones[:], ones[:].unsqueeze(1).to_broadcast([P, CHUNK // P, P]), start=True, stop=True)
-
         def take_trust(lo, hi):
             b, bank = live["trust", lo // 2]
             idle.append(b)
@@ -511,7 +505,6 @@ def tile_bank_relation_distill_d6_kernel(
             load_s_quadrants(6)
             load_s_quadrants(7)
             nc.vector.tensor_scalar(out=neg[:], in0=scale[:], scalar1=-1.0, scalar2=None, op0=MULT)
-            stir(4)
             spread_trust(0)
             widen(0, 0, 12)
             widen_flat(0, 12, 16)

from contextlib import ExitStack

import concourse.mybir as mybir
from concourse.masks import make_identity

M, K, J, N = 1024, 2048, 1024, 1536
FLOPS = 2 * M * N * (K + J)

F32 = mybir.dt.float32
BF16 = mybir.dt.bfloat16
I32 = mybir.dt.int32
U32 = mybir.dt.uint32
U8 = mybir.dt.uint8
FP8 = mybir.dt.float8_e4m3fn
FP8X4 = mybir.dt.float8_e4m3fn_x4
FP4X4 = mybir.dt.float4_e2m1fn_x4
MULT = mybir.AluOpType.mult
SQUARE = mybir.ActivationFunctionType.Square

P = 128
TILES = M // P
CHUNK = 512
CHUNKS = N // CHUNK
GT = K // 512
GS = J // 512
BANKS = 8
PAIRS = (2, 3)


def tile_bank_relation_distill_d6_kernel(
    tc, teacher_bytes, teacher_scale, tbank_words, tbank_scales, student, sbank, trust, out_0, out_1
):
    nc = tc.nc
    with ExitStack() as ctx:
        const = ctx.enter_context(tc.tile_pool(name="const", bufs=1))
        work = ctx.enter_context(tc.tile_pool(name="work", bufs=3))
        keep = ctx.enter_context(tc.tile_pool(name="keep", bufs=6))
        wide = ctx.enter_context(tc.tile_pool(name="wide", bufs=6))
        psum = ctx.enter_context(tc.psum_pool(name="psum", bufs=1))

        ident = const.tile([P, P], F32, name="ident")
        ones = const.tile([P, P], BF16, name="ones")
        trust_row = const.tile([P, N], BF16, name="trust_row")
        trust_all = const.tile([P, N + 5], BF16, name="trust_all")
        first_words = [const.tile([P, 4 * CHUNK], U8, name="first_words%d" % g, align_bytes=64) for g in range(GT)]
        last_words = [const.tile([P, 2, 2 * CHUNK], U8, name="last_words%d" % h, align_bytes=64) for h in range(2)]
        first_scales = const.tile([P, GT, 2 * CHUNK], U8, name="first_scales", align_bytes=64)
        last_scales = const.tile([P, GT, CHUNK], U8, name="last_scales", align_bytes=64)
        scale = const.tile([P, TILES, K // P], F32, name="scale")
        neg = const.tile([P, TILES, K // P], F32, name="neg")
        total = const.tile([P, TILES - 1], F32, name="total")
        parts = const.tile([P, TILES - 1, CHUNKS], F32, name="parts")
        shares = const.tile([P, P + 5], F32, name="shares")
        final = const.tile([P, P], F32, name="final")
        means = const.tile([P, TILES], F32, name="means")

        t_view = teacher_bytes.rearrange("(p m) k -> p m k", m=TILES)
        s_view = student.rearrange("(p m) k -> p m k", m=TILES)
        o_view = out_0.rearrange("(p m) n -> p m n", m=TILES)

        t_half = [const.tile([P, K // 2], U8, name="t_half%d" % h, align_bytes=64) for h in range(2)]
        t_raw = {m: const.tile([P, K], U8, name="t_raw%d" % m, align_bytes=64) for m in range(1, TILES)}
        s_pair = const.tile([P, 2, J], BF16, name="s_pair", align_bytes=64)
        s_raw = [s_pair[:, 0], s_pair[:, 1]]
        s_raw.extend(const.tile([P, J], BF16, name="s_raw%d" % m, align_bytes=64)[:] for m in range(2, TILES))
        b_pair = {j: const.tile([P, 2, J], BF16, name="b_pair%d" % j, align_bytes=64) for j in PAIRS}
        b_raw = [
            b_pair[i // 2][:, i % 2] if i // 2 in PAIRS else const.tile([P, J], BF16, name="b_raw%d" % i, align_bytes=64)[:]
            for i in range(12)
        ]
        b_codes = [const.tile([P, GS, CHUNK], U32, name="b_codes%d" % n, align_bytes=64) for n in range(CHUNKS)]
        b_scales = [const.tile([P, GS, CHUNK], U8, name="b_scales%d" % n, align_bytes=64) for n in range(CHUNKS)]

        def load_s(m):
            nc.sync.dma_start(out=s_raw[m][:], in_=s_view[:, m, :])

        def load_quadrants(raw, rows):
            for a in (0, 2, 1, 3):
                nc.sync.dma_start(out=raw[32 * a : 32 * (a + 1), :].rearrange("p (s k) -> p s k", s=4), in_=rows[a])

        def load_s_quadrants(m):
            rows = student.rearrange("(s i m) (a k) -> m a i s k", s=4, i=32, a=4)[m]
            load_quadrants(s_raw[m], rows)

        def load_b_tile_quadrants(i):
            rows = sbank[P * i : P * (i + 1), :].rearrange("(s i) (a k) -> a i s k", s=4, a=4)
            load_quadrants(b_raw[i], rows)

        def load_t(m):
            nc.sync.dma_start(out=t_raw[m][:], in_=t_view[:, m, :])

        def load_t_half(h):
            nc.sync.dma_start(out=t_half[h][:], in_=t_view[:, 0, K // 2 * h : K // 2 * (h + 1)])

        def block(m, c):
            if m == 0:
                return t_half[c // 8][:, P * (c % 8) : P * (c % 8 + 1)].bitcast(FP8)
            return t_raw[m][:, P * c : P * (c + 1)].bitcast(FP8)

        def load_b(lo, hi):
            for i in range(lo, hi):
                nc.sync.dma_start(out=b_raw[i][:], in_=sbank[P * i : P * (i + 1), :])

        def load_b_pair(j):
            rows = sbank[2 * P * j : 2 * P * (j + 1), :].rearrange("(e p) k -> p e k", e=2)
            nc.sync.dma_start(out=b_pair[j][:], in_=rows)

        def load_first_words(g):
            nc.sync.dma_start(out=first_words[g][:].bitcast(I32), in_=tbank_words[g, :, : 4 * CHUNK].bitcast(I32))

        def load_last_words():
            for h in range(2):
                rows = tbank_words[2 * h : 2 * h + 2, :, 4 * CHUNK :].rearrange("g p w -> p g w")
                nc.sync.dma_start(out=last_words[h][:].bitcast(I32), in_=rows.bitcast(I32))

        def clear_scales(tile):
            nc.vector.memset(tile[:].rearrange("p g n -> p (g n)").bitcast(I32), 0)

        def load_scales(tile, lo, hi, g0=0, g1=GT):
            for r in range(4):
                nc.sync.dma_start(
                    out=tile[r:P:32].bitcast(I32),
                    in_=tbank_scales[g0:g1, r:16:4, lo:hi].rearrange("g q n -> q g n").bitcast(I32),
                )

        def tb_operand(n, g, lo, hi):
            if n < CHUNKS - 1:
                lo, hi = CHUNK * n + lo, CHUNK * n + hi
                return first_words[g][:, 2 * lo : 2 * hi], first_scales[:, g, lo:hi]
            return last_words[g // 2][:, g % 2, 2 * lo : 2 * hi], last_scales[:, g, lo:hi]

        def load_s_pair(m):
            nc.sync.dma_start(out=s_pair[:], in_=s_view[:, m : m + 2, :])

        live = {}
        idle = list(range(BANKS))

        def claim(shape, dtype):
            b = idle.pop(0)
            return b, psum.tile(shape, dtype, name="bank%d" % b)

        def perm(key, raw, on_scalar):
            x = wide.tile([P, GS, 2, P], F32, name="x", align_bytes=64)
            live[key] = x
            src = raw[:].bitcast(F32).rearrange("p (q g u r) -> p g u q r", g=GS, u=2, r=8)
            dst = x[:].rearrange("p g u (q r) -> p g u q r", r=8)
            if on_scalar:
                nc.scalar.copy(out=dst, in_=src)
            else:
                nc.vector.tensor_copy(out=dst, in_=src)

        def perm_s(m, on_scalar=False):
            perm(("xs", m), s_raw[m], on_scalar)

        def perm_b(i, on_scalar=False):
            perm(("xb", i), b_raw[i], on_scalar)

        def turn(key):
            b, bank = claim([P, GS, 2, P], F32)
            for g in range(GS):
                for u in range(2):
                    nc.tensor.transpose(bank[:, g, u, :], live[key][:, g, u, :], ident[:])
            return b, bank

        def turn_s(m):
            live["bs", m] = turn(("xs", m))

        def turn_b(i):
            live["bb", i] = turn(("xb", i))

        def take(dst, claimed, on_scalar):
            b, bank = claimed
            idle.append(b)
            src = bank[:].rearrange("p g u r -> p g r u")
            if on_scalar:
                nc.scalar.copy(out=dst, in_=src)
            else:
                nc.vector.tensor_copy(out=dst, in_=src)

        def take_s(m, on_scalar=True):
            grouped = work.tile([P, GS, P, 2], F32, name="s_grouped", align_bytes=64)
            live["gs", m] = grouped
            take(grouped[:], live["bs", m], on_scalar)

        def flip(key):
            y = work.tile([P, GS, 2, P], F32, name="y", align_bytes=64, bufs=5)
            nc.vector.transpose(
                out=y[:].rearrange("p g u r -> p (g u r)"), in_=live[key][:].rearrange("p g u r -> p (g u r)")
            )
            return y

        def flip_s(m):
            live["ys", m] = flip(("xs", m))

        def flip_b(i):
            live["yb", i] = flip(("xb", i))

        def weave(dst, y, on_scalar):
            src = y[:].rearrange("p g u r -> p g r u")
            if on_scalar:
                nc.scalar.copy(out=dst, in_=src)
            else:
                nc.vector.tensor_copy(out=dst, in_=src)

        def weave_s(m, on_scalar=True):
            grouped = work.tile([P, GS, P, 2], F32, name="s_grouped", align_bytes=64)
            live["gs", m] = grouped
            weave(grouped[:], live["ys", m], on_scalar)

        def b_slot(i):
            j, e = divmod(i, 2)
            if ("gb", j) not in live:
                live["gb", j] = work.tile([P, GS, 2 * P, 2], F32, name="b_grouped", align_bytes=64, bufs=4)
            return live["gb", j][:, :, P * e : P * (e + 1), :]

        def weave_b(i, on_scalar=True):
            weave(b_slot(i), live["yb", i], on_scalar)

        def quant_s(m):
            codes = keep.tile([P, GS, P], U32, name="s_codes", align_bytes=64)
            scales = keep.tile([P, GS, P], U8, name="s_scales", align_bytes=64)
            live["cs", m] = (codes, scales)
            nc.vector.quantize_mx(
                out=codes[:].rearrange("p g r -> p (g r)").bitcast(FP8X4),
                scales=scales[:].rearrange("p g r -> p (g r)"),
                in_=live["gs", m][:].rearrange("p g r u -> p (g r u)").bitcast(BF16),
            )

        def widen(m, lo, hi):
            if lo == 0:
                live["xt", m] = work.tile([P, GT, 2, P, 2], BF16, name="xt", align_bytes=64)
            xt = live["xt", m]
            for c in range(lo, hi):
                g, q = divmod(c, 4)
                nc.vector.tensor_scalar(
                    out=xt[:, g, :, 32 * q : 32 * (q + 1), :].rearrange("p u w e -> p w u e"),
                    in0=block(m, c).rearrange("p (w u e) -> p w u e", u=2, e=2),
                    scalar1=neg[:, m, c : c + 1],
                    scalar2=None,
                    op0=MULT,
                )

        def widen_parked(m, h):
            xq = work.tile([P, 4, 2, 2, 32, 2], BF16, name="xt", align_bytes=64)
            for c in range(8 * h, 8 * h + 8):
                g, q = divmod(c, 4)
                nc.vector.tensor_scalar(
                    out=xq[:, q, g % 2].rearrange("p u w e -> p w u e"),
                    in0=block(m, c).rearrange("p (w u e) -> p w u e", u=2, e=2),
                    scalar1=neg[:, m, c : c + 1],
                    scalar2=None,
                    op0=MULT,
                )
            park = o_view[:, TILES - 1, CHUNK * h : CHUNK * (h + 1)].bitcast(BF16)
            nc.sync.dma_start(out=park, in_=xq[:].rearrange("p q g u w e -> p (q g u w e)"))
            live["park", m, h] = park

        def widen_parked_flat(m, h):
            xq = work.tile([P, 4, 2, P], BF16, name="xt", align_bytes=64)
            for c in range(8 * h, 8 * h + 8):
                g, q = divmod(c, 4)
                nc.scalar.activation(
                    out=xq[:, q, g % 2],
                    in_=block(m, c),
                    func=mybir.ActivationFunctionType.Copy,
                    scale=neg[:, m, c : c + 1],
                )
            park = o_view[:, TILES - 1, CHUNK * h : CHUNK * (h + 1)].bitcast(BF16)
            nc.sync.dma_start(out=park, in_=xq[:].rearrange("p q g k -> p (q g k)"))
            live["park", m, h] = park

        def part_t(m, h):
            x = wide.tile([P, 8, 2, 32], F32, name="x", align_bytes=64)
            nc.scalar.copy(out=x[:], in_=live["back", m, h].rearrange("p (b j u) -> p b u j", b=8, u=2))
            live["back", m, h] = x[:].rearrange("p b u j -> p (b u j)")

        def fetch_parked(m, h):
            park = live["park", m, h]
            back = wide.tile([P, 2 * CHUNK], BF16, name="x", align_bytes=64)
            live["back", m, h] = back[:].bitcast(F32)
            rows = park.rearrange("(s i) (a w) -> a i s w", s=4, a=4)
            for a in (0, 2, 1, 3):
                nc.sync.dma_start(out=back[32 * a : 32 * (a + 1), :].rearrange("p (s w) -> p s w", s=4), in_=rows[a])

        def flip_t(m, h):
            y = work.tile([P, CHUNK], F32, name="y", align_bytes=64, bufs=5)
            live["yt", m, h] = y
            nc.vector.transpose(out=y[:], in_=live["back", m, h])

        def weave_t(m, h):
            if ("gt", m) not in live:
                live["gt", m] = work.tile([P, GT, P, 2], F32, name="t_grouped", align_bytes=64)
            nc.scalar.copy(
                out=live["gt", m][:, 2 * h : 2 * h + 2].rearrange("p g (s i) u -> p g s i u", s=4),
                in_=live["yt", m, h][:].rearrange("p (s g u i) -> p g s i u", s=4, g=2, u=2),
            )

        def widen_flat(m, lo, hi):
            live["flat", m] = work.tile([P, P * (hi - lo)], BF16, name="flat", align_bytes=64, bufs=2)
            for c in range(lo, hi):
                nc.scalar.activation(
                    out=live["flat", m][:, P * (c - lo) : P * (c - lo + 1)],
                    in_=block(m, c),
                    func=mybir.ActivationFunctionType.Copy,
                    scale=neg[:, m, c : c + 1],
                )

        def turn_t(m, h):
            words = live["xt", m][:].rearrange("p g u w e -> p (g u w e)").bitcast(F32)
            b, bank = claim([P, 2, 2, P], F32)
            live["bt", m, h] = (b, bank)
            for g in range(2):
                for u in range(2):
                    at = P * (2 * (2 * h + g) + u)
                    nc.tensor.transpose(bank[:, g, u, :], words[:, at : at + P], ident[:])

        def turn_flat(m, g):
            words = live["flat", m][:].bitcast(F32)
            if ("bt", m, g // 2) not in live:
                live["bt", m, g // 2] = claim([P, 2, 2, P], F32)
            bank = live["bt", m, g // 2][1]
            for u in range(2):
                nc.tensor.transpose(bank[:, g % 2, u, :], words[:, u : 2 * P : 2], ident[:])

        def turn_half(m, g):
            words = live["xt", m][:].rearrange("p g u w e -> p (g u w e)").bitcast(F32)
            if ("bt", m, g // 2) not in live:
                live["bt", m, g // 2] = claim([P, 2, 2, P], F32)
            bank = live["bt", m, g // 2][1]
            for u in range(2):
                at = P * (2 * g + u)
                nc.tensor.transpose(bank[:, g % 2, u, :], words[:, at : at + P], ident[:])

        def turn_pass(m, g):
            words = live["xt", m][:].rearrange("p g u w e -> p (g u w e)").bitcast(F32)
            b, bank = claim([P, 1, 2, P], F32)
            live["bp", m, g] = (b, bank)
            for u in range(2):
                at = P * (2 * g + u)
                nc.tensor.transpose(bank[:, 0, u, :], words[:, at : at + P], ident[:])

        def take_pass(m, g):
            if g == 0:
                live["gt", m] = work.tile([P, GT, P, 2], F32, name="t_grouped", align_bytes=64)
            take(live["gt", m][:, g : g + 1], live["bp", m, g], True)

        def take_t(m, h, on_scalar=True):
            if ("gt", m) not in live:
                live["gt", m] = work.tile([P, GT, P, 2], F32, name="t_grouped", align_bytes=64)
            take(live["gt", m][:, 2 * h : 2 * h + 2], live["bt", m, h], on_scalar)

        def quant_t(m, lo=0, hi=GT):
            if lo == 0:
                codes = keep.tile([P, GT, P], U32, name="t_codes", align_bytes=64)
                scales = keep.tile([P, GT, P], U8, name="t_scales", align_bytes=64)
                live["ct", m] = (codes, scales)
            codes, scales = live["ct", m]
            nc.vector.quantize_mx(
                out=codes[:, lo:hi].rearrange("p g r -> p (g r)").bitcast(FP8X4),
                scales=scales[:, lo:hi].rearrange("p g r -> p (g r)"),
                in_=live["gt", m][:, lo:hi].rearrange("p g r u -> p (g r u)").bitcast(BF16),
            )

        def take_b(i, on_scalar=True):
            take(b_slot(i), live["bb", i], on_scalar)

        def quant_b(c, lo=0, hi=CHUNK):
            for g in range(GS):
                nc.vector.quantize_mx(
                    out=b_codes[c][:, g, lo:hi].bitcast(FP8X4),
                    scales=b_scales[c][:, g, lo:hi],
                    in_=live["gb", 2 * c + lo // (2 * P)][:, g].rearrange("p r u -> p (r u)").bitcast(BF16),
                )

        def passes_s(m, n, acc, lo, hi, first, last):
            codes, scales = live["cs", m]
            for g in range(GS):
                nc.tensor.matmul_mx(
                    out=acc,
                    lhsT=codes[:, g, :].bitcast(FP8X4),
                    lhsT_scale=scales[:, g, :],
                    rhs=b_codes[n][:, g, lo:hi].bitcast(FP8X4),
                    rhs_scale=b_scales[n][:, g, lo:hi],
                    start=first and g == 0,
                    stop=last and g == GS - 1,
                )

        def passes_t(m, n, acc, lo, hi, first, last, g0=0, g1=GT):
            codes, scales = live["ct", m]
            for g in range(g0, g1):
                words, word_scales = tb_operand(n, g, lo, hi)
                nc.tensor.matmul_mx(
                    out=acc,
                    lhsT=codes[:, g, :].bitcast(FP8X4),
                    lhsT_scale=scales[:, g, :],
                    rhs=words.bitcast(FP4X4),
                    rhs_scale=word_scales,
                    start=first and g == 0,
                    stop=last and g == GT - 1,
                )

        def multiply(m, n, lo=0, hi=CHUNK):
            live["acc", m, n, lo] = claim([P, CHUNK], F32)
            view = live["acc", m, n, lo][1][:, : hi - lo]
            passes_t(m, n, view, lo, hi, True, False)
            passes_s(m, n, view, lo, hi, False, True)

        def multiply_late_half(m, n):
            live["acc", m, n, 0] = claim([P, CHUNK], F32)
            view = live["acc", m, n, 0][1][:]
            passes_t(m, n, view, 0, CHUNK, True, False, 0, 2)
            passes_s(m, n, view, 0, CHUNK, False, False)
            passes_t(m, n, view, 0, CHUNK, False, True, 2, GT)

        def open_group(m, n, g0=0, g1=GT):
            if g0 == 0:
                live["acc", m, n, 0] = claim([P, CHUNK], F32)
            passes_t(m, n, live["acc", m, n, 0][1][:], 0, CHUNK, True, False, g0, g1)

        def close_group(m, n):
            passes_s(m, n, live["acc", m, n, 0][1][:], 0, CHUNK, False, True)

        def square(m, n, lo=0, hi=CHUNK):
            if ("sq", m) not in live:
                live["sq", m] = work.tile([P, N + 5], F32, name="sq", bufs=7)
            b, acc = live["acc", m, n, lo]
            idle.append(b)
            nc.scalar.activation(
                out=live["sq", m][:, CHUNK * n + lo : CHUNK * n + hi], in_=acc[:, : hi - lo], func=SQUARE
            )

        def store(m, lo, hi):
            nc.sync.dma_start(out=o_view[:, m, lo:hi], in_=live["sq", m][:, lo:hi])

        def weigh(m, lo=0, hi=N, part=None, held=False):
            res = live["sq", m][:, lo:hi]
            nc.vector.scalar_tensor_tensor(
                out=res,
                in0=res,
                scalar=1.0,
                in1=trust_all[:, lo:hi],
                op0=MULT,
                op1=MULT,
                accum_out=parts[:, m, lo // CHUNK : lo // CHUNK + 1] if part is None else part,
            )
            if not held:
                store(m, lo, hi)

        def spread_trust(n):
            if n % 2 == 0:
                live["trust", n // 2] = claim([P, min(2 * CHUNK, N - CHUNK * n)], BF16)
            bank = live["trust", n // 2][1]
            nc.tensor.matmul(
                bank[:, CHUNK * (n % 2) : CHUNK * (n % 2 + 1)],
                ones[:],
                trust_row[:, CHUNK * n : CHUNK * (n + 1)],
                start=True,
                stop=True,
            )

        def take_trust(lo, hi):
            b, bank = live["trust", lo // 2]
            idle.append(b)
            nc.scalar.copy(out=trust_all[:, CHUNK * lo : CHUNK * hi], in_=bank[:])

        with tc.manual_schedule():
            nc.vector.memset(ones[:], 1.0)
            nc.scalar.activation(out=trust_all[:, N:], in_=ones[:, :5], func=SQUARE)
            nc.vector.memset(trust_row[:].bitcast(I32), 0)
            clear_scales(first_scales)
            make_identity(nc, ident[:])
            clear_scales(last_scales)
            nc.vector.memset(parts[:], 0.0)
            nc.sync.dma_start(out=scale[:], in_=teacher_scale.rearrange("(p m) c -> p m c", m=TILES))
            load_t_half(0)
            load_t_half(1)
            nc.sync.dma_start(out=trust_row[0:1, :], in_=trust.rearrange("(o n) -> o n", o=1))
            load_t(1)
            load_scales(first_scales, 0, 2 * CHUNK)
            load_first_words(0)
            load_first_words(1)
            load_first_words(2)
            load_t(2)
            load_b(0, 2)
            load_first_words(3)
            load_b(2, 4)
            load_s_pair(0)
            load_s(2)
            load_t(3)
            load_b_pair(2)
            load_b_pair(3)
            load_t(4)
            load_scales(last_scales, 2 * CHUNK, N)
            load_last_words()
            load_s_quadrants(3)
            load_t(5)
            load_s_quadrants(4)
            load_b_tile_quadrants(8)
            load_b_tile_quadrants(9)
            load_s_quadrants(5)
            load_b_tile_quadrants(10)
            load_b_tile_quadrants(11)
            load_t(7)
            load_t(6)
            load_s_quadrants(6)
            load_s_quadrants(7)
            nc.vector.tensor_scalar(out=neg[:], in0=scale[:], scalar1=-1.0, scalar2=None, op0=MULT)
            spread_trust(0)
            widen(0, 0, 12)
            widen_flat(0, 12, 16)
            widen(1, 0, 12)
            widen_flat(1, 12, 16)
            turn_pass(0, 0)
            turn_pass(0, 1)
            spread_trust(1)
            take_pass(0, 0)
            take_pass(0, 1)
            turn_flat(0, 3)
            turn_half(0, 2)
            turn_pass(1, 0)
            take_pass(1, 0)
            spread_trust(2)
            turn_pass(1, 1)
            take_pass(1, 1)
            turn_flat(1, 3)
            turn_half(1, 2)
            quant_t(0, 0, 1)
            quant_t(0, 1, 2)
            take_t(0, 1, False)
            take_t(1, 1)
            quant_t(1, 0, 1)
            quant_t(1, 1, 2)
            quant_t(0, 2, 4)
            quant_t(1, 2, 4)
            take_trust(0, 2)
            take_trust(2, 3)
            for m in range(2):
                for g in range(2):
                    open_group(m, 0, g, g + 1)
                    open_group(m, 1, g, g + 1)
            open_group(0,0,2,3)
            open_group(0,1,2,3)
            open_group(1,0,2,3)
            open_group(1,1,2,3)
            widen(2,0,16)
            perm_b(0,True)
            perm_b(1,True)
            turn_t(2,0)
            turn_t(2,1)
            turn_b(0)
            turn_b(1)
            take_t(2,0)
            take_b(0)
            take_b(1)
            open_group(0,0,3,4)
            open_group(0,1,3,4)
            open_group(1,0,3,4)
            perm_b(2)
            take_t(2,1,False)
            perm_b(3)
            quant_t(2,0,2)
            quant_t(2,2,4)
            turn_b(2)
            take_b(2)
            turn_b(3)
            take_b(3)
            perm_s(0)
            perm_s(1)
            perm_s(2)
            quant_b(0,0,256)
            open_group(2,0,0,3)
            turn_s(0)
            take_s(0)
            turn_s(1)
            take_s(1)
            turn_s(2)
            take_s(2)
            quant_b(0,256,512)
            widen(3,0,5)
            open_group(1,1,3,4)
            open_group(2,0,3,4)
            open_group(2,1)
            quant_s(0)
            widen(3,5,7)
            perm_b(5,True)
            quant_s(1)
            widen(3,7,9)
            quant_s(2)
            perm_b(4)
            widen(3,9,16)
            perm_b(6)
            perm_b(7)
            widen(4,0,16)
            close_group(0,0)
            square(0,0)
            weigh(0,0,512)
            close_group(1,0)
            square(1,0)
            close_group(2,0)
            square(2,0)
            turn_b(4)
            take_b(4)
            turn_b(5)
            take_b(5)
            turn_b(6)
            take_b(6)
            turn_b(7)
            take_b(7)
            open_group(0,2)
            open_group(1,2)
            quant_b(1,0,256)
            weigh(1,0,512)
            quant_b(1,256,512)
            turn_t(3,0)
            turn_t(3,1)
            turn_t(4,0)
            perm_s(3,True)
            take_t(3,0)
            take_t(3,1)
            flip_s(3)
            weigh(2,0,512)
            quant_t(3,0,2)
            weave_s(3)
            take_t(4,0)
            close_group(0,1)
            square(0,1)
            close_group(1,1)
            square(1,1)
            close_group(2,1)
            square(2,1)
            quant_t(3,2,4)
            widen(5,0,8)
            quant_s(3)
            widen(5,8,16)
            quant_t(4,0,2)
            perm_s(4,True)
            perm_b(8,True)
            open_group(3,0,0,2)
            open_group(3,1,0,2)
            open_group(3,0,2,4)
            open_group(3,1,2,4)
            close_group(3,0)
            square(3,0)
            weigh(0,512,1024,held=True)
            flip_s(4)
            flip_b(8)
            close_group(3,1)
            square(3,1)
            turn_t(4,1)
            turn_t(5,0)
            turn_t(5,1)
            take_t(4,1)
            weave_s(4)
            take_t(5,0)
            take_t(5,1)
            weigh(1,512,1024,held=True)
            quant_t(4,2,4)
            perm_b(9)
            quant_s(4)
            flip_b(9)
            weigh(2,512,1024,held=True)
            open_group(2,2)
            open_group(3,2)
            perm_s(5,True)
            perm_b(10,True)
            weave_b(8)
            weave_b(9)
            quant_t(5)
            flip_s(5)
            perm_b(11)
            flip_b(10)
            flip_b(11)
            multiply(4,0)
            square(4,0)
            weave_s(5)
            weave_b(10)
            quant_s(5)
            quant_b(2,0,256)
            multiply(4,1)
            weave_b(11)
            square(4,1)
            widen_parked(7,0)
            store(0,512,1024)
            quant_b(2,256,512)
            perm_s(6,True)
            widen_parked_flat(7,1)
            store(1,512,1024)
            store(2,512,1024)
            fetch_parked(7,0)
            fetch_parked(7,1)
            widen(6,0,16)
            open_group(5,0)
            open_group(5,1)
            close_group(5,0)
            square(5,0)
            close_group(5,1)
            square(5,1)
            close_group(0,2)
            square(0,2)
            close_group(1,2)
            square(1,2)
            close_group(2,2)
            square(2,2)
            close_group(3,2)
            square(3,2)
            flip_s(6)
            weigh(3,0,1024)
            weigh(0,1024,1536)
            weigh(4,0,512)
            turn_t(6,0)
            turn_t(6,1)
            take_t(6,0)
            take_t(6,1)
            weave_s(6)
            perm_s(7,True)
            multiply(4,2)
            weigh(1,1024,1536)
            weigh(4,512,1024)
            quant_t(6)
            quant_s(6)
            weigh(2,1024,1536)
            flip_s(7)
            square(4,2)
            flip_t(7,0)
            weave_s(7)
            part_t(7,1)
            weave_t(7,0)
            multiply(5,2)
            weigh(3,1024,1536)
            weigh(4,1024,1536)
            flip_t(7,1)
            square(5,2)
            weave_t(7,1)
            quant_s(7)
            quant_t(7,0,2)
            multiply(6,0)
            square(6,0)
            weigh(5,0,512)
            quant_t(7,2,4)
            weigh(5,512,1024)
            weigh(5,1024,1536)
            multiply(6,1)
            square(6,1)
            weigh(6,0,512)
            weigh(6,512,1024)
            multiply(6,2)
            last = TILES - 1
            multiply_late_half(last, 0)
            square(last - 1, 2)
            weigh(last - 1, 1024, 1536)
            multiply(last, 1, 0, 256)
            square(last, 0)
            weigh(last, 0, 512, part=live["sq", last][:, N + 0 : N + 1])
            nc.vector.tensor_reduce(out=total[:], in_=parts[:], axis=mybir.AxisListType.X, op=mybir.AluOpType.add)
            multiply(last, 1, 256, 512)
            square(last, 1, 0, 256)
            weigh(last, 512, 768, part=live["sq", last][:, N + 1 : N + 2])
            nc.vector.tensor_scalar(out=means[:, :last], in0=total[:], scalar1=1.0 / N, scalar2=None, op0=MULT)
            multiply(last, 2, 0, 256)
            square(last, 1, 256, 512)
            weigh(last, 768, 1024, part=live["sq", last][:, N + 2 : N + 3])
            multiply(last, 2, 256, 384)
            square(last, 2, 0, 256)
            weigh(last, 1024, 1280, part=live["sq", last][:, N + 3 : N + 4])
            multiply(last, 2, 384, 512)
            square(last, 2, 256, 384)
            weigh(last, 1280, 1408, part=live["sq", last][:, N + 4 : N + 5])
            square(last, 2, 384, 512)
            nc.vector.tensor_tensor(out=final[:], in0=live["sq", last][:, N - P : N], in1=trust_all[:, N - P : N], op=MULT)
            nc.sync.dma_start(out=o_view[:, last, N - P : N], in_=final[:])
            nc.vector.scalar_tensor_tensor(
                out=shares[:],
                in0=live["sq", last][:, N - P : N + 5],
                scalar=1.0 / N,
                in1=trust_all[:, N - P : N + 5],
                op0=MULT,
                op1=MULT,
                accum_out=means[:, last:],
            )
            nc.scalar.dma_start(out=out_1.rearrange("(p m) -> p m", m=TILES), in_=means[:])
